import numpy as np
import ml_dtypes


def mxq(x, axis, fmt="e4m3"):
    dtype, down = {"e4m3": (ml_dtypes.float8_e4m3fn, 7), "e5m2": (ml_dtypes.float8_e5m2, 14)}[fmt]
    v = np.moveaxis(np.asarray(x, np.float32).astype(ml_dtypes.bfloat16).astype(np.float64), axis, -1)
    blocks = v.reshape(v.shape[:-1] + (-1, 32))
    amax = np.abs(blocks).max(-1, keepdims=True)
    byte = np.maximum(np.where(amax > 0, np.frexp(amax)[1] - 1 + 127, 0) - down, 1)
    scale = np.exp2(byte - 127.0)
    codes = (blocks / scale).astype(np.float32).astype(dtype).astype(np.float64)
    return np.moveaxis((codes * scale).reshape(v.shape), -1, axis)


WIDE = False


def mx_kscale(k):
    if not WIDE:
        return np.ones(k)
    levels = np.array([10, -10, 5, -5, 0])
    if k % 512:
        return np.exp2(np.random.permutation(np.resize(levels, k // 32))).repeat(32)
    a = np.empty((k // 512, 16))
    for p in range(k // 512):
        a[p, :8] = np.random.permutation(np.resize(levels, 8))
        for g in range(8):
            far = levels[np.abs(levels - a[p, g]) >= 10]
            a[p, g + 8] = far[np.random.randint(len(far))]
    return np.exp2(a.ravel()).repeat(32)


def f64(x):
    return np.asarray(x).astype(np.float64)


def striped(idx):
    return np.tile(idx.reshape(-1, 16).T, (8, 1)).astype(np.uint16)


def unstriped(offs):
    return offs[:16].T.reshape(-1).astype(np.int64)


E2M1 = np.array([0.0, 0.5, 1.0, 1.5, 2.0, 3.0, 4.0, 6.0, -0.0, -0.5, -1.0, -1.5, -2.0, -3.0, -4.0, -6.0])


def pack_weight(w, fmt):
    k, n = w.shape
    w = f64(np.asarray(w, np.float32).astype(ml_dtypes.bfloat16)).reshape(k // 32, 32, n)
    amax = np.abs(w).max(1)
    if fmt == "e4m3":
        byte = np.frexp(amax)[1] - 1 + 127 - 7
    else:
        mant, ex = np.frexp(amax / 6.0)
        byte = np.where(mant > 0.5, ex, ex - 1) + 127
    byte = np.clip(np.where(amax > 0, byte, 1), 1, 254)
    scaled = (w * np.exp2(127.0 - byte)[:, None, :]).reshape(k, n).astype(np.float32)
    by_word = np.ascontiguousarray(scaled.reshape(k // 512, 128, 4, n).transpose(0, 1, 3, 2))
    if fmt == "e4m3":
        words = by_word.astype(ml_dtypes.float8_e4m3fn).view(np.uint8)
    else:
        c = by_word.astype(ml_dtypes.float4_e2m1fn).view(np.uint8) & 0xF
        words = (c[..., 0::2] | (c[..., 1::2] << 4)).reshape(k // 512, 128, 2 * n)
    return np.ascontiguousarray(words), np.ascontiguousarray(byte.astype(np.uint8).reshape(k // 512, 16, n))


def unpack_weight(words, scales, fmt):
    g, _, n = scales.shape
    words = np.ascontiguousarray(words).reshape(g, 128, n, -1)
    if fmt == "e4m3":
        vals = words.view(ml_dtypes.float8_e4m3fn).astype(np.float64)
    else:
        nib = np.empty((g, 128, n, 4), np.uint8)
        nib[..., 0::2] = words & 0xF
        nib[..., 1::2] = words >> 4
        vals = E2M1[nib]
    vals = vals * np.repeat(np.exp2(scales.astype(np.float64) - 127.0), 8, axis=1)[..., None]
    return vals.transpose(0, 1, 3, 2).reshape(g * 512, n)


def silu(v):
    return v / (1.0 + np.exp(-np.maximum(v, -700.0)))


K, T, E, C, H, N, HOT = 1536, 1280, 10, 128, 512, 256, 2


def by_expert(wq, xq):
    return np.concatenate([wq[e].T @ xq[:, e * C:(e + 1) * C] for e in range(E)], axis=1)


def setup_inputs():
    n = np.random.standard_normal
    s = mx_kscale(K)
    u = mx_kscale(H)
    slot_token = np.random.permutation(T)[:E * C]
    x = pack_weight(n((K, T)) * s[:, None], "e4m3")
    w1h = [pack_weight(m, "e4m3") for m in n((HOT, K, H)) / np.sqrt(K) / s[None, :, None] * u]
    w2h = [pack_weight(m, "e4m3") for m in n((HOT, H, N)) / np.sqrt(H) / u[None, :, None]]
    w1c = [pack_weight(m, "e2m1") for m in n((E - HOT, K, H)) / np.sqrt(K) / s[None, :, None] * u]
    w2c = [pack_weight(m, "e2m1") for m in n((E - HOT, H, N)) / np.sqrt(H) / u[None, :, None]]
    return {
        "x_words": x[0],
        "x_scales": x[1],
        "w1h_words": np.stack([m[0] for m in w1h]),
        "w1h_scales": np.stack([m[1] for m in w1h]),
        "w2h_words": np.stack([m[0] for m in w2h]),
        "w2h_scales": np.stack([m[1] for m in w2h]),
        "w1c_words": np.stack([m[0] for m in w1c]),
        "w1c_scales": np.stack([m[1] for m in w1c]),
        "w2c_words": np.stack([m[0] for m in w2c]),
        "w2c_scales": np.stack([m[1] for m in w2c]),
        "gate": np.tile(np.random.uniform(0.2, 1.0, E * C), (128, 1)).astype(np.float32),
        "offs": striped(slot_token),
    }


def reference(x_words, x_scales, w1h_words, w1h_scales, w2h_words, w2h_scales, w1c_words, w1c_scales, w2c_words, w2c_scales, gate, offs):
    w1h = np.stack([unpack_weight(w1h_words[e], w1h_scales[e], "e4m3") for e in range(HOT)])
    w2h = np.stack([unpack_weight(w2h_words[e], w2h_scales[e], "e4m3") for e in range(HOT)])
    w1c = np.stack([unpack_weight(w1c_words[e], w1c_scales[e], "e2m1") for e in range(E - HOT)])
    w2c = np.stack([unpack_weight(w2c_words[e], w2c_scales[e], "e2m1") for e in range(E - HOT)])
    idx = unstriped(offs)
    xq = unpack_weight(x_words, x_scales, "e4m3")[:, idx]
    w1 = [*w1h, *w1c]
    w2 = [*w2h, *w2c]
    h = silu(by_expert(w1, xq))
    y = by_expert(w2, mxq(h, 0, "e4m3"))
    out = np.zeros((N, T))
    out[:, idx] = f64(gate[:1]) * y
    return out

@@ -1,0 +1,245 @@
+from contextlib import ExitStack
+
+import concourse.mybir as mybir
+from concourse.masks import make_identity
+
+K, T, E, C, H, N, HOT = 1536, 1280, 10, 128, 512, 256, 2
+FLOPS = 2 * T * (K * H + H * N)
+
+F32 = mybir.dt.float32
+BF16 = mybir.dt.bfloat16
+I32 = mybir.dt.int32
+U32 = mybir.dt.uint32
+U16 = mybir.dt.uint16
+U8 = mybir.dt.uint8
+FP8X4 = mybir.dt.float8_e4m3fn_x4
+FP4X4 = mybir.dt.float4_e2m1fn_x4
+SILU = mybir.ActivationFunctionType.Silu
+MULT = mybir.AluOpType.mult
+
+P = 128
+PASSES = K // 512
+COLD = E - HOT
+HALVES = N // P
+SHIFT_ROWS = 112
+GROUPS = [[2, 3], [4, 5], [6, 7], [8, 9], [1], [0]]
+
+
+def tile_moe_hot_mlp_silu_kernel(
+    tc, x_words, x_scales, w1h_words, w1h_scales, w2h_words, w2h_scales,
+    w1c_words, w1c_scales, w2c_words, w2c_scales, gate, offs, out,
+):
+    nc = tc.nc
+    with ExitStack() as ctx:
+        keep = ctx.enter_context(tc.tile_pool(name="keep", bufs=1))
+        ring = ctx.enter_context(tc.tile_pool(name="ring", bufs=3))
+        work = ctx.enter_context(tc.tile_pool(name="work", bufs=3))
+        psum1 = ctx.enter_context(tc.psum_pool(name="psum1", bufs=6))
+        psum2 = ctx.enter_context(tc.psum_pool(name="psum2", bufs=1))
+
+        def zeroed_plane(name, shape):
+            plane = keep.tile(shape, U8, name=name, align_bytes=64)
+            flat = plane[:] if len(shape) == 2 else plane[:].rearrange("p a b -> p (a b)")
+            nc.vector.memset(flat.bitcast(I32), 0)
+            return plane
+
+        def load_plane(plane, scales):
+            rows = scales.rearrange("a (q r) w -> r q a w", r=4)
+            for r in range(4):
+                nc.sync.dma_start(plane[r:P:32, :, :].bitcast(I32), rows[r].bitcast(I32))
+
+        def listed(a, b):
+            return offsets[:, a // 16 : b // 16]
+
+        xw = [keep.tile([P, T], I32, name="xw%d" % s, align_bytes=64) for s in range(PASSES)]
+        offsets = keep.tile([P, T // 16], U16, name="offsets")
+        nc.sync.dma_start(xw[0][:], x_words[0].rearrange("p t d -> p (t d)").bitcast(I32))
+        nc.sync.dma_start(offsets[:], offs)
+        for s in range(1, PASSES):
+            nc.sync.dma_start(xw[s][:], x_words[s].rearrange("p t d -> p (t d)").bitcast(I32))
+
+        xs = zeroed_plane("xs", [P, T])
+        for q in range(4):
+            nc.scalar.dma_start(
+                xs[32 * q : 32 * q + 4 * PASSES, :].bitcast(I32),
+                x_scales[:, 4 * q : 4 * q + 4, :].bitcast(I32),
+            )
+
+        ident = keep.tile([P, P], F32, name="ident")
+        make_identity(nc, ident[:])
+
+        s1c = [zeroed_plane("s1c0", [P, 4 * PASSES, H])]
+
+        w1 = {}
+
+        def load_w1(g):
+            tile = ring.tile([P, 2 * PASSES * 2 * H], U8, name="w1", align_bytes=64)
+            first = GROUPS[g][0]
+            if first >= HOT:
+                src = w1c_words[first - HOT : first - HOT + 2].rearrange("e s p b -> p (e s) b")
+                nc.sync.dma_start(tile[:].rearrange("p (a b) -> p a b", b=2 * H).bitcast(I32), src.bitcast(I32))
+            else:
+                src = w1h_words[first].rearrange("s p i d -> p s (i d)")
+                nc.sync.dma_start(tile[:].rearrange("p (a b) -> p a b", b=4 * H).bitcast(I32), src.bitcast(I32))
+            w1[g] = tile
+
+        load_w1(0)
+        load_plane(s1c[0], w1c_scales[0:4].rearrange("e s b i -> (e s) b i"))
+        load_w1(1)
+
+        gw = {}
+        gs = {}
+
+        def gather_words(a, b, s):
+            tile = keep.tile([P, b - a], U32, name="gw%d_%d" % (a, s), align_bytes=64)
+            nc.vector.tensor_copy(tile[:], xw[s][:].bitcast(U32).indirect(listed(a, b)))
+            for e in range(a // C, b // C):
+                gw[(e, s)] = tile[:, e * C - a : (e + 1) * C - a]
+
+        def gather_scales(a, b, shifted):
+            tile = keep.tile([P, b - a], U8, name="gs%d" % a, align_bytes=64)
+            nc.vector.tensor_copy(tile[:], xs[:].indirect(listed(a, b)))
+            for e in range(a // C, b // C):
+                cols = slice(e * C - a, (e + 1) * C - a)
+                gs[(e, 0)] = tile[:, cols]
+                for s in range(1, PASSES):
+                    gs[(e, s)] = tile[4 * s : P, cols] if shifted is None else shifted[:, s - 1, cols]
+            if shifted is not None:
+                for s in range(1, PASSES):
+                    nc.scalar.dma_start(
+                        shifted[0:SHIFT_ROWS, s - 1, :].bitcast(I32),
+                        tile[4 * s : 4 * s + SHIFT_ROWS, :].bitcast(I32),
+                    )
+
+        shift_a = zeroed_plane("shift_a", [P, PASSES - 1, 2 * C])
+        shift_b = zeroed_plane("shift_b", [P, PASSES - 1, 6 * C])
+        s2c = zeroed_plane("s2c", [P, COLD, N])
+        load_plane(s2c, w2c_scales.rearrange("e s b n -> (e s) b n"))
+        w2c = keep.tile([P, COLD, 2 * N], U8, name="w2c", align_bytes=64)
+        nc.sync.dma_start(w2c[:].bitcast(I32), w2c_words.rearrange("e s p b -> p (e s) b").bitcast(I32))
+        s1c.append(zeroed_plane("s1c1", [P, 4 * PASSES, H]))
+        load_plane(s1c[1], w1c_scales[4:8].rearrange("e s b i -> (e s) b i"))
+        gates = keep.tile([P, T], F32, name="gates")
+        nc.sync.dma_start(gates[:], gate)
+        load_w1(2)
+        s1h = zeroed_plane("s1h", [P, HOT * PASSES, H])
+        s2h = zeroed_plane("s2h", [P, HOT, N])
+        w2h = keep.tile([P, HOT, 4 * N], U8, name="w2h", align_bytes=64)
+
+        ys = keep.tile([P, HALVES, T], F32, name="ys")
+        outs = [keep.tile([P, T], F32, name="out%d" % h) for h in range(HALVES)]
+        hq_in = {}
+
+        def first_layer(g):
+            experts = GROUPS[g]
+            turned = psum2.tile([P, len(experts), 2, C], F32, name="turned", tag="bank%d" % (g % 2))
+            for j, e in enumerate(experts):
+                acc = psum1.tile([P, H], F32, name="acc")
+                for s in range(PASSES):
+                    if e >= HOT:
+                        a = j * PASSES + s
+                        rhs = w1[g][:, a * 2 * H : (a + 1) * 2 * H].bitcast(FP4X4)
+                        f = e - HOT
+                        rhs_scale = s1c[f // 4][:, (f % 4) * PASSES + s, :]
+                    else:
+                        rhs = w1[g][:, s * 4 * H : (s + 1) * 4 * H].bitcast(FP8X4)
+                        rhs_scale = s1h[:, e * PASSES + s, :]
+                    nc.tensor.matmul_mx(
+                        out=acc[:], lhsT=gw[(e, s)].bitcast(FP8X4), lhsT_scale=gs[(e, s)],
+                        rhs=rhs, rhs_scale=rhs_scale, start=(s == 0), stop=(s == PASSES - 1),
+                    )
+                hid = work.tile([P, 2, P, 2], BF16, name="hid", align_bytes=64)
+                nc.scalar.activation(hid[:], acc[:].rearrange("c (p u v) -> c u p v", u=2, v=2), SILU)
+                pairs = hid[:].rearrange("c u p v -> c (u p v)").bitcast(F32)
+                for u in range(2):
+                    nc.tensor.transpose(turned[:, j, u, :], pairs[:, u * P : (u + 1) * P], ident[:])
+            grouped = work.tile([P, len(experts) * C * 4], BF16, name="grouped", align_bytes=64)
+            nc.scalar.copy(
+                grouped[:].bitcast(F32).rearrange("p (j c u) -> p j c u", u=2, c=C),
+                turned[:].rearrange("p j u c -> p j c u"),
+            )
+            hq_in[g] = grouped
+
+        hq = {}
+
+        def quantize(g):
+            width = len(GROUPS[g]) * C
+            codes = work.tile([P, width], U32, name="codes", align_bytes=64)
+            scales = work.tile([P, width], U8, name="scales", align_bytes=64)
+            nc.vector.quantize_mx(out=codes[:].bitcast(FP8X4), scales=scales[:], in_=hq_in[g][:])
+            hq[g] = (codes, scales)
+
+        def second_layer(g):
+            experts = GROUPS[g]
+            width = len(experts) * C
+            codes, scales = hq[g]
+            y = psum2.tile([P, HALVES, width], F32, name="y", tag="bank%d" % ((g + 1) % 2))
+            for j, e in enumerate(experts):
+                cols = slice(j * C, (j + 1) * C)
+                for h in range(HALVES):
+                    if e >= HOT:
+                        lhsT = w2c[:, e - HOT, h * 2 * P : (h + 1) * 2 * P].bitcast(FP4X4)
+                        lhsT_scale = s2c[:, e - HOT, h * P : (h + 1) * P]
+                    else:
+                        lhsT = w2h[:, e, h * 4 * P : (h + 1) * 4 * P].bitcast(FP8X4)
+                        lhsT_scale = s2h[:, e, h * P : (h + 1) * P]
+                    nc.tensor.matmul_mx(
+                        out=y[:, h, cols], lhsT=lhsT, lhsT_scale=lhsT_scale,
+                        rhs=codes[:, cols].bitcast(FP8X4), rhs_scale=scales[:, cols], start=True, stop=True,
+                    )
+            a = experts[0] * C
+            nc.scalar.copy(ys[:, :, a : a + width], y[:])
+
+        def scatter(h, a, b):
+            nc.vector.tensor_tensor(outs[h][:].indirect(listed(a, b)), ys[:, h, a:b], gates[:, a:b], MULT)
+
+        gather_words(256, 768, 0)
+        gather_words(768, 1280, 0)
+        gather_words(0, 256, 0)
+        gather_scales(256, 512, shift_a)
+        gather_words(256, 512, 1)
+        gather_words(256, 512, 2)
+        gather_scales(512, 1280, shift_b)
+        gather_words(512, 768, 1)
+        gather_words(512, 768, 2)
+        gather_words(768, 1280, 1)
+        gather_words(768, 1280, 2)
+        gather_scales(0, 256, None)
+        gather_words(0, 256, 1)
+        gather_words(0, 256, 2)
+        first_layer(0)
+        load_w1(3)
+        load_plane(s1h, w1h_scales.rearrange("e s b i -> (e s) b i"))
+        load_plane(s2h, w2h_scales.rearrange("e s b n -> (e s) b n"))
+        nc.sync.dma_start(w2h[:].bitcast(I32), w2h_words.rearrange("e s p n d -> p (e s) (n d)").bitcast(I32))
+        quantize(0)
+        first_layer(1)
+        load_w1(4)
+        quantize(1)
+        second_layer(0)
+        first_layer(2)
+        load_w1(5)
+        scatter(0, 320, 512)
+        scatter(1, 320, 512)
+        quantize(2)
+        second_layer(1)
+        first_layer(3)
+        scatter(0, 512, 768)
+        scatter(1, 512, 768)
+        quantize(3)
+        second_layer(2)
+        first_layer(4)
+        scatter(0, 768, 1024)
+        scatter(1, 768, 1024)
+        quantize(4)
+        second_layer(3)
+        first_layer(5)
+        scatter(0, 1024, 1280)
+        quantize(5)
+        second_layer(4)
+        second_layer(5)
+        scatter(1, 1024, 1280)
+        scatter(0, 0, 320)
+        nc.sync.dma_start(out[0:P, :], outs[0][:])
+        scatter(1, 0, 320)
+        nc.sync.dma_start(out[P : 2 * P, :], outs[1][:])

@@ -23,6 +23,7 @@ COLD = E - HOT
 HALVES = N // P
 SHIFT_ROWS = 112
 GROUPS = [[2, 3], [4, 5], [6, 7], [8, 9], [1], [0]]
+ORDER = [e for group in GROUPS for e in group]
 
 
 def tile_moe_hot_mlp_silu_kernel(
@@ -32,10 +33,10 @@ def tile_moe_hot_mlp_silu_kernel(
     nc = tc.nc
     with ExitStack() as ctx:
         keep = ctx.enter_context(tc.tile_pool(name="keep", bufs=1))
-        ring = ctx.enter_context(tc.tile_pool(name="ring", bufs=3))
-        work = ctx.enter_context(tc.tile_pool(name="work", bufs=3))
-        psum1 = ctx.enter_context(tc.psum_pool(name="psum1", bufs=6))
-        psum2 = ctx.enter_context(tc.psum_pool(name="psum2", bufs=1))
+        work = ctx.enter_context(tc.tile_pool(name="work", bufs=4))
+        psum = ctx.enter_context(tc.psum_pool(name="psum", bufs=1))
+        banks = [psum.tile([P, H], F32, name="bank%d" % b) for b in range(8)]
+        acc_banks, turn_banks, y_banks = banks[0:4], banks[4:6], banks[6:8]
 
         def zeroed_plane(name, shape):
             plane = keep.tile(shape, U8, name=name, align_bytes=64)
@@ -43,20 +44,21 @@ def tile_moe_hot_mlp_silu_kernel(
             nc.vector.memset(flat.bitcast(I32), 0)
             return plane
 
-        def load_plane(plane, scales):
-            rows = scales.rearrange("a (q r) w -> r q a w", r=4)
+        def load_plane(queue, plane, scales):
+            rows = scales.rearrange("e s (q r) w -> r q (e s) w", r=4)
             for r in range(4):
-                nc.sync.dma_start(plane[r:P:32, :, :].bitcast(I32), rows[r].bitcast(I32))
+                queue.dma_start(plane[r:P:32, :, :].bitcast(I32), rows[r].bitcast(I32))
 
         def listed(a, b):
             return offsets[:, a // 16 : b // 16]
 
-        xw = [keep.tile([P, T], I32, name="xw%d" % s, align_bytes=64) for s in range(PASSES)]
+        xw_first = keep.tile([P, T], I32, name="xw_first", align_bytes=64)
+        xw_rest = keep.tile([P, PASSES - 1, T], I32, name="xw_rest", align_bytes=64)
+        xw = [xw_first[:]] + [xw_rest[:, s, :] for s in range(PASSES - 1)]
         offsets = keep.tile([P, T // 16], U16, name="offsets")
-        nc.sync.dma_start(xw[0][:], x_words[0].rearrange("p t d -> p (t d)").bitcast(I32))
+        nc.sync.dma_start(xw_first[:], x_words[0].rearrange("p t d -> p (t d)").bitcast(I32))
         nc.sync.dma_start(offsets[:], offs)
-        for s in range(1, PASSES):
-            nc.sync.dma_start(xw[s][:], x_words[s].rearrange("p t d -> p (t d)").bitcast(I32))
+        nc.sync.dma_start(xw_rest[:], x_words[1:PASSES].rearrange("s p t d -> p s (t d)").bitcast(I32))
 
         xs = zeroed_plane("xs", [P, T])
         for q in range(4):
@@ -68,12 +70,23 @@ def tile_moe_hot_mlp_silu_kernel(
         ident = keep.tile([P, P], F32, name="ident")
         make_identity(nc, ident[:])
 
-        s1c = [zeroed_plane("s1c0", [P, 4 * PASSES, H])]
+        gate_rows = keep.tile([P, C], F32, name="gate_rows")
+        nc.gpsimd.memset(gate_rows[:], 0.0)
+        nc.scalar.dma_start(gate_rows[0:E, :], gate[0:1, :].rearrange("o (e c) -> (o e) c", c=C))
+
+        s1c = zeroed_plane("s1c", [P, COLD * PASSES, H])
+        s1h = zeroed_plane("s1h", [P, HOT * PASSES, H])
+        s2h = zeroed_plane("s2h", [P, HOT, N])
+        s2c = zeroed_plane("s2c", [P, COLD, N])
+        shift_a = zeroed_plane("shift_a", [P, PASSES - 1, 4 * C])
+        shift_b = zeroed_plane("shift_b", [P, PASSES - 1, 4 * C])
+        w2c = keep.tile([P, COLD, 2 * N], U8, name="w2c", align_bytes=64)
+        w2h = keep.tile([P, HOT, 4 * N], U8, name="w2h", align_bytes=64)
 
         w1 = {}
 
         def load_w1(g):
-            tile = ring.tile([P, 2 * PASSES * 2 * H], U8, name="w1", align_bytes=64)
+            tile = keep.tile([P, 2 * PASSES * 2 * H], U8, name="w1_%d" % g, align_bytes=64)
             first = GROUPS[g][0]
             if first >= HOT:
                 src = w1c_words[first - HOT : first - HOT + 2].rearrange("e s p b -> p (e s) b")
@@ -84,15 +97,37 @@ def tile_moe_hot_mlp_silu_kernel(
             w1[g] = tile
 
         load_w1(0)
-        load_plane(s1c[0], w1c_scales[0:4].rearrange("e s b i -> (e s) b i"))
+        load_plane(nc.sync, s1c, w1c_scales)
         load_w1(1)
+        nc.sync.dma_start(w2c[:].bitcast(I32), w2c_words.rearrange("e s p b -> p (e s) b").bitcast(I32))
+        load_plane(nc.sync, s2c, w2c_scales)
+        load_w1(2)
+        load_w1(3)
+        nc.sync.dma_start(w2h[:].bitcast(I32), w2h_words.rearrange("e s p n d -> p (e s) (n d)").bitcast(I32))
+        load_w1(4)
+        load_w1(5)
+        load_plane(nc.gpsimd, s1h, w1h_scales)
+        load_plane(nc.gpsimd, s2h, w2h_scales)
+
+        gate_turned = acc_banks[0]
+        nc.tensor.transpose(gate_turned[:, 0:P], gate_rows[:], ident[:])
+        gate_cols = keep.tile([P, E], F32, name="gate_cols")
+        nc.scalar.copy(gate_cols[:], gate_turned[:, 0:E])
+        gates = keep.tile([P, T], F32, name="gates")
+        for first in range(0, E, 4):
+            count = min(4, E - first)
+            spread = acc_banks[1 + first // 4]
+            for j in range(count):
+                column = gate_cols[:, first + j : first + j + 1]
+                nc.tensor.transpose(spread[:, j * C : (j + 1) * C], column.to_broadcast([P, P]), ident[:])
+            nc.scalar.copy(gates[:, first * C : (first + count) * C], spread[:, 0 : count * C])
 
         gw = {}
         gs = {}
 
         def gather_words(a, b, s):
             tile = keep.tile([P, b - a], U32, name="gw%d_%d" % (a, s), align_bytes=64)
-            nc.vector.tensor_copy(tile[:], xw[s][:].bitcast(U32).indirect(listed(a, b)))
+            nc.vector.tensor_copy(tile[:], xw[s].bitcast(U32).indirect(listed(a, b)))
             for e in range(a // C, b // C):
                 gw[(e, s)] = tile[:, e * C - a : (e + 1) * C - a]
 
@@ -111,36 +146,21 @@ def tile_moe_hot_mlp_silu_kernel(
                         tile[4 * s : 4 * s + SHIFT_ROWS, :].bitcast(I32),
                     )
 
-        shift_a = zeroed_plane("shift_a", [P, PASSES - 1, 2 * C])
-        shift_b = zeroed_plane("shift_b", [P, PASSES - 1, 6 * C])
-        s2c = zeroed_plane("s2c", [P, COLD, N])
-        load_plane(s2c, w2c_scales.rearrange("e s b n -> (e s) b n"))
-        w2c = keep.tile([P, COLD, 2 * N], U8, name="w2c", align_bytes=64)
-        nc.sync.dma_start(w2c[:].bitcast(I32), w2c_words.rearrange("e s p b -> p (e s) b").bitcast(I32))
-        s1c.append(zeroed_plane("s1c1", [P, 4 * PASSES, H]))
-        load_plane(s1c[1], w1c_scales[4:8].rearrange("e s b i -> (e s) b i"))
-        gates = keep.tile([P, T], F32, name="gates")
-        nc.sync.dma_start(gates[:], gate)
-        load_w1(2)
-        s1h = zeroed_plane("s1h", [P, HOT * PASSES, H])
-        s2h = zeroed_plane("s2h", [P, HOT, N])
-        w2h = keep.tile([P, HOT, 4 * N], U8, name="w2h", align_bytes=64)
-
         ys = keep.tile([P, HALVES, T], F32, name="ys")
         outs = [keep.tile([P, T], F32, name="out%d" % h) for h in range(HALVES)]
         hq_in = {}
 
         def first_layer(g):
             experts = GROUPS[g]
-            turned = psum2.tile([P, len(experts), 2, C], F32, name="turned", tag="bank%d" % (g % 2))
+            turned = turn_banks[g % 2][:, 0 : len(experts) * 2 * C].rearrange("p (j u c) -> p j u c", u=2, c=C)
             for j, e in enumerate(experts):
-                acc = psum1.tile([P, H], F32, name="acc")
+                acc = acc_banks[ORDER.index(e) % 4]
                 for s in range(PASSES):
                     if e >= HOT:
                         a = j * PASSES + s
                         rhs = w1[g][:, a * 2 * H : (a + 1) * 2 * H].bitcast(FP4X4)
                         f = e - HOT
-                        rhs_scale = s1c[f // 4][:, (f % 4) * PASSES + s, :]
+                        rhs_scale = s1c[:, f * PASSES + s, :]
                     else:
                         rhs = w1[g][:, s * 4 * H : (s + 1) * 4 * H].bitcast(FP8X4)
                         rhs_scale = s1h[:, e * PASSES + s, :]
@@ -156,7 +176,7 @@ def tile_moe_hot_mlp_silu_kernel(
             grouped = work.tile([P, len(experts) * C * 4], BF16, name="grouped", align_bytes=64)
             nc.scalar.copy(
                 grouped[:].bitcast(F32).rearrange("p (j c u) -> p j c u", u=2, c=C),
-                turned[:].rearrange("p j u c -> p j c u"),
+                turned.rearrange("p j u c -> p j c u"),
             )
             hq_in[g] = grouped
 
@@ -169,77 +189,50 @@ def tile_moe_hot_mlp_silu_kernel(
             nc.vector.quantize_mx(out=codes[:].bitcast(FP8X4), scales=scales[:], in_=hq_in[g][:])
             hq[g] = (codes, scales)
 
-        def second_layer(g):
+        def second_layer(g, h):
             experts = GROUPS[g]
             width = len(experts) * C
             codes, scales = hq[g]
-            y = psum2.tile([P, HALVES, width], F32, name="y", tag="bank%d" % ((g + 1) % 2))
+            y = y_banks[g % 2] if h == 0 else turn_banks[(g + 1) % 2]
             for j, e in enumerate(experts):
                 cols = slice(j * C, (j + 1) * C)
-                for h in range(HALVES):
-                    if e >= HOT:
-                        lhsT = w2c[:, e - HOT, h * 2 * P : (h + 1) * 2 * P].bitcast(FP4X4)
-                        lhsT_scale = s2c[:, e - HOT, h * P : (h + 1) * P]
-                    else:
-                        lhsT = w2h[:, e, h * 4 * P : (h + 1) * 4 * P].bitcast(FP8X4)
-                        lhsT_scale = s2h[:, e, h * P : (h + 1) * P]
-                    nc.tensor.matmul_mx(
-                        out=y[:, h, cols], lhsT=lhsT, lhsT_scale=lhsT_scale,
-                        rhs=codes[:, cols].bitcast(FP8X4), rhs_scale=scales[:, cols], start=True, stop=True,
-                    )
+                if e >= HOT:
+                    lhsT = w2c[:, e - HOT, h * 2 * P : (h + 1) * 2 * P].bitcast(FP4X4)
+                    lhsT_scale = s2c[:, e - HOT, h * P : (h + 1) * P]
+                else:
+                    lhsT = w2h[:, e, h * 4 * P : (h + 1) * 4 * P].bitcast(FP8X4)
+                    lhsT_scale = s2h[:, e, h * P : (h + 1) * P]
+                nc.tensor.matmul_mx(
+                    out=y[:, cols], lhsT=lhsT, lhsT_scale=lhsT_scale,
+                    rhs=codes[:, cols].bitcast(FP8X4), rhs_scale=scales[:, cols], start=True, stop=True,
+                )
             a = experts[0] * C
-            nc.scalar.copy(ys[:, :, a : a + width], y[:])
+            nc.scalar.copy(ys[:, h, a : a + width], y[:, 0:width])
 
         def scatter(h, a, b):
             nc.vector.tensor_tensor(outs[h][:].indirect(listed(a, b)), ys[:, h, a:b], gates[:, a:b], MULT)
 
-        gather_words(256, 768, 0)
-        gather_words(768, 1280, 0)
-        gather_words(0, 256, 0)
-        gather_scales(256, 512, shift_a)
-        gather_words(256, 512, 1)
-        gather_words(256, 512, 2)
-        gather_scales(512, 1280, shift_b)
-        gather_words(512, 768, 1)
-        gather_words(512, 768, 2)
-        gather_words(768, 1280, 1)
-        gather_words(768, 1280, 2)
-        gather_scales(0, 256, None)
-        gather_words(0, 256, 1)
-        gather_words(0, 256, 2)
-        first_layer(0)
-        load_w1(3)
-        load_plane(s1h, w1h_scales.rearrange("e s b i -> (e s) b i"))
-        load_plane(s2h, w2h_scales.rearrange("e s b n -> (e s) b n"))
-        nc.sync.dma_start(w2h[:].bitcast(I32), w2h_words.rearrange("e s p n d -> p (e s) (n d)").bitcast(I32))
-        quantize(0)
-        first_layer(1)
-        load_w1(4)
-        quantize(1)
-        second_layer(0)
-        first_layer(2)
-        load_w1(5)
-        scatter(0, 320, 512)
-        scatter(1, 320, 512)
-        quantize(2)
-        second_layer(1)
-        first_layer(3)
-        scatter(0, 512, 768)
-        scatter(1, 512, 768)
-        quantize(3)
-        second_layer(2)
-        first_layer(4)
-        scatter(0, 768, 1024)
-        scatter(1, 768, 1024)
-        quantize(4)
-        second_layer(3)
-        first_layer(5)
-        scatter(0, 1024, 1280)
-        quantize(5)
-        second_layer(4)
-        second_layer(5)
-        scatter(1, 1024, 1280)
-        scatter(0, 0, 320)
+        pieces = [(256, 768, shift_a), (768, 1280, shift_b), (0, 256, None)]
+        for a, b, shifted in pieces:
+            gather_words(a, b, 0)
+        for a, b, shifted in pieces:
+            gather_scales(a, b, shifted)
+        for a, b, shifted in pieces:
+            for s in range(1, PASSES):
+                gather_words(a, b, s)
+
+        spans = [(320, 512), (512, 768), (768, 1024), (1024, 1280), (160, 320), (0, 160)]
+        last = len(GROUPS) - 1
+        for g in range(len(GROUPS)):
+            first_layer(g)
+            quantize(g)
+            if g > 0:
+                second_layer(g - 1, 1)
+            second_layer(g, 0)
+            if g > 0:
+                scatter(1, *spans[g - 1])
+            scatter(0, *spans[g])
         nc.sync.dma_start(out[0:P, :], outs[0][:])
-        scatter(1, 0, 320)
+        second_layer(last, 1)
+        scatter(1, *spans[last])
         nc.sync.dma_start(out[P : 2 * P, :], outs[1][:])

@@ -22,6 +22,7 @@ PASSES = K // 512
 COLD = E - HOT
 HALVES = N // P
 SHIFT_ROWS = 112
+HOT_WORDS_AT = 4 * C
 GROUPS = [[2, 3], [4, 5], [6, 7], [8, 9], [1], [0]]
 ORDER = [e for group in GROUPS for e in group]
 
@@ -60,26 +61,27 @@ def tile_moe_hot_mlp_silu_kernel(
         nc.sync.dma_start(offsets[:], offs)
         nc.sync.dma_start(xw_rest[:], x_words[1:PASSES].rearrange("s p t d -> p s (t d)").bitcast(I32))
 
+        gate_rows = keep.tile([P, C], F32, name="gate_rows")
+        nc.scalar.dma_start(gate_rows[:], gate.rearrange("o (e c) -> (o e) c", c=C)[0:P, :])
+        ident = keep.tile([P, P], F32, name="ident")
+        make_identity(nc, ident[:])
         xs = zeroed_plane("xs", [P, T])
+        s1c = [zeroed_plane("s1c_a", [P, 4 * PASSES, H])]
+        s2c = zeroed_plane("s2c", [P, COLD, N])
+        shift_a = zeroed_plane("shift_a", [P, PASSES - 1, 4 * C])
+        shift_b = zeroed_plane("shift_b", [P, PASSES - 1, 4 * C])
+        s1c.append(zeroed_plane("s1c_b", [P, 4 * PASSES, H]))
+        s1h = zeroed_plane("s1h", [P, HOT * PASSES, H])
+        s2h = zeroed_plane("s2h", [P, HOT, N])
         for q in range(4):
             nc.scalar.dma_start(
                 xs[32 * q : 32 * q + 4 * PASSES, :].bitcast(I32),
                 x_scales[:, 4 * q : 4 * q + 4, :].bitcast(I32),
             )
-
-        ident = keep.tile([P, P], F32, name="ident")
-        make_identity(nc, ident[:])
-
-        gate_rows = keep.tile([P, C], F32, name="gate_rows")
-        nc.gpsimd.memset(gate_rows[:], 0.0)
-        nc.scalar.dma_start(gate_rows[0:E, :], gate[0:1, :].rearrange("o (e c) -> (o e) c", c=C))
-
-        s1c = zeroed_plane("s1c", [P, COLD * PASSES, H])
-        s1h = zeroed_plane("s1h", [P, HOT * PASSES, H])
-        s2h = zeroed_plane("s2h", [P, HOT, N])
-        s2c = zeroed_plane("s2c", [P, COLD, N])
-        shift_a = zeroed_plane("shift_a", [P, PASSES - 1, 4 * C])
-        shift_b = zeroed_plane("shift_b", [P, PASSES - 1, 4 * C])
+        load_plane(nc.gpsimd, s1c[0], w1c_scales[0:4])
+        load_plane(nc.gpsimd, s2c, w2c_scales)
+        load_plane(nc.gpsimd, s1h, w1h_scales)
+        load_plane(nc.gpsimd, s2h, w2h_scales)
         w2c = keep.tile([P, COLD, 2 * N], U8, name="w2c", align_bytes=64)
         w2h = keep.tile([P, HOT, 4 * N], U8, name="w2h", align_bytes=64)
 
@@ -97,39 +99,37 @@ def tile_moe_hot_mlp_silu_kernel(
             w1[g] = tile
 
         load_w1(0)
-        load_plane(nc.sync, s1c, w1c_scales)
         load_w1(1)
         nc.sync.dma_start(w2c[:].bitcast(I32), w2c_words.rearrange("e s p b -> p (e s) b").bitcast(I32))
-        load_plane(nc.sync, s2c, w2c_scales)
         load_w1(2)
+        load_plane(nc.sync, s1c[1], w1c_scales[4:8])
         load_w1(3)
         nc.sync.dma_start(w2h[:].bitcast(I32), w2h_words.rearrange("e s p n d -> p (e s) (n d)").bitcast(I32))
         load_w1(4)
         load_w1(5)
-        load_plane(nc.gpsimd, s1h, w1h_scales)
-        load_plane(nc.gpsimd, s2h, w2h_scales)
 
-        gate_turned = acc_banks[0]
+        gate_turned = banks[7]
         nc.tensor.transpose(gate_turned[:, 0:P], gate_rows[:], ident[:])
         gate_cols = keep.tile([P, E], F32, name="gate_cols")
         nc.scalar.copy(gate_cols[:], gate_turned[:, 0:E])
         gates = keep.tile([P, T], F32, name="gates")
         for first in range(0, E, 4):
             count = min(4, E - first)
-            spread = acc_banks[1 + first // 4]
+            spread = banks[4 + first // 4]
             for j in range(count):
                 column = gate_cols[:, first + j : first + j + 1]
                 nc.tensor.transpose(spread[:, j * C : (j + 1) * C], column.to_broadcast([P, P]), ident[:])
             nc.scalar.copy(gates[:, first * C : (first + count) * C], spread[:, 0 : count * C])
 
-        gw = {}
+        gw = [keep.tile([P, COLD * C], U32, name="gw%d" % s, align_bytes=64) for s in range(PASSES)]
         gs = {}
 
+        def word_columns(a, b):
+            start = a - HOT * C if a >= HOT * C else a + HOT_WORDS_AT
+            return slice(start, start + b - a)
+
         def gather_words(a, b, s):
-            tile = keep.tile([P, b - a], U32, name="gw%d_%d" % (a, s), align_bytes=64)
-            nc.vector.tensor_copy(tile[:], xw[s].bitcast(U32).indirect(listed(a, b)))
-            for e in range(a // C, b // C):
-                gw[(e, s)] = tile[:, e * C - a : (e + 1) * C - a]
+            nc.vector.tensor_copy(gw[s][:, word_columns(a, b)], xw[s].bitcast(U32).indirect(listed(a, b)))
 
         def gather_scales(a, b, shifted):
             tile = keep.tile([P, b - a], U8, name="gs%d" % a, align_bytes=64)
@@ -160,12 +160,12 @@ def tile_moe_hot_mlp_silu_kernel(
                         a = j * PASSES + s
                         rhs = w1[g][:, a * 2 * H : (a + 1) * 2 * H].bitcast(FP4X4)
                         f = e - HOT
-                        rhs_scale = s1c[:, f * PASSES + s, :]
+                        rhs_scale = s1c[f // 4][:, (f % 4) * PASSES + s, :]
                     else:
                         rhs = w1[g][:, s * 4 * H : (s + 1) * 4 * H].bitcast(FP8X4)
                         rhs_scale = s1h[:, e * PASSES + s, :]
                     nc.tensor.matmul_mx(
-                        out=acc[:], lhsT=gw[(e, s)].bitcast(FP8X4), lhsT_scale=gs[(e, s)],
+                        out=acc[:], lhsT=gw[s][:, word_columns(e * C, (e + 1) * C)].bitcast(FP8X4), lhsT_scale=gs[(e, s)],
                         rhs=rhs, rhs_scale=rhs_scale, start=(s == 0), stop=(s == PASSES - 1),
                     )
                 hid = work.tile([P, 2, P, 2], BF16, name="hid", align_bytes=64)
@@ -212,19 +212,22 @@ def tile_moe_hot_mlp_silu_kernel(
         def scatter(h, a, b):
             nc.vector.tensor_tensor(outs[h][:].indirect(listed(a, b)), ys[:, h, a:b], gates[:, a:b], MULT)
 
-        pieces = [(256, 768, shift_a), (768, 1280, shift_b), (0, 256, None)]
-        for a, b, shifted in pieces:
-            gather_words(a, b, 0)
-        for a, b, shifted in pieces:
-            gather_scales(a, b, shifted)
-        for a, b, shifted in pieces:
+        gather_words(256, 768, 0)
+        gather_scales(256, 768, shift_a)
+        gather_scales(768, 1280, shift_b)
+        gather_words(768, 1280, 0)
+        for a, b in ((256, 512), (512, 768), (768, 1280)):
             for s in range(1, PASSES):
                 gather_words(a, b, s)
+        gather_scales(0, 256, None)
 
         spans = [(320, 512), (512, 768), (768, 1024), (1024, 1280), (160, 320), (0, 160)]
         last = len(GROUPS) - 1
         for g in range(len(GROUPS)):
             first_layer(g)
+            if g == 2:
+                for s in range(PASSES):
+                    gather_words(0, HOT * C, s)
             quantize(g)
             if g > 0:
                 second_layer(g - 1, 1)

@@ -22,9 +22,7 @@ PASSES = K // 512
 COLD = E - HOT
 HALVES = N // P
 SHIFT_ROWS = 112
-HOT_WORDS_AT = 4 * C
 GROUPS = [[2, 3], [4, 5], [6, 7], [8, 9], [1], [0]]
-ORDER = [e for group in GROUPS for e in group]
 
 
 def tile_moe_hot_mlp_silu_kernel(
@@ -34,15 +32,14 @@ def tile_moe_hot_mlp_silu_kernel(
     nc = tc.nc
     with ExitStack() as ctx:
         keep = ctx.enter_context(tc.tile_pool(name="keep", bufs=1))
-        work = ctx.enter_context(tc.tile_pool(name="work", bufs=4))
+        work = ctx.enter_context(tc.tile_pool(name="work", bufs=6))
         psum = ctx.enter_context(tc.psum_pool(name="psum", bufs=1))
         banks = [psum.tile([P, H], F32, name="bank%d" % b) for b in range(8)]
-        acc_banks, turn_banks, y_banks = banks[0:4], banks[4:6], banks[6:8]
 
-        def zeroed_plane(name, shape):
+        def zeroed_plane(name, shape, engine=nc.vector):
             plane = keep.tile(shape, U8, name=name, align_bytes=64)
             flat = plane[:] if len(shape) == 2 else plane[:].rearrange("p a b -> p (a b)")
-            nc.vector.memset(flat.bitcast(I32), 0)
+            engine.memset(flat.bitcast(I32), 0)
             return plane
 
         def load_plane(queue, plane, scales):
@@ -63,73 +60,46 @@ def tile_moe_hot_mlp_silu_kernel(
 
         gate_rows = keep.tile([P, C], F32, name="gate_rows")
         nc.scalar.dma_start(gate_rows[:], gate.rearrange("o (e c) -> (o e) c", c=C)[0:P, :])
-        ident = keep.tile([P, P], F32, name="ident")
-        make_identity(nc, ident[:])
         xs = zeroed_plane("xs", [P, T])
         s1c = [zeroed_plane("s1c_a", [P, 4 * PASSES, H])]
+        ident = keep.tile([P, P], F32, name="ident")
+        make_identity(nc, ident[:])
         s2c = zeroed_plane("s2c", [P, COLD, N])
         shift_a = zeroed_plane("shift_a", [P, PASSES - 1, 4 * C])
         shift_b = zeroed_plane("shift_b", [P, PASSES - 1, 4 * C])
-        s1c.append(zeroed_plane("s1c_b", [P, 4 * PASSES, H]))
-        s1h = zeroed_plane("s1h", [P, HOT * PASSES, H])
-        s2h = zeroed_plane("s2h", [P, HOT, N])
+        s1c.append(zeroed_plane("s1c_b", [P, 4 * PASSES, H], nc.gpsimd))
+        s1h = zeroed_plane("s1h", [P, HOT * PASSES, H], nc.gpsimd)
+        s2h = zeroed_plane("s2h", [P, HOT, N], nc.gpsimd)
         for q in range(4):
             nc.scalar.dma_start(
                 xs[32 * q : 32 * q + 4 * PASSES, :].bitcast(I32),
                 x_scales[:, 4 * q : 4 * q + 4, :].bitcast(I32),
             )
-        load_plane(nc.gpsimd, s1c[0], w1c_scales[0:4])
-        load_plane(nc.gpsimd, s2c, w2c_scales)
-        load_plane(nc.gpsimd, s1h, w1h_scales)
-        load_plane(nc.gpsimd, s2h, w2h_scales)
         w2c = keep.tile([P, COLD, 2 * N], U8, name="w2c", align_bytes=64)
         w2h = keep.tile([P, HOT, 4 * N], U8, name="w2h", align_bytes=64)
 
+        gates = keep.tile([P, T], F32, name="gates")
         w1 = {}
 
-        def load_w1(g):
-            tile = keep.tile([P, 2 * PASSES * 2 * H], U8, name="w1_%d" % g, align_bytes=64)
-            first = GROUPS[g][0]
+        def load_w1(first):
+            tile = keep.tile([P, 2 * PASSES * 2 * H], U8, name="w1_%d" % first, align_bytes=64)
             if first >= HOT:
                 src = w1c_words[first - HOT : first - HOT + 2].rearrange("e s p b -> p (e s) b")
                 nc.sync.dma_start(tile[:].rearrange("p (a b) -> p a b", b=2 * H).bitcast(I32), src.bitcast(I32))
             else:
                 src = w1h_words[first].rearrange("s p i d -> p s (i d)")
                 nc.sync.dma_start(tile[:].rearrange("p (a b) -> p a b", b=4 * H).bitcast(I32), src.bitcast(I32))
-            w1[g] = tile
+            w1[first] = tile
 
-        load_w1(0)
-        load_w1(1)
-        nc.sync.dma_start(w2c[:].bitcast(I32), w2c_words.rearrange("e s p b -> p (e s) b").bitcast(I32))
-        load_w1(2)
-        load_plane(nc.sync, s1c[1], w1c_scales[4:8])
-        load_w1(3)
-        nc.sync.dma_start(w2h[:].bitcast(I32), w2h_words.rearrange("e s p n d -> p (e s) (n d)").bitcast(I32))
-        load_w1(4)
-        load_w1(5)
+        def load_w2c(a, b):
+            src = w2c_words[a:b].rearrange("e s p b -> p (e s) b")
+            nc.sync.dma_start(w2c[:, a:b, :].bitcast(I32), src.bitcast(I32))
 
-        gate_turned = banks[7]
-        nc.tensor.transpose(gate_turned[:, 0:P], gate_rows[:], ident[:])
-        gate_cols = keep.tile([P, E], F32, name="gate_cols")
-        nc.scalar.copy(gate_cols[:], gate_turned[:, 0:E])
-        gates = keep.tile([P, T], F32, name="gates")
-        for first in range(0, E, 4):
-            count = min(4, E - first)
-            spread = banks[4 + first // 4]
-            for j in range(count):
-                column = gate_cols[:, first + j : first + j + 1]
-                nc.tensor.transpose(spread[:, j * C : (j + 1) * C], column.to_broadcast([P, P]), ident[:])
-            nc.scalar.copy(gates[:, first * C : (first + count) * C], spread[:, 0 : count * C])
-
-        gw = [keep.tile([P, COLD * C], U32, name="gw%d" % s, align_bytes=64) for s in range(PASSES)]
+        gw = [keep.tile([P, T], U32, name="gw%d" % s, align_bytes=64) for s in range(PASSES)]
         gs = {}
 
-        def word_columns(a, b):
-            start = a - HOT * C if a >= HOT * C else a + HOT_WORDS_AT
-            return slice(start, start + b - a)
-
         def gather_words(a, b, s):
-            nc.vector.tensor_copy(gw[s][:, word_columns(a, b)], xw[s].bitcast(U32).indirect(listed(a, b)))
+            nc.vector.tensor_copy(gw[s][:, a:b], xw[s].bitcast(U32).indirect(listed(a, b)))
 
         def gather_scales(a, b, shifted):
             tile = keep.tile([P, b - a], U8, name="gs%d" % a, align_bytes=64)
@@ -141,10 +111,41 @@ def tile_moe_hot_mlp_silu_kernel(
                     gs[(e, s)] = tile[4 * s : P, cols] if shifted is None else shifted[:, s - 1, cols]
             if shifted is not None:
                 for s in range(1, PASSES):
-                    nc.scalar.dma_start(
+                    nc.sync.dma_start(
                         shifted[0:SHIFT_ROWS, s - 1, :].bitcast(I32),
                         tile[4 * s : 4 * s + SHIFT_ROWS, :].bitcast(I32),
                     )
+
+        gather_words(256, 768, 0)
+        gather_words(768, 1280, 0)
+        load_plane(nc.sync, s2c, w2c_scales)
+        load_plane(nc.sync, s1c[0], w1c_scales[0:4])
+        load_w1(2)
+        gather_scales(256, 768, shift_a)
+        load_w1(4)
+        gather_scales(768, 1280, shift_b)
+        load_plane(nc.sync, s2h, w2h_scales)
+        load_plane(nc.sync, s1h, w1h_scales)
+        load_plane(nc.sync, s1c[1], w1c_scales[4:8])
+        load_w2c(0, 4)
+        load_w1(6)
+        load_w1(8)
+        load_w2c(4, 8)
+        load_w1(1)
+        load_w1(0)
+        nc.sync.dma_start(w2h[:].bitcast(I32), w2h_words.rearrange("e s p n d -> p (e s) (n d)").bitcast(I32))
+
+        gate_turned = banks[7]
+        nc.tensor.transpose(gate_turned[:, 0:P], gate_rows[:], ident[:])
+        gate_cols = keep.tile([P, E], F32, name="gate_cols")
+        nc.scalar.copy(gate_cols[:], gate_turned[:, 0:E])
+        for first in range(0, E, 4):
+            count = min(4, E - first)
+            spread = banks[6 + (first // 4) % 2]
+            for j in range(count):
+                column = gate_cols[:, first + j : first + j + 1]
+                nc.tensor.transpose(spread[:, j * C : (j + 1) * C], column.to_broadcast([P, P]), ident[:])
+            nc.scalar.copy(gates[:, first * C : (first + count) * C], spread[:, 0 : count * C])
 
         ys = keep.tile([P, HALVES, T], F32, name="ys")
         outs = [keep.tile([P, T], F32, name="out%d" % h) for h in range(HALVES)]
@@ -152,24 +153,27 @@ def tile_moe_hot_mlp_silu_kernel(
 
         def first_layer(g):
             experts = GROUPS[g]
-            turned = turn_banks[g % 2][:, 0 : len(experts) * 2 * C].rearrange("p (j u c) -> p j u c", u=2, c=C)
+            turned = banks[2 * (g % 3) + 1][:, 0 : len(experts) * 2 * C].rearrange("p (j u c) -> p j u c", u=2, c=C)
+            hids = []
             for j, e in enumerate(experts):
-                acc = acc_banks[ORDER.index(e) % 4]
+                acc = banks[2 * (g % 3) + j]
                 for s in range(PASSES):
                     if e >= HOT:
                         a = j * PASSES + s
-                        rhs = w1[g][:, a * 2 * H : (a + 1) * 2 * H].bitcast(FP4X4)
+                        rhs = w1[experts[0]][:, a * 2 * H : (a + 1) * 2 * H].bitcast(FP4X4)
                         f = e - HOT
                         rhs_scale = s1c[f // 4][:, (f % 4) * PASSES + s, :]
                     else:
-                        rhs = w1[g][:, s * 4 * H : (s + 1) * 4 * H].bitcast(FP8X4)
+                        rhs = w1[e][:, s * 4 * H : (s + 1) * 4 * H].bitcast(FP8X4)
                         rhs_scale = s1h[:, e * PASSES + s, :]
                     nc.tensor.matmul_mx(
-                        out=acc[:], lhsT=gw[s][:, word_columns(e * C, (e + 1) * C)].bitcast(FP8X4), lhsT_scale=gs[(e, s)],
+                        out=acc[:], lhsT=gw[s][:, e * C : (e + 1) * C].bitcast(FP8X4), lhsT_scale=gs[(e, s)],
                         rhs=rhs, rhs_scale=rhs_scale, start=(s == 0), stop=(s == PASSES - 1),
                     )
                 hid = work.tile([P, 2, P, 2], BF16, name="hid", align_bytes=64)
                 nc.scalar.activation(hid[:], acc[:].rearrange("c (p u v) -> c u p v", u=2, v=2), SILU)
+                hids.append(hid)
+            for j, hid in enumerate(hids):
                 pairs = hid[:].rearrange("c u p v -> c (u p v)").bitcast(F32)
                 for u in range(2):
                     nc.tensor.transpose(turned[:, j, u, :], pairs[:, u * P : (u + 1) * P], ident[:])
@@ -193,7 +197,7 @@ def tile_moe_hot_mlp_silu_kernel(
             experts = GROUPS[g]
             width = len(experts) * C
             codes, scales = hq[g]
-            y = y_banks[g % 2] if h == 0 else turn_banks[(g + 1) % 2]
+            y = banks[2 * (g % 3)] if h == 0 else banks[2 * ((g if g < 2 else g + 1) % 3) + 1]
             for j, e in enumerate(experts):
                 cols = slice(j * C, (j + 1) * C)
                 if e >= HOT:
@@ -212,22 +216,18 @@ def tile_moe_hot_mlp_silu_kernel(
         def scatter(h, a, b):
             nc.vector.tensor_tensor(outs[h][:].indirect(listed(a, b)), ys[:, h, a:b], gates[:, a:b], MULT)
 
-        gather_words(256, 768, 0)
-        gather_scales(256, 768, shift_a)
-        gather_scales(768, 1280, shift_b)
-        gather_words(768, 1280, 0)
         for a, b in ((256, 512), (512, 768), (768, 1280)):
             for s in range(1, PASSES):
                 gather_words(a, b, s)
+        gather_words(0, 256, 0)
         gather_scales(0, 256, None)
+        for s in range(1, PASSES):
+            gather_words(0, 256, s)
 
         spans = [(320, 512), (512, 768), (768, 1024), (1024, 1280), (160, 320), (0, 160)]
         last = len(GROUPS) - 1
         for g in range(len(GROUPS)):
             first_layer(g)
-            if g == 2:
-                for s in range(PASSES):
-                    gather_words(0, HOT * C, s)
             quantize(g)
             if g > 0:
                 second_layer(g - 1, 1)

@@ -22,7 +22,8 @@ PASSES = K // 512
 COLD = E - HOT
 HALVES = N // P
 SHIFT_ROWS = 112
-GROUPS = [[2, 3], [4, 5], [6, 7], [8, 9], [1], [0]]
+HOT_ROW = 4
+GROUPS = [[2, 3], [4, 5], [6, 7], [8, 9], [0, 1]]
 
 
 def tile_moe_hot_mlp_silu_kernel(
@@ -36,16 +37,16 @@ def tile_moe_hot_mlp_silu_kernel(
         psum = ctx.enter_context(tc.psum_pool(name="psum", bufs=1))
         banks = [psum.tile([P, H], F32, name="bank%d" % b) for b in range(8)]
 
-        def zeroed_plane(name, shape, engine=nc.vector):
+        def zeroed_plane(name, shape):
             plane = keep.tile(shape, U8, name=name, align_bytes=64)
             flat = plane[:] if len(shape) == 2 else plane[:].rearrange("p a b -> p (a b)")
-            engine.memset(flat.bitcast(I32), 0)
+            nc.vector.memset(flat.bitcast(I32), 0)
             return plane
 
-        def load_plane(queue, plane, scales):
+        def load_plane(queue, plane, scales, row):
             rows = scales.rearrange("e s (q r) w -> r q (e s) w", r=4)
             for r in range(4):
-                queue.dma_start(plane[r:P:32, :, :].bitcast(I32), rows[r].bitcast(I32))
+                queue.dma_start(plane[row + r : P : 32, :, :].bitcast(I32), rows[r].bitcast(I32))
 
         def listed(a, b):
             return offsets[:, a // 16 : b // 16]
@@ -54,52 +55,57 @@ def tile_moe_hot_mlp_silu_kernel(
         xw_rest = keep.tile([P, PASSES - 1, T], I32, name="xw_rest", align_bytes=64)
         xw = [xw_first[:]] + [xw_rest[:, s, :] for s in range(PASSES - 1)]
         offsets = keep.tile([P, T // 16], U16, name="offsets")
+        xs = zeroed_plane("xs", [P, T])
+        gate_rows = keep.tile([P, C], F32, name="gate_rows")
+        nc.vector.memset(gate_rows[:], 0.0)
         nc.sync.dma_start(xw_first[:], x_words[0].rearrange("p t d -> p (t d)").bitcast(I32))
         nc.sync.dma_start(offsets[:], offs)
-        nc.sync.dma_start(xw_rest[:], x_words[1:PASSES].rearrange("s p t d -> p s (t d)").bitcast(I32))
-
-        gate_rows = keep.tile([P, C], F32, name="gate_rows")
-        nc.scalar.dma_start(gate_rows[:], gate.rearrange("o (e c) -> (o e) c", c=C)[0:P, :])
-        xs = zeroed_plane("xs", [P, T])
-        s1c = [zeroed_plane("s1c_a", [P, 4 * PASSES, H])]
-        ident = keep.tile([P, P], F32, name="ident")
-        make_identity(nc, ident[:])
-        s2c = zeroed_plane("s2c", [P, COLD, N])
-        shift_a = zeroed_plane("shift_a", [P, PASSES - 1, 4 * C])
-        shift_b = zeroed_plane("shift_b", [P, PASSES - 1, 4 * C])
-        s1c.append(zeroed_plane("s1c_b", [P, 4 * PASSES, H], nc.gpsimd))
-        s1h = zeroed_plane("s1h", [P, HOT * PASSES, H], nc.gpsimd)
-        s2h = zeroed_plane("s2h", [P, HOT, N], nc.gpsimd)
         for q in range(4):
-            nc.scalar.dma_start(
+            queue = nc.sync if q % 2 else nc.scalar
+            queue.dma_start(
                 xs[32 * q : 32 * q + 4 * PASSES, :].bitcast(I32),
                 x_scales[:, 4 * q : 4 * q + 4, :].bitcast(I32),
             )
+        nc.scalar.dma_start(gate_rows[0:E, :], gate[0:1, :].rearrange("o (e c) -> (o e) c", c=C))
+        nc.sync.dma_start(xw_rest[:], x_words[1:PASSES].rearrange("s p t d -> p s (t d)").bitcast(I32))
+
+        s1 = [zeroed_plane("s1_a", [P, 4 * PASSES, H])]
+        s2 = zeroed_plane("s2", [P, COLD, N])
+        shifts = [zeroed_plane("shift%d" % b, [P, PASSES - 1, 4 * C]) for b in range(2)]
+        s1.append(zeroed_plane("s1_b", [P, 4 * PASSES, H]))
+        ident = keep.tile([P, P], F32, name="ident")
+        make_identity(nc, ident[:])
         w2c = keep.tile([P, COLD, 2 * N], U8, name="w2c", align_bytes=64)
         w2h = keep.tile([P, HOT, 4 * N], U8, name="w2h", align_bytes=64)
+        s1_hot = s1[1][:, 2 * PASSES : 4 * PASSES, :]
+        s2_hot = s2[:, COLD - HOT : COLD, :]
 
         gates = keep.tile([P, T], F32, name="gates")
         w1 = {}
 
-        def load_w1(first):
-            tile = keep.tile([P, 2 * PASSES * 2 * H], U8, name="w1_%d" % first, align_bytes=64)
+        def load_w1(first, count):
+            width = 2 * H if first >= HOT else 4 * H
+            tile = keep.tile([P, count * PASSES, width], U8, name="w1_%d" % first, align_bytes=64)
             if first >= HOT:
-                src = w1c_words[first - HOT : first - HOT + 2].rearrange("e s p b -> p (e s) b")
-                nc.sync.dma_start(tile[:].rearrange("p (a b) -> p a b", b=2 * H).bitcast(I32), src.bitcast(I32))
+                src = w1c_words[first - HOT : first - HOT + count].rearrange("e s p b -> p (e s) b")
             else:
-                src = w1h_words[first].rearrange("s p i d -> p s (i d)")
-                nc.sync.dma_start(tile[:].rearrange("p (a b) -> p a b", b=4 * H).bitcast(I32), src.bitcast(I32))
-            w1[first] = tile
+                src = w1h_words[first : first + count].rearrange("e s p i d -> p (e s) (i d)")
+            nc.sync.dma_start(tile[:].bitcast(I32), src.bitcast(I32))
+            for j in range(count):
+                for s in range(PASSES):
+                    w1[(first + j, s)] = tile[:, j * PASSES + s, :]
 
         def load_w2c(a, b):
             src = w2c_words[a:b].rearrange("e s p b -> p (e s) b")
             nc.sync.dma_start(w2c[:, a:b, :].bitcast(I32), src.bitcast(I32))
 
-        gw = [keep.tile([P, T], U32, name="gw%d" % s, align_bytes=64) for s in range(PASSES)]
+        gw = {}
         gs = {}
 
-        def gather_words(a, b, s):
-            nc.vector.tensor_copy(gw[s][:, a:b], xw[s].bitcast(U32).indirect(listed(a, b)))
+        def gather_words(tile, a, b, s):
+            nc.vector.tensor_copy(tile, xw[s].bitcast(U32).indirect(listed(a, b)))
+            for e in range(a // C, b // C):
+                gw[(e, s)] = tile[:, e * C - a : (e + 1) * C - a]
 
         def gather_scales(a, b, shifted):
             tile = keep.tile([P, b - a], U8, name="gs%d" % a, align_bytes=64)
@@ -109,30 +115,37 @@ def tile_moe_hot_mlp_silu_kernel(
                 gs[(e, 0)] = tile[:, cols]
                 for s in range(1, PASSES):
                     gs[(e, s)] = tile[4 * s : P, cols] if shifted is None else shifted[:, s - 1, cols]
-            if shifted is not None:
-                for s in range(1, PASSES):
-                    nc.sync.dma_start(
-                        shifted[0:SHIFT_ROWS, s - 1, :].bitcast(I32),
-                        tile[4 * s : 4 * s + SHIFT_ROWS, :].bitcast(I32),
-                    )
+            return tile
 
-        gather_words(256, 768, 0)
-        gather_words(768, 1280, 0)
-        load_plane(nc.sync, s2c, w2c_scales)
-        load_plane(nc.sync, s1c[0], w1c_scales[0:4])
-        load_w1(2)
-        gather_scales(256, 768, shift_a)
-        load_w1(4)
-        gather_scales(768, 1280, shift_b)
-        load_plane(nc.sync, s2h, w2h_scales)
-        load_plane(nc.sync, s1h, w1h_scales)
-        load_plane(nc.sync, s1c[1], w1c_scales[4:8])
+        def shift_planes(queue, shifted, tile):
+            for s in range(1, PASSES):
+                queue.dma_start(
+                    shifted[0:SHIFT_ROWS, s - 1, :].bitcast(I32),
+                    tile[4 * s : 4 * s + SHIFT_ROWS, :].bitcast(I32),
+                )
+
+        PAIR = 2 * C
+        gathered = [keep.tile([P, T], U32, name="gw%d" % s, align_bytes=64) for s in range(PASSES)]
+        gather_words(gathered[0][:, 256:768], 256, 768, 0)
+        shift_planes(nc.scalar, shifts[0], gather_scales(256, 768, shifts[0]))
+        scales_b = gather_scales(768, 1280, shifts[1])
+        gather_scales(0, 256, None)
+
+        load_plane(nc.sync, s1[0], w1c_scales[0:4], 0)
+        load_w1(2, 1)
+        load_w1(3, 1)
+        load_plane(nc.sync, s2, w2c_scales, 0)
         load_w2c(0, 4)
-        load_w1(6)
-        load_w1(8)
+        load_w1(4, 2)
+        shift_planes(nc.sync, shifts[1], scales_b)
+        load_plane(nc.sync, s1[1], w1c_scales[4:8], 0)
+        load_w1(6, 2)
         load_w2c(4, 8)
-        load_w1(1)
-        load_w1(0)
+        load_plane(nc.sync, s1_hot, w1h_scales, HOT_ROW)
+        load_plane(nc.sync, s2_hot, w2h_scales, HOT_ROW)
+        load_w1(8, 2)
+        load_w1(0, 1)
+        load_w1(1, 1)
         nc.sync.dma_start(w2h[:].bitcast(I32), w2h_words.rearrange("e s p n d -> p (e s) (n d)").bitcast(I32))
 
         gate_turned = banks[7]
@@ -141,101 +154,96 @@ def tile_moe_hot_mlp_silu_kernel(
         nc.scalar.copy(gate_cols[:], gate_turned[:, 0:E])
         for first in range(0, E, 4):
             count = min(4, E - first)
-            spread = banks[6 + (first // 4) % 2]
+            spread = banks[4 + first // 4]
             for j in range(count):
                 column = gate_cols[:, first + j : first + j + 1]
                 nc.tensor.transpose(spread[:, j * C : (j + 1) * C], column.to_broadcast([P, P]), ident[:])
             nc.scalar.copy(gates[:, first * C : (first + count) * C], spread[:, 0 : count * C])
 
-        ys = keep.tile([P, HALVES, T], F32, name="ys")
-        outs = [keep.tile([P, T], F32, name="out%d" % h) for h in range(HALVES)]
-        hq_in = {}
+        for a, b in ((256, 512), (512, 768)):
+            for s in range(1, PASSES):
+                gather_words(gathered[s][:, a:b], a, b, s)
+        after_scales = keep.tile([P, 512], U32, name="xs", align_bytes=64)
+        gather_words(after_scales[:], 768, 1280, 0)
+        for s in range(1, PASSES):
+            gather_words(gathered[s][:, 768:1280], 768, 1280, s)
 
-        def first_layer(g):
-            experts = GROUPS[g]
-            turned = banks[2 * (g % 3) + 1][:, 0 : len(experts) * 2 * C].rearrange("p (j u c) -> p j u c", u=2, c=C)
+        outs = [keep.tile([P, T], F32, name="out%d" % h) for h in range(HALVES)]
+
+        def first_products(g):
             hids = []
-            for j, e in enumerate(experts):
-                acc = banks[2 * (g % 3) + j]
+            for j, e in enumerate(GROUPS[g]):
+                acc = banks[(g + j) % 3]
                 for s in range(PASSES):
                     if e >= HOT:
-                        a = j * PASSES + s
-                        rhs = w1[experts[0]][:, a * 2 * H : (a + 1) * 2 * H].bitcast(FP4X4)
                         f = e - HOT
-                        rhs_scale = s1c[f // 4][:, (f % 4) * PASSES + s, :]
+                        rhs = w1[(e, s)].bitcast(FP4X4)
+                        rhs_scale = s1[f // 4][:, (f % 4) * PASSES + s, :]
                     else:
-                        rhs = w1[e][:, s * 4 * H : (s + 1) * 4 * H].bitcast(FP8X4)
-                        rhs_scale = s1h[:, e * PASSES + s, :]
+                        rhs = w1[(e, s)].bitcast(FP8X4)
+                        rhs_scale = s1_hot[HOT_ROW:P, e * PASSES + s, :]
                     nc.tensor.matmul_mx(
-                        out=acc[:], lhsT=gw[s][:, e * C : (e + 1) * C].bitcast(FP8X4), lhsT_scale=gs[(e, s)],
+                        out=acc[:], lhsT=gw[(e, s)].bitcast(FP8X4), lhsT_scale=gs[(e, s)],
                         rhs=rhs, rhs_scale=rhs_scale, start=(s == 0), stop=(s == PASSES - 1),
                     )
-                hid = work.tile([P, 2, P, 2], BF16, name="hid", align_bytes=64)
+                hid = keep.tile([P, 2, P, 2], BF16, name="hid%d" % e, align_bytes=64)
                 nc.scalar.activation(hid[:], acc[:].rearrange("c (p u v) -> c u p v", u=2, v=2), SILU)
-                hids.append(hid)
-            for j, hid in enumerate(hids):
-                pairs = hid[:].rearrange("c u p v -> c (u p v)").bitcast(F32)
+                hids.append(hid[:].rearrange("c u p v -> c (u p v)").bitcast(F32))
+            return hids
+
+        def turn_and_quantize(g, hids):
+            turned = banks[(g + 2) % 3][:].rearrange("p (j u c) -> p j u c", u=2, c=C)
+            for j, pairs in enumerate(hids):
                 for u in range(2):
                     nc.tensor.transpose(turned[:, j, u, :], pairs[:, u * P : (u + 1) * P], ident[:])
-            grouped = work.tile([P, len(experts) * C * 4], BF16, name="grouped", align_bytes=64)
+            grouped = keep.tile([P, PAIR * 4], BF16, name="grouped%d" % g, align_bytes=64)
             nc.scalar.copy(
                 grouped[:].bitcast(F32).rearrange("p (j c u) -> p j c u", u=2, c=C),
                 turned.rearrange("p j u c -> p j c u"),
             )
-            hq_in[g] = grouped
+            codes = work.tile([P, PAIR], U32, name="codes", align_bytes=64)
+            scales = work.tile([P, PAIR], U8, name="scales", align_bytes=64)
+            nc.vector.quantize_mx(out=codes[:].bitcast(FP8X4), scales=scales[:], in_=grouped[:])
+            return codes, scales
 
-        hq = {}
+        def second_products(g, codes, scales):
+            for h in range(HALVES):
+                for j, e in enumerate(GROUPS[g]):
+                    cols = slice(j * C, (j + 1) * C)
+                    if e >= HOT:
+                        lhsT = w2c[:, e - HOT, h * 2 * P : (h + 1) * 2 * P].bitcast(FP4X4)
+                        lhsT_scale = s2[:, e - HOT, h * P : (h + 1) * P]
+                    else:
+                        lhsT = w2h[:, e, h * 4 * P : (h + 1) * 4 * P].bitcast(FP8X4)
+                        lhsT_scale = s2_hot[HOT_ROW:P, e, h * P : (h + 1) * P]
+                    nc.tensor.matmul_mx(
+                        out=banks[(g + 1) % 3][:, h * PAIR + j * C : h * PAIR + (j + 1) * C],
+                        lhsT=lhsT, lhsT_scale=lhsT_scale,
+                        rhs=codes[:, cols].bitcast(FP8X4), rhs_scale=scales[:, cols], start=True, stop=True,
+                    )
 
-        def quantize(g):
-            width = len(GROUPS[g]) * C
-            codes = work.tile([P, width], U32, name="codes", align_bytes=64)
-            scales = work.tile([P, width], U8, name="scales", align_bytes=64)
-            nc.vector.quantize_mx(out=codes[:].bitcast(FP8X4), scales=scales[:], in_=hq_in[g][:])
-            hq[g] = (codes, scales)
+        def scatter(g, h, staged):
+            a = GROUPS[g][0] * C
+            nc.scalar.copy(staged, banks[(g + 1) % 3][:, h * PAIR : (h + 1) * PAIR])
+            nc.vector.tensor_tensor(outs[h][:].indirect(listed(a, a + PAIR)), staged, gates[:, a : a + PAIR], MULT)
 
-        def second_layer(g, h):
-            experts = GROUPS[g]
-            width = len(experts) * C
-            codes, scales = hq[g]
-            y = banks[2 * (g % 3)] if h == 0 else banks[2 * ((g if g < 2 else g + 1) % 3) + 1]
-            for j, e in enumerate(experts):
-                cols = slice(j * C, (j + 1) * C)
-                if e >= HOT:
-                    lhsT = w2c[:, e - HOT, h * 2 * P : (h + 1) * 2 * P].bitcast(FP4X4)
-                    lhsT_scale = s2c[:, e - HOT, h * P : (h + 1) * P]
-                else:
-                    lhsT = w2h[:, e, h * 4 * P : (h + 1) * 4 * P].bitcast(FP8X4)
-                    lhsT_scale = s2h[:, e, h * P : (h + 1) * P]
-                nc.tensor.matmul_mx(
-                    out=y[:, cols], lhsT=lhsT, lhsT_scale=lhsT_scale,
-                    rhs=codes[:, cols].bitcast(FP8X4), rhs_scale=scales[:, cols], start=True, stop=True,
-                )
-            a = experts[0] * C
-            nc.scalar.copy(ys[:, h, a : a + width], y[:, 0:width])
-
-        def scatter(h, a, b):
-            nc.vector.tensor_tensor(outs[h][:].indirect(listed(a, b)), ys[:, h, a:b], gates[:, a:b], MULT)
-
-        for a, b in ((256, 512), (512, 768), (768, 1280)):
-            for s in range(1, PASSES):
-                gather_words(a, b, s)
-        gather_words(0, 256, 0)
-        gather_scales(0, 256, None)
-        for s in range(1, PASSES):
-            gather_words(0, 256, s)
-
-        spans = [(320, 512), (512, 768), (768, 1024), (1024, 1280), (160, 320), (0, 160)]
         last = len(GROUPS) - 1
+        quantized = None
         for g in range(len(GROUPS)):
-            first_layer(g)
-            quantize(g)
+            hids = first_products(g)
             if g > 0:
-                second_layer(g - 1, 1)
-            second_layer(g, 0)
+                second_products(g - 1, *quantized)
+                staged = work.tile([P, PAIR], F32, name="staged")
+                scatter(g - 1, 0, staged[:])
+            quantized = turn_and_quantize(g, hids)
             if g > 0:
-                scatter(1, *spans[g - 1])
-            scatter(0, *spans[g])
-        nc.sync.dma_start(out[0:P, :], outs[0][:])
-        second_layer(last, 1)
-        scatter(1, *spans[last])
-        nc.sync.dma_start(out[P : 2 * P, :], outs[1][:])
+                scatter(g - 1, 1, hids[1])
+            else:
+                late = keep.tile([P, PASSES, PAIR], U32, name="grouped0", align_bytes=64)
+                for s in range(PASSES):
+                    gather_words(late[:, s, :], 0, PAIR, s)
+        second_products(last, *quantized)
+        for h in range(HALVES):
+            staged = work.tile([P, PAIR], F32, name="staged")
+            scatter(last, h, staged[:])
+            nc.sync.dma_start(out[h * P : (h + 1) * P, :], outs[h][:])

@@ -37,10 +37,10 @@ def tile_moe_hot_mlp_silu_kernel(
         psum = ctx.enter_context(tc.psum_pool(name="psum", bufs=1))
         banks = [psum.tile([P, H], F32, name="bank%d" % b) for b in range(8)]
 
-        def zeroed_plane(name, shape):
+        def zeroed_plane(name, shape, engine=nc.vector):
             plane = keep.tile(shape, U8, name=name, align_bytes=64)
             flat = plane[:] if len(shape) == 2 else plane[:].rearrange("p a b -> p (a b)")
-            nc.vector.memset(flat.bitcast(I32), 0)
+            engine.memset(flat.bitcast(I32), 0)
             return plane
 
         def load_plane(queue, plane, scales, row):
@@ -56,7 +56,7 @@ def tile_moe_hot_mlp_silu_kernel(
         xw = [xw_first[:]] + [xw_rest[:, s, :] for s in range(PASSES - 1)]
         offsets = keep.tile([P, T // 16], U16, name="offsets")
         xs = zeroed_plane("xs", [P, T])
-        gate_rows = keep.tile([P, C], F32, name="gate_rows")
+        gate_rows = keep.tile([P, C], F32, name="gate_rows", align_bytes=64)
         nc.vector.memset(gate_rows[:], 0.0)
         nc.sync.dma_start(xw_first[:], x_words[0].rearrange("p t d -> p (t d)").bitcast(I32))
         nc.sync.dma_start(offsets[:], offs)
@@ -67,14 +67,16 @@ def tile_moe_hot_mlp_silu_kernel(
                 x_scales[:, 4 * q : 4 * q + 4, :].bitcast(I32),
             )
         nc.scalar.dma_start(gate_rows[0:E, :], gate[0:1, :].rearrange("o (e c) -> (o e) c", c=C))
+        warm = keep.tile([P, 1], F32, name="warm")
+        nc.scalar.activation(warm[64:P, :], gate_rows[64:P, 0:1], SILU)
         nc.sync.dma_start(xw_rest[:], x_words[1:PASSES].rearrange("s p t d -> p s (t d)").bitcast(I32))
 
         s1 = [zeroed_plane("s1_a", [P, 4 * PASSES, H])]
         s2 = zeroed_plane("s2", [P, COLD, N])
         shifts = [zeroed_plane("shift%d" % b, [P, PASSES - 1, 4 * C]) for b in range(2)]
-        s1.append(zeroed_plane("s1_b", [P, 4 * PASSES, H]))
         ident = keep.tile([P, P], F32, name="ident")
         make_identity(nc, ident[:])
+        s1.append(zeroed_plane("s1_b", [P, 4 * PASSES, H], nc.gpsimd))
         w2c = keep.tile([P, COLD, 2 * N], U8, name="w2c", align_bytes=64)
         w2h = keep.tile([P, HOT, 4 * N], U8, name="w2h", align_bytes=64)
         s1_hot = s1[1][:, 2 * PASSES : 4 * PASSES, :]
@@ -102,13 +104,14 @@ def tile_moe_hot_mlp_silu_kernel(
         gw = {}
         gs = {}
 
-        def gather_words(tile, a, b, s):
+        def gather_words(a, b, s, name=None):
+            tile = keep.tile([P, b - a], U32, name=name or "gw%d_%d" % (s, a), align_bytes=64)[:]
             nc.vector.tensor_copy(tile, xw[s].bitcast(U32).indirect(listed(a, b)))
             for e in range(a // C, b // C):
                 gw[(e, s)] = tile[:, e * C - a : (e + 1) * C - a]
 
-        def gather_scales(a, b, shifted):
-            tile = keep.tile([P, b - a], U8, name="gs%d" % a, align_bytes=64)
+        def gather_scales(a, b, shifted, name=None):
+            tile = keep.tile([P, b - a], U8, name=name or "gs%d" % a, align_bytes=64)
             nc.vector.tensor_copy(tile[:], xs[:].indirect(listed(a, b)))
             for e in range(a // C, b // C):
                 cols = slice(e * C - a, (e + 1) * C - a)
@@ -125,18 +128,16 @@ def tile_moe_hot_mlp_silu_kernel(
                 )
 
         PAIR = 2 * C
-        gathered = [keep.tile([P, T], U32, name="gw%d" % s, align_bytes=64) for s in range(PASSES)]
-        gather_words(gathered[0][:, 256:768], 256, 768, 0)
+        gather_words(256, 768, 0)
         shift_planes(nc.scalar, shifts[0], gather_scales(256, 768, shifts[0]))
         scales_b = gather_scales(768, 1280, shifts[1])
-        gather_scales(0, 256, None)
 
         load_plane(nc.sync, s1[0], w1c_scales[0:4], 0)
         load_w1(2, 1)
         load_w1(3, 1)
-        load_plane(nc.sync, s2, w2c_scales, 0)
-        load_w2c(0, 4)
         load_w1(4, 2)
+        load_w2c(0, 4)
+        load_plane(nc.sync, s2, w2c_scales, 0)
         shift_planes(nc.sync, shifts[1], scales_b)
         load_plane(nc.sync, s1[1], w1c_scales[4:8], 0)
         load_w1(6, 2)
@@ -150,7 +151,7 @@ def tile_moe_hot_mlp_silu_kernel(
 
         gate_turned = banks[7]
         nc.tensor.transpose(gate_turned[:, 0:P], gate_rows[:], ident[:])
-        gate_cols = keep.tile([P, E], F32, name="gate_cols")
+        gate_cols = keep.tile([P, E], F32, name="gate_cols", align_bytes=64)
         nc.scalar.copy(gate_cols[:], gate_turned[:, 0:E])
         for first in range(0, E, 4):
             count = min(4, E - first)
@@ -162,11 +163,11 @@ def tile_moe_hot_mlp_silu_kernel(
 
         for a, b in ((256, 512), (512, 768)):
             for s in range(1, PASSES):
-                gather_words(gathered[s][:, a:b], a, b, s)
-        after_scales = keep.tile([P, 512], U32, name="xs", align_bytes=64)
-        gather_words(after_scales[:], 768, 1280, 0)
+                gather_words(a, b, s)
+        gather_words(768, 1280, 0, "gate_rows")
         for s in range(1, PASSES):
-            gather_words(gathered[s][:, 768:1280], 768, 1280, s)
+            gather_words(768, 1280, s)
+        gather_scales(0, 256, None, "gate_cols")
 
         outs = [keep.tile([P, T], F32, name="out%d" % h) for h in range(HALVES)]
 
@@ -241,7 +242,9 @@ def tile_moe_hot_mlp_silu_kernel(
             else:
                 late = keep.tile([P, PASSES, PAIR], U32, name="grouped0", align_bytes=64)
                 for s in range(PASSES):
-                    gather_words(late[:, s, :], 0, PAIR, s)
+                    nc.vector.tensor_copy(late[:, s, :], xw[s].bitcast(U32).indirect(listed(0, PAIR)))
+                    for e in range(HOT):
+                        gw[(e, s)] = late[:, s, e * C : (e + 1) * C]
         second_products(last, *quantized)
         for h in range(HALVES):
             staged = work.tile([P, PAIR], F32, name="staged")

@@ -22,7 +22,7 @@ PASSES = K // 512
 COLD = E - HOT
 HALVES = N // P
 SHIFT_ROWS = 112
-HOT_ROW = 4
+HOT_ROW = 0
 GROUPS = [[2, 3], [4, 5], [6, 7], [8, 9], [0, 1]]
 
 
@@ -77,10 +77,10 @@ def tile_moe_hot_mlp_silu_kernel(
         ident = keep.tile([P, P], F32, name="ident")
         make_identity(nc, ident[:])
         s1.append(zeroed_plane("s1_b", [P, 4 * PASSES, H], nc.gpsimd))
-        w2c = keep.tile([P, COLD, 2 * N], U8, name="w2c", align_bytes=64)
+        w2c = [keep.tile([P, 4, 2 * N], U8, name="w2c%d" % b, align_bytes=64) for b in range(2)]
         w2h = keep.tile([P, HOT, 4 * N], U8, name="w2h", align_bytes=64)
-        s1_hot = s1[1][:, 2 * PASSES : 4 * PASSES, :]
-        s2_hot = s2[:, COLD - HOT : COLD, :]
+        s1_hot = zeroed_plane("s1_hot", [P, HOT * PASSES, H], nc.gpsimd)
+        s2_hot = zeroed_plane("s2_hot", [P, HOT, N], nc.gpsimd)
 
         gates = keep.tile([P, T], F32, name="gates")
         w1 = {}
@@ -99,7 +99,7 @@ def tile_moe_hot_mlp_silu_kernel(
 
         def load_w2c(a, b):
             src = w2c_words[a:b].rearrange("e s p b -> p (e s) b")
-            nc.sync.dma_start(w2c[:, a:b, :].bitcast(I32), src.bitcast(I32))
+            nc.sync.dma_start(w2c[a // 4][:].bitcast(I32), src.bitcast(I32))
 
         gw = {}
         gs = {}
@@ -212,7 +212,7 @@ def tile_moe_hot_mlp_silu_kernel(
                 for j, e in enumerate(GROUPS[g]):
                     cols = slice(j * C, (j + 1) * C)
                     if e >= HOT:
-                        lhsT = w2c[:, e - HOT, h * 2 * P : (h + 1) * 2 * P].bitcast(FP4X4)
+                        lhsT = w2c[(e - HOT) // 4][:, (e - HOT) % 4, h * 2 * P : (h + 1) * 2 * P].bitcast(FP4X4)
                         lhsT_scale = s2[:, e - HOT, h * P : (h + 1) * P]
                     else:
                         lhsT = w2h[:, e, h * 4 * P : (h + 1) * 4 * P].bitcast(FP8X4)

@@ -22,7 +22,6 @@ PASSES = K // 512
 COLD = E - HOT
 HALVES = N // P
 SHIFT_ROWS = 112
-HOT_ROW = 0
 GROUPS = [[2, 3], [4, 5], [6, 7], [8, 9], [0, 1]]
 
 
@@ -37,16 +36,16 @@ def tile_moe_hot_mlp_silu_kernel(
         psum = ctx.enter_context(tc.psum_pool(name="psum", bufs=1))
         banks = [psum.tile([P, H], F32, name="bank%d" % b) for b in range(8)]
 
-        def zeroed_plane(name, shape, engine=nc.vector):
+        def zeroed_plane(name, shape):
             plane = keep.tile(shape, U8, name=name, align_bytes=64)
             flat = plane[:] if len(shape) == 2 else plane[:].rearrange("p a b -> p (a b)")
-            engine.memset(flat.bitcast(I32), 0)
+            nc.vector.memset(flat.bitcast(I32), 0)
             return plane
 
-        def load_plane(queue, plane, scales, row):
+        def load_plane(plane, scales):
             rows = scales.rearrange("e s (q r) w -> r q (e s) w", r=4)
             for r in range(4):
-                queue.dma_start(plane[row + r : P : 32, :, :].bitcast(I32), rows[r].bitcast(I32))
+                nc.sync.dma_start(plane[r:P:32, :, :].bitcast(I32), rows[r].bitcast(I32))
 
         def listed(a, b):
             return offsets[:, a // 16 : b // 16]
@@ -71,16 +70,13 @@ def tile_moe_hot_mlp_silu_kernel(
         nc.scalar.activation(warm[64:P, :], gate_rows[64:P, 0:1], SILU)
         nc.sync.dma_start(xw_rest[:], x_words[1:PASSES].rearrange("s p t d -> p s (t d)").bitcast(I32))
 
-        s1 = [zeroed_plane("s1_a", [P, 4 * PASSES, H])]
+        s1_wide = zeroed_plane("s1_wide", [P, 4 * PASSES, H])
+        shifts = [zeroed_plane("shift0", [P, PASSES - 1, 4 * C])]
         s2 = zeroed_plane("s2", [P, COLD, N])
-        shifts = [zeroed_plane("shift%d" % b, [P, PASSES - 1, 4 * C]) for b in range(2)]
         ident = keep.tile([P, P], F32, name="ident")
         make_identity(nc, ident[:])
-        s1.append(zeroed_plane("s1_b", [P, 4 * PASSES, H], nc.gpsimd))
         w2c = [keep.tile([P, 4, 2 * N], U8, name="w2c%d" % b, align_bytes=64) for b in range(2)]
         w2h = keep.tile([P, HOT, 4 * N], U8, name="w2h", align_bytes=64)
-        s1_hot = zeroed_plane("s1_hot", [P, HOT * PASSES, H], nc.gpsimd)
-        s2_hot = zeroed_plane("s2_hot", [P, HOT, N], nc.gpsimd)
 
         gates = keep.tile([P, T], F32, name="gates")
         w1 = {}
@@ -130,24 +126,29 @@ def tile_moe_hot_mlp_silu_kernel(
         PAIR = 2 * C
         gather_words(256, 768, 0)
         shift_planes(nc.scalar, shifts[0], gather_scales(256, 768, shifts[0]))
+        shifts.append(zeroed_plane("shift1", [P, PASSES - 1, 4 * C]))
         scales_b = gather_scales(768, 1280, shifts[1])
+        s1_late = zeroed_plane("s1_late", [P, 4 * PASSES, H])
+        s1_hot = zeroed_plane("s1_hot", [P, HOT * PASSES, H])
+        s2_hot = zeroed_plane("s2_hot", [P, HOT, N])
+        s1 = [t[:, a : a + 2 * PASSES, :] for t in (s1_wide, s1_late) for a in (0, 2 * PASSES)] + [s1_hot[:]]
 
-        load_plane(nc.sync, s1[0], w1c_scales[0:4], 0)
+        load_plane(s1_wide, w1c_scales[0:4])
         load_w1(2, 1)
         load_w1(3, 1)
         load_w1(4, 2)
         load_w2c(0, 4)
-        load_plane(nc.sync, s2, w2c_scales, 0)
-        shift_planes(nc.sync, shifts[1], scales_b)
-        load_plane(nc.sync, s1[1], w1c_scales[4:8], 0)
+        load_plane(s2, w2c_scales)
         load_w1(6, 2)
+        shift_planes(nc.sync, shifts[1], scales_b)
+        load_plane(s1_late, w1c_scales[4:8])
         load_w2c(4, 8)
-        load_plane(nc.sync, s1_hot, w1h_scales, HOT_ROW)
-        load_plane(nc.sync, s2_hot, w2h_scales, HOT_ROW)
         load_w1(8, 2)
+        load_plane(s1_hot, w1h_scales)
         load_w1(0, 1)
-        load_w1(1, 1)
+        load_plane(s2_hot, w2h_scales)
         nc.sync.dma_start(w2h[:].bitcast(I32), w2h_words.rearrange("e s p n d -> p (e s) (n d)").bitcast(I32))
+        load_w1(1, 1)
 
         gate_turned = banks[7]
         nc.tensor.transpose(gate_turned[:, 0:P], gate_rows[:], ident[:])
@@ -177,12 +178,10 @@ def tile_moe_hot_mlp_silu_kernel(
                 acc = banks[(g + j) % 3]
                 for s in range(PASSES):
                     if e >= HOT:
-                        f = e - HOT
                         rhs = w1[(e, s)].bitcast(FP4X4)
-                        rhs_scale = s1[f // 4][:, (f % 4) * PASSES + s, :]
                     else:
                         rhs = w1[(e, s)].bitcast(FP8X4)
-                        rhs_scale = s1_hot[HOT_ROW:P, e * PASSES + s, :]
+                    rhs_scale = s1[g][:, j * PASSES + s, :]
                     nc.tensor.matmul_mx(
                         out=acc[:], lhsT=gw[(e, s)].bitcast(FP8X4), lhsT_scale=gs[(e, s)],
                         rhs=rhs, rhs_scale=rhs_scale, start=(s == 0), stop=(s == PASSES - 1),
@@ -216,7 +215,7 @@ def tile_moe_hot_mlp_silu_kernel(
                         lhsT_scale = s2[:, e - HOT, h * P : (h + 1) * P]
                     else:
                         lhsT = w2h[:, e, h * 4 * P : (h + 1) * 4 * P].bitcast(FP8X4)
-                        lhsT_scale = s2_hot[HOT_ROW:P, e, h * P : (h + 1) * P]
+                        lhsT_scale = s2_hot[:, e, h * P : (h + 1) * P]
                     nc.tensor.matmul_mx(
                         out=banks[(g + 1) % 3][:, h * PAIR + j * C : h * PAIR + (j + 1) * C],
                         lhsT=lhsT, lhsT_scale=lhsT_scale,

@@ -21,8 +21,14 @@ P = 128
 PASSES = K // 512
 COLD = E - HOT
 HALVES = N // P
-SHIFT_ROWS = 112
-GROUPS = [[2, 3], [4, 5], [6, 7], [8, 9], [0, 1]]
+PAIR = 2 * C
+QUAD = 4
+PLANE_ROWS = 3 * 32 + 4
+BANK_BLOCKS = H // P
+GROUPS = [[2, 3], [4, 5], [6, 7], [8, 9], [1], [0]]
+PAIRS = COLD // 2
+CARRY = 2 * (T // 8) - PAIR
+EARLY, LATER, HOT_SLOTS = (PAIR, 3 * PAIR), (3 * PAIR, T), (0, PAIR)
 
 
 def tile_moe_hot_mlp_silu_kernel(
@@ -32,20 +38,19 @@ def tile_moe_hot_mlp_silu_kernel(
     nc = tc.nc
     with ExitStack() as ctx:
         keep = ctx.enter_context(tc.tile_pool(name="keep", bufs=1))
-        work = ctx.enter_context(tc.tile_pool(name="work", bufs=6))
         psum = ctx.enter_context(tc.psum_pool(name="psum", bufs=1))
         banks = [psum.tile([P, H], F32, name="bank%d" % b) for b in range(8)]
 
-        def zeroed_plane(name, shape):
-            plane = keep.tile(shape, U8, name=name, align_bytes=64)
-            flat = plane[:] if len(shape) == 2 else plane[:].rearrange("p a b -> p (a b)")
+        def zeroed_planes(name, shape):
+            planes = keep.tile(shape, U8, name=name, align_bytes=64)
+            flat = planes[:] if len(shape) == 2 else planes[:].rearrange("p a b -> p (a b)")
             nc.vector.memset(flat.bitcast(I32), 0)
-            return plane
+            return planes
 
-        def load_plane(plane, scales):
+        def load_planes(planes, scales):
             rows = scales.rearrange("e s (q r) w -> r q (e s) w", r=4)
             for r in range(4):
-                nc.sync.dma_start(plane[r:P:32, :, :].bitcast(I32), rows[r].bitcast(I32))
+                nc.sync.dma_start(planes[r:P:32, :, :].bitcast(I32), rows[r].bitcast(I32))
 
         def listed(a, b):
             return offsets[:, a // 16 : b // 16]
@@ -54,7 +59,7 @@ def tile_moe_hot_mlp_silu_kernel(
         xw_rest = keep.tile([P, PASSES - 1, T], I32, name="xw_rest", align_bytes=64)
         xw = [xw_first[:]] + [xw_rest[:, s, :] for s in range(PASSES - 1)]
         offsets = keep.tile([P, T // 16], U16, name="offsets")
-        xs = zeroed_plane("xs", [P, T])
+        xs = zeroed_planes("xs", [P, T])
         gate_rows = keep.tile([P, C], F32, name="gate_rows", align_bytes=64)
         nc.vector.memset(gate_rows[:], 0.0)
         nc.sync.dma_start(xw_first[:], x_words[0].rearrange("p t d -> p (t d)").bitcast(I32))
@@ -70,14 +75,13 @@ def tile_moe_hot_mlp_silu_kernel(
         nc.scalar.activation(warm[64:P, :], gate_rows[64:P, 0:1], SILU)
         nc.sync.dma_start(xw_rest[:], x_words[1:PASSES].rearrange("s p t d -> p s (t d)").bitcast(I32))
 
-        s1_wide = zeroed_plane("s1_wide", [P, 4 * PASSES, H])
-        shifts = [zeroed_plane("shift0", [P, PASSES - 1, 4 * C])]
-        s2 = zeroed_plane("s2", [P, COLD, N])
+        s1_early = zeroed_planes("s1_early", [P, QUAD * PASSES, H])
+        moved_early = zeroed_planes("moved_early", [P, PASSES - 1, QUAD * C])
+        s2_cold = zeroed_planes("s2_cold", [P, COLD, N])
         ident = keep.tile([P, P], F32, name="ident")
         make_identity(nc, ident[:])
-        w2c = [keep.tile([P, 4, 2 * N], U8, name="w2c%d" % b, align_bytes=64) for b in range(2)]
+        w2c = [keep.tile([P, QUAD, 2 * N], U8, name="w2c%d" % b, align_bytes=64) for b in range(COLD // QUAD)]
         w2h = keep.tile([P, HOT, 4 * N], U8, name="w2h", align_bytes=64)
-
         gates = keep.tile([P, T], F32, name="gates")
         w1 = {}
 
@@ -93,159 +97,186 @@ def tile_moe_hot_mlp_silu_kernel(
                 for s in range(PASSES):
                     w1[(first + j, s)] = tile[:, j * PASSES + s, :]
 
-        def load_w2c(a, b):
-            src = w2c_words[a:b].rearrange("e s p b -> p (e s) b")
-            nc.sync.dma_start(w2c[a // 4][:].bitcast(I32), src.bitcast(I32))
+        def load_w2c(b):
+            src = w2c_words[b * QUAD : (b + 1) * QUAD].rearrange("e s p b -> p (e s) b")
+            nc.sync.dma_start(w2c[b][:].bitcast(I32), src.bitcast(I32))
 
-        gw = {}
-        gs = {}
+        words = {}
+        planes_of = {}
 
-        def gather_words(a, b, s, name=None):
-            tile = keep.tile([P, b - a], U32, name=name or "gw%d_%d" % (s, a), align_bytes=64)[:]
-            nc.vector.tensor_copy(tile, xw[s].bitcast(U32).indirect(listed(a, b)))
+        def gather_words(into, slots, s):
+            a, b = slots
+            nc.vector.tensor_copy(into, xw[s].bitcast(U32).indirect(listed(a, b)))
             for e in range(a // C, b // C):
-                gw[(e, s)] = tile[:, e * C - a : (e + 1) * C - a]
+                words[(e, s)] = into[:, e * C - a : (e + 1) * C - a]
 
-        def gather_scales(a, b, shifted, name=None):
-            tile = keep.tile([P, b - a], U8, name=name or "gs%d" % a, align_bytes=64)
-            nc.vector.tensor_copy(tile[:], xs[:].indirect(listed(a, b)))
+        def words_tile(slots, s, tag=None):
+            name = "words%d_%d" % (s, slots[0])
+            return keep.tile([P, slots[1] - slots[0]], U32, name=name, tag=tag or name, align_bytes=64)[:]
+
+        def gather_scales(slots, moved, tag=None):
+            a, b = slots
+            name = "bytes%d" % a
+            gathered = keep.tile([P, b - a], U8, name=name, tag=tag or name, align_bytes=64)
+            nc.vector.tensor_copy(gathered[:], xs[:].indirect(listed(a, b)))
             for e in range(a // C, b // C):
                 cols = slice(e * C - a, (e + 1) * C - a)
-                gs[(e, 0)] = tile[:, cols]
+                planes_of[(e, 0)] = gathered[:, cols]
                 for s in range(1, PASSES):
-                    gs[(e, s)] = tile[4 * s : P, cols] if shifted is None else shifted[:, s - 1, cols]
-            return tile
+                    planes_of[(e, s)] = gathered[4 * s : P, cols] if moved is None else moved[:, s - 1, cols]
+            return gathered
 
-        def shift_planes(queue, shifted, tile):
+        def move_planes(queue, moved, gathered):
             for s in range(1, PASSES):
                 queue.dma_start(
-                    shifted[0:SHIFT_ROWS, s - 1, :].bitcast(I32),
-                    tile[4 * s : 4 * s + SHIFT_ROWS, :].bitcast(I32),
+                    moved[0:PLANE_ROWS, s - 1, :].bitcast(I32),
+                    gathered[4 * s : 4 * s + PLANE_ROWS, :].bitcast(I32),
                 )
 
-        PAIR = 2 * C
-        gather_words(256, 768, 0)
-        shift_planes(nc.scalar, shifts[0], gather_scales(256, 768, shifts[0]))
-        shifts.append(zeroed_plane("shift1", [P, PASSES - 1, 4 * C]))
-        scales_b = gather_scales(768, 1280, shifts[1])
-        s1_late = zeroed_plane("s1_late", [P, 4 * PASSES, H])
-        s1_hot = zeroed_plane("s1_hot", [P, HOT * PASSES, H])
-        s2_hot = zeroed_plane("s2_hot", [P, HOT, N])
-        s1 = [t[:, a : a + 2 * PASSES, :] for t in (s1_wide, s1_late) for a in (0, 2 * PASSES)] + [s1_hot[:]]
+        gather_words(words_tile(EARLY, 0), EARLY, 0)
+        move_planes(nc.scalar, moved_early, gather_scales(EARLY, moved_early))
+        moved_later = zeroed_planes("moved_later", [P, PASSES - 1, QUAD * C])
+        bytes_later = gather_scales(LATER, moved_later)
+        s1_later = zeroed_planes("s1_later", [P, QUAD * PASSES, H])
+        s1_hot = s1_early[:, 0 : HOT * PASSES, :]
+        s2_hot = s1_early[:, HOT * PASSES, :].rearrange("p (e n) -> p e n", e=HOT)
+        s1 = [t[:, a : a + 2 * PASSES, :] for t in (s1_early, s1_later) for a in (0, 2 * PASSES)]
+        s1 += [s1_hot[:, PASSES : 2 * PASSES, :], s1_hot[:, 0:PASSES, :]]
 
-        load_plane(s1_wide, w1c_scales[0:4])
+        load_planes(s1_early, w1c_scales[0:QUAD])
         load_w1(2, 1)
         load_w1(3, 1)
         load_w1(4, 2)
-        load_w2c(0, 4)
-        load_plane(s2, w2c_scales)
+        load_w2c(0)
+        load_planes(s2_cold, w2c_scales)
         load_w1(6, 2)
-        shift_planes(nc.sync, shifts[1], scales_b)
-        load_plane(s1_late, w1c_scales[4:8])
-        load_w2c(4, 8)
+        move_planes(nc.sync, moved_later, bytes_later)
+        load_planes(s1_later, w1c_scales[QUAD:COLD])
+        load_w2c(1)
         load_w1(8, 2)
-        load_plane(s1_hot, w1h_scales)
-        load_w1(0, 1)
-        load_plane(s2_hot, w2h_scales)
-        nc.sync.dma_start(w2h[:].bitcast(I32), w2h_words.rearrange("e s p n d -> p (e s) (n d)").bitcast(I32))
         load_w1(1, 1)
+
+        def load_hot_rest():
+            load_planes(s1_hot, w1h_scales)
+            load_planes(s2_hot, w2h_scales)
+            nc.sync.dma_start(w2h[:].bitcast(I32), w2h_words.rearrange("e s p n d -> p (e s) (n d)").bitcast(I32))
+            load_w1(0, 1)
 
         gate_turned = banks[7]
         nc.tensor.transpose(gate_turned[:, 0:P], gate_rows[:], ident[:])
         gate_cols = keep.tile([P, E], F32, name="gate_cols", align_bytes=64)
         nc.scalar.copy(gate_cols[:], gate_turned[:, 0:E])
-        for first in range(0, E, 4):
-            count = min(4, E - first)
-            spread = banks[4 + first // 4]
+        for first in range(0, E, BANK_BLOCKS):
+            count = min(BANK_BLOCKS, E - first)
+            spread = banks[4 + first // BANK_BLOCKS]
             for j in range(count):
                 column = gate_cols[:, first + j : first + j + 1]
                 nc.tensor.transpose(spread[:, j * C : (j + 1) * C], column.to_broadcast([P, P]), ident[:])
             nc.scalar.copy(gates[:, first * C : (first + count) * C], spread[:, 0 : count * C])
 
-        for a, b in ((256, 512), (512, 768)):
-            for s in range(1, PASSES):
-                gather_words(a, b, s)
-        gather_words(768, 1280, 0, "gate_rows")
         for s in range(1, PASSES):
-            gather_words(768, 1280, s)
-        gather_scales(0, 256, None, "gate_cols")
+            gather_words(words_tile(EARLY, s), EARLY, s)
+        gather_words(words_tile(LATER, 0, "gate_rows"), LATER, 0)
+        for s in range(1, PASSES):
+            gather_words(words_tile(LATER, s), LATER, s)
+        gather_scales(HOT_SLOTS, None, "gate_cols")
 
         outs = [keep.tile([P, T], F32, name="out%d" % h) for h in range(HALVES)]
+        ends = [keep.tile([P, PAIR + CARRY], F32, name="end%d" % h, align_bytes=64) for h in range(HALVES)]
 
-        def first_products(g):
-            hids = []
+        def first_products(g, accs, hid_words):
             for j, e in enumerate(GROUPS[g]):
-                acc = banks[(g + j) % 3]
                 for s in range(PASSES):
-                    if e >= HOT:
-                        rhs = w1[(e, s)].bitcast(FP4X4)
-                    else:
-                        rhs = w1[(e, s)].bitcast(FP8X4)
-                    rhs_scale = s1[g][:, j * PASSES + s, :]
                     nc.tensor.matmul_mx(
-                        out=acc[:], lhsT=gw[(e, s)].bitcast(FP8X4), lhsT_scale=gs[(e, s)],
-                        rhs=rhs, rhs_scale=rhs_scale, start=(s == 0), stop=(s == PASSES - 1),
+                        out=accs[j][:], lhsT=words[(e, s)].bitcast(FP8X4), lhsT_scale=planes_of[(e, s)],
+                        rhs=w1[(e, s)].bitcast(FP4X4 if e >= HOT else FP8X4), rhs_scale=s1[g][:, j * PASSES + s, :],
+                        start=(s == 0), stop=(s == PASSES - 1),
                     )
-                hid = keep.tile([P, 2, P, 2], BF16, name="hid%d" % e, align_bytes=64)
-                nc.scalar.activation(hid[:], acc[:].rearrange("c (p u v) -> c u p v", u=2, v=2), SILU)
-                hids.append(hid[:].rearrange("c u p v -> c (u p v)").bitcast(F32))
-            return hids
+                hid = hid_words[j].bitcast(BF16).rearrange("c (u p v) -> c u p v", u=2, v=2)
+                nc.scalar.activation(hid, accs[j][:].rearrange("c (p u v) -> c u p v", u=2, v=2), SILU)
 
-        def turn_and_quantize(g, hids):
-            turned = banks[(g + 2) % 3][:].rearrange("p (j u c) -> p j u c", u=2, c=C)
-            for j, pairs in enumerate(hids):
+        def turn_and_quantize(g, bank, hid_words):
+            width = len(GROUPS[g]) * C
+            turned = bank[:, 0 : 2 * width].rearrange("p (j u c) -> p j u c", u=2, c=C)
+            for j, pairs in enumerate(hid_words):
                 for u in range(2):
                     nc.tensor.transpose(turned[:, j, u, :], pairs[:, u * P : (u + 1) * P], ident[:])
-            grouped = keep.tile([P, PAIR * 4], BF16, name="grouped%d" % g, align_bytes=64)
+            grouped = keep.tile([P, width * 4], BF16, name="grouped%d" % g, align_bytes=64)
             nc.scalar.copy(
                 grouped[:].bitcast(F32).rearrange("p (j c u) -> p j c u", u=2, c=C),
                 turned.rearrange("p j u c -> p j c u"),
             )
-            codes = work.tile([P, PAIR], U32, name="codes", align_bytes=64)
-            scales = work.tile([P, PAIR], U8, name="scales", align_bytes=64)
+            codes = keep.tile([P, width], U32, name="codes%d" % g, align_bytes=64)
+            scales = keep.tile([P, width], U8, name="scales%d" % g, align_bytes=64)
             nc.vector.quantize_mx(out=codes[:].bitcast(FP8X4), scales=scales[:], in_=grouped[:])
             return codes, scales
 
-        def second_products(g, codes, scales):
+        def second_products(g, results, codes, scales):
             for h in range(HALVES):
                 for j, e in enumerate(GROUPS[g]):
                     cols = slice(j * C, (j + 1) * C)
                     if e >= HOT:
-                        lhsT = w2c[(e - HOT) // 4][:, (e - HOT) % 4, h * 2 * P : (h + 1) * 2 * P].bitcast(FP4X4)
-                        lhsT_scale = s2[:, e - HOT, h * P : (h + 1) * P]
+                        b, f = divmod(e - HOT, QUAD)
+                        lhsT = w2c[b][:, f, h * 2 * P : (h + 1) * 2 * P].bitcast(FP4X4)
+                        lhsT_scale = s2_cold[:, e - HOT, h * P : (h + 1) * P]
                     else:
                         lhsT = w2h[:, e, h * 4 * P : (h + 1) * 4 * P].bitcast(FP8X4)
                         lhsT_scale = s2_hot[:, e, h * P : (h + 1) * P]
                     nc.tensor.matmul_mx(
-                        out=banks[(g + 1) % 3][:, h * PAIR + j * C : h * PAIR + (j + 1) * C],
-                        lhsT=lhsT, lhsT_scale=lhsT_scale,
+                        out=results[h][:, cols], lhsT=lhsT, lhsT_scale=lhsT_scale,
                         rhs=codes[:, cols].bitcast(FP8X4), rhs_scale=scales[:, cols], start=True, stop=True,
                     )
 
-        def scatter(g, h, staged):
-            a = GROUPS[g][0] * C
-            nc.scalar.copy(staged, banks[(g + 1) % 3][:, h * PAIR : (h + 1) * PAIR])
-            nc.vector.tensor_tensor(outs[h][:].indirect(listed(a, a + PAIR)), staged, gates[:, a : a + PAIR], MULT)
+        def scatter(h, a, b, staged):
+            nc.vector.tensor_tensor(outs[h][:].indirect(listed(a, b)), staged, gates[:, a:b], MULT)
 
-        last = len(GROUPS) - 1
+        def send_pair(g, h, result, staged):
+            a = GROUPS[g][0] * C
+            held = CARRY if g == 0 else 0
+            nc.scalar.copy(staged[:, held:PAIR], result[:, held:PAIR])
+            scatter(h, a + held, a + PAIR, staged[:, held:PAIR])
+            if held:
+                nc.scalar.copy(ends[h][:, PAIR : PAIR + CARRY], result[:, 0:CARRY])
+
+        def hid_tile(e):
+            return keep.tile([P, H // 2], F32, name="hid%d" % e, align_bytes=64)[:]
+
+        def both_halves(bank, width):
+            return [bank[:, h * width : (h + 1) * width] for h in range(HALVES)]
+
         quantized = None
-        for g in range(len(GROUPS)):
-            hids = first_products(g)
+        for g in range(PAIRS + 1):
+            accs = [banks[(g + j) % 3] for j in range(len(GROUPS[g]))]
+            hid_words = [hid_tile(e) for e in GROUPS[g]]
+            first_products(g, accs, hid_words)
+            if g == QUAD // 2 - 1:
+                load_hot_rest()
             if g > 0:
-                second_products(g - 1, *quantized)
-                staged = work.tile([P, PAIR], F32, name="staged")
-                scatter(g - 1, 0, staged[:])
-            quantized = turn_and_quantize(g, hids)
+                results = both_halves(accs[0], PAIR)
+                second_products(g - 1, results, *quantized)
+                staged = keep.tile([P, PAIR], F32, name="staged%d" % g)
+                send_pair(g - 1, 0, results[0], staged[:])
+            quantized = turn_and_quantize(g, banks[(g + 2) % 3], hid_words)
             if g > 0:
-                scatter(g - 1, 1, hids[1])
+                send_pair(g - 1, 1, results[1], hid_words[-1])
             else:
-                late = keep.tile([P, PASSES, PAIR], U32, name="grouped0", align_bytes=64)
+                words_hot = keep.tile([P, PASSES, PAIR], U32, name="words_hot", tag="grouped0", align_bytes=64)
                 for s in range(PASSES):
-                    nc.vector.tensor_copy(late[:, s, :], xw[s].bitcast(U32).indirect(listed(0, PAIR)))
-                    for e in range(HOT):
-                        gw[(e, s)] = late[:, s, e * C : (e + 1) * C]
-        second_products(last, *quantized)
+                    gather_words(words_hot[:, s, :], HOT_SLOTS, s)
+
+        split = (PAIR + CARRY) // 2
+        hid_words = [ends[1][:, 0 : H // 2]]
+        first_products(PAIRS + 1, [banks[3]], hid_words)
+        results = both_halves(banks[3], C)
+        second_products(PAIRS, results, *quantized)
+        nc.scalar.copy(ends[0][:, C:PAIR], results[0])
+        scatter(0, split, PAIR + CARRY, ends[0][:, split : PAIR + CARRY])
+        quantized = turn_and_quantize(PAIRS + 1, banks[2], hid_words)
+        nc.scalar.copy(ends[1][:, C:PAIR], results[1])
+        scatter(1, split, PAIR + CARRY, ends[1][:, split : PAIR + CARRY])
+        results = both_halves(banks[0], C)
+        second_products(PAIRS + 1, results, *quantized)
         for h in range(HALVES):
-            staged = work.tile([P, PAIR], F32, name="staged")
-            scatter(last, h, staged[:])
+            nc.scalar.copy(ends[h][:, 0:C], results[h])
+            scatter(h, 0, split, ends[h][:, 0:split])
             nc.sync.dma_start(out[h * P : (h + 1) * P, :], outs[h][:])

@@ -25,9 +25,7 @@ PAIR = 2 * C
 QUAD = 4
 PLANE_ROWS = 3 * 32 + 4
 BANK_BLOCKS = H // P
-GROUPS = [[2, 3], [4, 5], [6, 7], [8, 9], [1], [0]]
-PAIRS = COLD // 2
-CARRY = 2 * (T // 8) - PAIR
+ORDER = list(range(HOT, E)) + [1, 0]
 EARLY, LATER, HOT_SLOTS = (PAIR, 3 * PAIR), (3 * PAIR, T), (0, PAIR)
 
 
@@ -40,6 +38,7 @@ def tile_moe_hot_mlp_silu_kernel(
         keep = ctx.enter_context(tc.tile_pool(name="keep", bufs=1))
         psum = ctx.enter_context(tc.psum_pool(name="psum", bufs=1))
         banks = [psum.tile([P, H], F32, name="bank%d" % b) for b in range(8)]
+        first_banks, second_banks, turn_banks, spare_banks = banks[0:2], banks[2:4], banks[4:6], banks[6:8]
 
         def zeroed_planes(name, shape):
             planes = keep.tile(shape, U8, name=name, align_bytes=64)
@@ -55,14 +54,16 @@ def tile_moe_hot_mlp_silu_kernel(
         def listed(a, b):
             return offsets[:, a // 16 : b // 16]
 
-        xw_first = keep.tile([P, T], I32, name="xw_first", align_bytes=64)
-        xw_rest = keep.tile([P, PASSES - 1, T], I32, name="xw_rest", align_bytes=64)
-        xw = [xw_first[:]] + [xw_rest[:, s, :] for s in range(PASSES - 1)]
+        xw = [keep.tile([P, T], I32, name="xw%d" % s, align_bytes=64) for s in range(PASSES)]
         offsets = keep.tile([P, T // 16], U16, name="offsets")
         xs = zeroed_planes("xs", [P, T])
         gate_rows = keep.tile([P, C], F32, name="gate_rows", align_bytes=64)
         nc.vector.memset(gate_rows[:], 0.0)
-        nc.sync.dma_start(xw_first[:], x_words[0].rearrange("p t d -> p (t d)").bitcast(I32))
+
+        def load_words(s):
+            nc.sync.dma_start(xw[s][:], x_words[s].rearrange("p t d -> p (t d)").bitcast(I32))
+
+        load_words(0)
         nc.sync.dma_start(offsets[:], offs)
         for q in range(4):
             queue = nc.sync if q % 2 else nc.scalar
@@ -70,151 +71,164 @@ def tile_moe_hot_mlp_silu_kernel(
                 xs[32 * q : 32 * q + 4 * PASSES, :].bitcast(I32),
                 x_scales[:, 4 * q : 4 * q + 4, :].bitcast(I32),
             )
-        nc.scalar.dma_start(gate_rows[0:E, :], gate[0:1, :].rearrange("o (e c) -> (o e) c", c=C))
         warm = keep.tile([P, 1], F32, name="warm")
         nc.scalar.activation(warm[64:P, :], gate_rows[64:P, 0:1], SILU)
-        nc.sync.dma_start(xw_rest[:], x_words[1:PASSES].rearrange("s p t d -> p s (t d)").bitcast(I32))
+        for s in range(1, PASSES):
+            load_words(s)
+        nc.sync.dma_start(gate_rows[0:E, :], gate[0:1, :].rearrange("o (e c) -> (o e) c", c=C))
 
         s1_early = zeroed_planes("s1_early", [P, QUAD * PASSES, H])
-        moved_early = zeroed_planes("moved_early", [P, PASSES - 1, QUAD * C])
+        moved = zeroed_planes("moved", [P, PASSES - 1, COLD * C])
         s2_cold = zeroed_planes("s2_cold", [P, COLD, N])
         ident = keep.tile([P, P], F32, name="ident")
         make_identity(nc, ident[:])
         w2c = [keep.tile([P, QUAD, 2 * N], U8, name="w2c%d" % b, align_bytes=64) for b in range(COLD // QUAD)]
         w2h = keep.tile([P, HOT, 4 * N], U8, name="w2h", align_bytes=64)
         gates = keep.tile([P, T], F32, name="gates")
-        w1 = {}
 
-        def load_w1(first, count):
-            width = 2 * H if first >= HOT else 4 * H
-            tile = keep.tile([P, count * PASSES, width], U8, name="w1_%d" % first, align_bytes=64)
-            if first >= HOT:
-                src = w1c_words[first - HOT : first - HOT + count].rearrange("e s p b -> p (e s) b")
+        w1_first = keep.tile([P, 2 * PASSES, 2 * H], U8, name="w1_first", align_bytes=64)
+        w1 = {HOT + j: w1_first[:, j * PASSES : (j + 1) * PASSES, :] for j in range(2)}
+        for e in ORDER[2:]:
+            width = 2 * H if e >= HOT else 4 * H
+            w1[e] = keep.tile([P, PASSES, width], U8, name="w1_%d" % e, align_bytes=64)[:]
+
+        def load_w1(e):
+            if e >= HOT:
+                src = w1c_words[e - HOT].rearrange("s p b -> p s b")
             else:
-                src = w1h_words[first : first + count].rearrange("e s p i d -> p (e s) (i d)")
-            nc.sync.dma_start(tile[:].bitcast(I32), src.bitcast(I32))
-            for j in range(count):
-                for s in range(PASSES):
-                    w1[(first + j, s)] = tile[:, j * PASSES + s, :]
+                src = w1h_words[e].rearrange("s p i d -> p s (i d)")
+            nc.sync.dma_start(w1[e].bitcast(I32), src.bitcast(I32))
 
         def load_w2c(b):
             src = w2c_words[b * QUAD : (b + 1) * QUAD].rearrange("e s p b -> p (e s) b")
             nc.sync.dma_start(w2c[b][:].bitcast(I32), src.bitcast(I32))
+
+        def as_planes(words_tile, count, width):
+            flat = words_tile.rearrange("p a b -> p (a b)")
+            return flat[:, 0 : count * width].rearrange("p (a w) -> p a w", w=width)
+
+        s1_later = as_planes(w1_first[:], QUAD * PASSES, H)
+        s1_hot = as_planes(w1[4], HOT * PASSES, H)
+        s2_hot = as_planes(w1[5], HOT, N)
+
+        def s1(e, s):
+            if e < HOT:
+                return s1_hot[:, e * PASSES + s, :]
+            b, f = divmod(e - HOT, QUAD)
+            return (s1_later if b else s1_early)[:, f * PASSES + s, :]
 
         words = {}
         planes_of = {}
 
         def gather_words(into, slots, s):
             a, b = slots
-            nc.vector.tensor_copy(into, xw[s].bitcast(U32).indirect(listed(a, b)))
+            nc.vector.tensor_copy(into, xw[s][:].bitcast(U32).indirect(listed(a, b)))
             for e in range(a // C, b // C):
                 words[(e, s)] = into[:, e * C - a : (e + 1) * C - a]
 
-        def words_tile(slots, s, tag=None):
-            name = "words%d_%d" % (s, slots[0])
-            return keep.tile([P, slots[1] - slots[0]], U32, name=name, tag=tag or name, align_bytes=64)[:]
+        def words_tile(name, shape, tag=None):
+            return keep.tile([P] + shape, U32, name=name, tag=tag or name, align_bytes=64)
 
-        def gather_scales(slots, moved, tag=None):
-            a, b = slots
-            name = "bytes%d" % a
-            gathered = keep.tile([P, b - a], U8, name=name, tag=tag or name, align_bytes=64)
-            nc.vector.tensor_copy(gathered[:], xs[:].indirect(listed(a, b)))
-            for e in range(a // C, b // C):
-                cols = slice(e * C - a, (e + 1) * C - a)
-                planes_of[(e, 0)] = gathered[:, cols]
-                for s in range(1, PASSES):
-                    planes_of[(e, s)] = gathered[4 * s : P, cols] if moved is None else moved[:, s - 1, cols]
-            return gathered
-
-        def move_planes(queue, moved, gathered):
+        gather_words(words_tile("words_early0", [QUAD * C])[:], EARLY, 0)
+        bytes_cold = keep.tile([P, COLD * C], U8, name="bytes_cold", align_bytes=64)
+        for a, b in (EARLY, LATER):
+            nc.vector.tensor_copy(bytes_cold[:, a - PAIR : b - PAIR], xs[:].indirect(listed(a, b)))
+        for s in range(1, PASSES):
+            nc.scalar.dma_start(
+                moved[0:PLANE_ROWS, s - 1, :].bitcast(I32),
+                bytes_cold[4 * s : 4 * s + PLANE_ROWS, :].bitcast(I32),
+            )
+        for e in range(HOT, E):
+            cols = slice((e - HOT) * C, (e - HOT + 1) * C)
+            planes_of[(e, 0)] = bytes_cold[:, cols]
             for s in range(1, PASSES):
-                queue.dma_start(
-                    moved[0:PLANE_ROWS, s - 1, :].bitcast(I32),
-                    gathered[4 * s : 4 * s + PLANE_ROWS, :].bitcast(I32),
-                )
-
-        gather_words(words_tile(EARLY, 0), EARLY, 0)
-        move_planes(nc.scalar, moved_early, gather_scales(EARLY, moved_early))
-        moved_later = zeroed_planes("moved_later", [P, PASSES - 1, QUAD * C])
-        bytes_later = gather_scales(LATER, moved_later)
-        s1_later = zeroed_planes("s1_later", [P, QUAD * PASSES, H])
-        s1_hot = s1_early[:, 0 : HOT * PASSES, :]
-        s2_hot = s1_early[:, HOT * PASSES, :].rearrange("p (e n) -> p e n", e=HOT)
-        s1 = [t[:, a : a + 2 * PASSES, :] for t in (s1_early, s1_later) for a in (0, 2 * PASSES)]
-        s1 += [s1_hot[:, PASSES : 2 * PASSES, :], s1_hot[:, 0:PASSES, :]]
+                planes_of[(e, s)] = moved[:, s - 1, cols]
+        for s in range(1, PASSES):
+            gather_words(words_tile("words_early%d" % s, [QUAD * C])[:], EARLY, s)
+        bytes_hot = keep.tile([P, PAIR], U8, name="bytes_hot", align_bytes=64)
+        nc.vector.tensor_copy(bytes_hot[:], xs[:].indirect(listed(*HOT_SLOTS)))
+        for e in range(HOT):
+            for s in range(PASSES):
+                planes_of[(e, s)] = bytes_hot[4 * s : P, e * C : (e + 1) * C]
 
         load_planes(s1_early, w1c_scales[0:QUAD])
-        load_w1(2, 1)
-        load_w1(3, 1)
-        load_w1(4, 2)
+        for e in ORDER[0:QUAD]:
+            load_w1(e)
         load_w2c(0)
         load_planes(s2_cold, w2c_scales)
-        load_w1(6, 2)
-        move_planes(nc.sync, moved_later, bytes_later)
-        load_planes(s1_later, w1c_scales[QUAD:COLD])
-        load_w2c(1)
-        load_w1(8, 2)
-        load_w1(1, 1)
 
-        def load_hot_rest():
+        def load_later():
+            load_planes(s1_later, w1c_scales[QUAD:COLD])
+            for e in ORDER[QUAD:COLD]:
+                load_w1(e)
+            load_w2c(1)
+
+        def load_hot():
             load_planes(s1_hot, w1h_scales)
-            load_planes(s2_hot, w2h_scales)
+            for e in ORDER[COLD:]:
+                load_w1(e)
             nc.sync.dma_start(w2h[:].bitcast(I32), w2h_words.rearrange("e s p n d -> p (e s) (n d)").bitcast(I32))
-            load_w1(0, 1)
+            load_planes(s2_hot, w2h_scales)
 
-        gate_turned = banks[7]
+        gate_turned = spare_banks[0]
         nc.tensor.transpose(gate_turned[:, 0:P], gate_rows[:], ident[:])
         gate_cols = keep.tile([P, E], F32, name="gate_cols", align_bytes=64)
         nc.scalar.copy(gate_cols[:], gate_turned[:, 0:E])
-        for first in range(0, E, BANK_BLOCKS):
+        for first, spread in zip(range(0, E, BANK_BLOCKS), (spare_banks[1], turn_banks[1], second_banks[1])):
             count = min(BANK_BLOCKS, E - first)
-            spread = banks[4 + first // BANK_BLOCKS]
             for j in range(count):
                 column = gate_cols[:, first + j : first + j + 1]
                 nc.tensor.transpose(spread[:, j * C : (j + 1) * C], column.to_broadcast([P, P]), ident[:])
             nc.scalar.copy(gates[:, first * C : (first + count) * C], spread[:, 0 : count * C])
 
-        for s in range(1, PASSES):
-            gather_words(words_tile(EARLY, s), EARLY, s)
-        gather_words(words_tile(LATER, 0, "gate_rows"), LATER, 0)
-        for s in range(1, PASSES):
-            gather_words(words_tile(LATER, s), LATER, s)
-        gather_scales(HOT_SLOTS, None, "gate_cols")
+        words_later = words_tile("words_later", [PASSES, QUAD * C], "gate_cols")
+        for s in range(PASSES):
+            gather_words(words_later[:, s, :], LATER, s)
 
         outs = [keep.tile([P, T], F32, name="out%d" % h) for h in range(HALVES)]
-        ends = [keep.tile([P, PAIR + CARRY], F32, name="end%d" % h, align_bytes=64) for h in range(HALVES)]
+        hids = {}
+        quantized = {}
+        results = {}
 
-        def first_products(g, accs, hid_words):
-            for j, e in enumerate(GROUPS[g]):
-                for s in range(PASSES):
-                    nc.tensor.matmul_mx(
-                        out=accs[j][:], lhsT=words[(e, s)].bitcast(FP8X4), lhsT_scale=planes_of[(e, s)],
-                        rhs=w1[(e, s)].bitcast(FP4X4 if e >= HOT else FP8X4), rhs_scale=s1[g][:, j * PASSES + s, :],
-                        start=(s == 0), stop=(s == PASSES - 1),
-                    )
-                hid = hid_words[j].bitcast(BF16).rearrange("c (u p v) -> c u p v", u=2, v=2)
-                nc.scalar.activation(hid, accs[j][:].rearrange("c (p u v) -> c u p v", u=2, v=2), SILU)
+        def first_bank(i):
+            return (second_banks if i % 2 else first_banks)[i // 2 % 2]
 
-        def turn_and_quantize(g, bank, hid_words):
-            width = len(GROUPS[g]) * C
-            turned = bank[:, 0 : 2 * width].rearrange("p (j u c) -> p j u c", u=2, c=C)
-            for j, pairs in enumerate(hid_words):
-                for u in range(2):
-                    nc.tensor.transpose(turned[:, j, u, :], pairs[:, u * P : (u + 1) * P], ident[:])
-            grouped = keep.tile([P, width * 4], BF16, name="grouped%d" % g, align_bytes=64)
+        def first_product(i):
+            e = ORDER[i]
+            acc = first_bank(i)
+            for s in range(PASSES):
+                nc.tensor.matmul_mx(
+                    out=acc[:], lhsT=words[(e, s)].bitcast(FP8X4), lhsT_scale=planes_of[(e, s)],
+                    rhs=w1[e][:, s, :].bitcast(FP4X4 if e >= HOT else FP8X4), rhs_scale=s1(e, s),
+                    start=(s == 0), stop=(s == PASSES - 1),
+                )
+            hids[i] = keep.tile([P, H // 2], F32, name="hid%d" % e, align_bytes=64)[:]
+            hid = hids[i].bitcast(BF16).rearrange("c (u p v) -> c u p v", u=2, v=2)
+            nc.scalar.activation(hid, acc[:].rearrange("c (p u v) -> c u p v", u=2, v=2), SILU)
+
+        def turn_and_quantize(i):
+            e = ORDER[i]
+            turned = turn_banks[i % 2][:, 0 : 2 * C].rearrange("p (u c) -> p u c", u=2)
+            for u in range(2):
+                nc.tensor.transpose(turned[:, u, :], hids[i][:, u * P : (u + 1) * P], ident[:])
+            grouped = keep.tile([P, C * 4], BF16, name="grouped%d" % i, align_bytes=64)
             nc.scalar.copy(
-                grouped[:].bitcast(F32).rearrange("p (j c u) -> p j c u", u=2, c=C),
-                turned.rearrange("p j u c -> p j c u"),
+                grouped[:].bitcast(F32).rearrange("p (c u) -> p c u", u=2), turned.rearrange("p u c -> p c u"),
             )
-            codes = keep.tile([P, width], U32, name="codes%d" % g, align_bytes=64)
-            scales = keep.tile([P, width], U8, name="scales%d" % g, align_bytes=64)
+            codes = keep.tile([P, C], U32, name="codes%d" % e, align_bytes=64)
+            scales = keep.tile([P, C], U8, name="scales%d" % e, align_bytes=64)
             nc.vector.quantize_mx(out=codes[:].bitcast(FP8X4), scales=scales[:], in_=grouped[:])
-            return codes, scales
+            quantized[e] = codes, scales
 
-        def second_products(g, results, codes, scales):
-            for h in range(HALVES):
-                for j, e in enumerate(GROUPS[g]):
-                    cols = slice(j * C, (j + 1) * C)
+        def pair_start(g):
+            return min(ORDER[2 * g : 2 * g + 2]) * C
+
+        def second_products(g, bank):
+            results[g] = [bank[:, h * PAIR : (h + 1) * PAIR] for h in range(HALVES)]
+            for e in ORDER[2 * g : 2 * g + 2]:
+                codes, scales = quantized[e]
+                cols = slice(e * C - pair_start(g), (e + 1) * C - pair_start(g))
+                for h in range(HALVES):
                     if e >= HOT:
                         b, f = divmod(e - HOT, QUAD)
                         lhsT = w2c[b][:, f, h * 2 * P : (h + 1) * 2 * P].bitcast(FP4X4)
@@ -223,60 +237,42 @@ def tile_moe_hot_mlp_silu_kernel(
                         lhsT = w2h[:, e, h * 4 * P : (h + 1) * 4 * P].bitcast(FP8X4)
                         lhsT_scale = s2_hot[:, e, h * P : (h + 1) * P]
                     nc.tensor.matmul_mx(
-                        out=results[h][:, cols], lhsT=lhsT, lhsT_scale=lhsT_scale,
-                        rhs=codes[:, cols].bitcast(FP8X4), rhs_scale=scales[:, cols], start=True, stop=True,
+                        out=results[g][h][:, cols], lhsT=lhsT, lhsT_scale=lhsT_scale,
+                        rhs=codes[:].bitcast(FP8X4), rhs_scale=scales[:], start=True, stop=True,
                     )
 
-        def scatter(h, a, b, staged):
-            nc.vector.tensor_tensor(outs[h][:].indirect(listed(a, b)), staged, gates[:, a:b], MULT)
+        def send(g, h, staged):
+            a = pair_start(g)
+            nc.scalar.copy(staged, results[g][h])
+            nc.vector.tensor_tensor(outs[h][:].indirect(listed(a, a + PAIR)), staged, gates[:, a : a + PAIR], MULT)
 
-        def send_pair(g, h, result, staged):
-            a = GROUPS[g][0] * C
-            held = CARRY if g == 0 else 0
-            nc.scalar.copy(staged[:, held:PAIR], result[:, held:PAIR])
-            scatter(h, a + held, a + PAIR, staged[:, held:PAIR])
-            if held:
-                nc.scalar.copy(ends[h][:, PAIR : PAIR + CARRY], result[:, 0:CARRY])
+        def staging(name):
+            return keep.tile([P, PAIR], F32, name=name, align_bytes=64)[:]
 
-        def hid_tile(e):
-            return keep.tile([P, H // 2], F32, name="hid%d" % e, align_bytes=64)[:]
+        for i in range(E + 1):
+            if i < E:
+                first_product(i)
+            if i == 1:
+                load_later()
+            if i == 3:
+                load_hot()
+            if i >= 1:
+                turn_and_quantize(i - 1)
+            if i == 1:
+                gather_words(words_tile("words_hot0", [PAIR], "grouped0")[:], HOT_SLOTS, 0)
+            if i == 2:
+                words_hot = words_tile("words_hot", [PASSES - 1, PAIR], "grouped1")
+                for s in range(1, PASSES):
+                    gather_words(words_hot[:, s - 1, :], HOT_SLOTS, s)
+            if i >= 3 and i % 2 == 1:
+                g = (i - 3) // 2
+                second_products(g, spare_banks[0] if i - 1 == QUAD else first_bank(i - 1))
+                send(g, 0, staging("staged%d" % g))
+            if i >= 4 and i % 2 == 0:
+                send((i - 4) // 2, 1, hids[i - 1])
 
-        def both_halves(bank, width):
-            return [bank[:, h * width : (h + 1) * width] for h in range(HALVES)]
-
-        quantized = None
-        for g in range(PAIRS + 1):
-            accs = [banks[(g + j) % 3] for j in range(len(GROUPS[g]))]
-            hid_words = [hid_tile(e) for e in GROUPS[g]]
-            first_products(g, accs, hid_words)
-            if g == QUAD // 2 - 1:
-                load_hot_rest()
-            if g > 0:
-                results = both_halves(accs[0], PAIR)
-                second_products(g - 1, results, *quantized)
-                staged = keep.tile([P, PAIR], F32, name="staged%d" % g)
-                send_pair(g - 1, 0, results[0], staged[:])
-            quantized = turn_and_quantize(g, banks[(g + 2) % 3], hid_words)
-            if g > 0:
-                send_pair(g - 1, 1, results[1], hid_words[-1])
-            else:
-                words_hot = keep.tile([P, PASSES, PAIR], U32, name="words_hot", tag="grouped0", align_bytes=64)
-                for s in range(PASSES):
-                    gather_words(words_hot[:, s, :], HOT_SLOTS, s)
-
-        split = (PAIR + CARRY) // 2
-        hid_words = [ends[1][:, 0 : H // 2]]
-        first_products(PAIRS + 1, [banks[3]], hid_words)
-        results = both_halves(banks[3], C)
-        second_products(PAIRS, results, *quantized)
-        nc.scalar.copy(ends[0][:, C:PAIR], results[0])
-        scatter(0, split, PAIR + CARRY, ends[0][:, split : PAIR + CARRY])
-        quantized = turn_and_quantize(PAIRS + 1, banks[2], hid_words)
-        nc.scalar.copy(ends[1][:, C:PAIR], results[1])
-        scatter(1, split, PAIR + CARRY, ends[1][:, split : PAIR + CARRY])
-        results = both_halves(banks[0], C)
-        second_products(PAIRS + 1, results, *quantized)
+        last = E // 2 - 1
+        second_products(last, spare_banks[1])
         for h in range(HALVES):
-            nc.scalar.copy(ends[h][:, 0:C], results[h])
-            scatter(h, 0, split, ends[h][:, 0:split])
+            send(last, h, staging("staged_last%d" % h))
             nc.sync.dma_start(out[h * P : (h + 1) * P, :], outs[h][:])

@@ -26,6 +26,8 @@ QUAD = 4
 PLANE_ROWS = 3 * 32 + 4
 BANK_BLOCKS = H // P
 ORDER = list(range(HOT, E)) + [1, 0]
+BATCHES = [4, 4]
+W2 = 4
 EARLY, LATER, HOT_SLOTS = (PAIR, 3 * PAIR), (3 * PAIR, T), (0, PAIR)
 
 
@@ -36,34 +38,34 @@ def tile_moe_hot_mlp_silu_kernel(
     nc = tc.nc
     with ExitStack() as ctx:
         keep = ctx.enter_context(tc.tile_pool(name="keep", bufs=1))
+        shared = ctx.enter_context(tc.tile_pool(name="shared", bufs=1))
         psum = ctx.enter_context(tc.psum_pool(name="psum", bufs=1))
         banks = [psum.tile([P, H], F32, name="bank%d" % b) for b in range(8)]
         first_banks, second_banks, turn_banks, spare_banks = banks[0:2], banks[2:4], banks[4:6], banks[6:8]
 
         def zeroed_planes(name, shape):
             planes = keep.tile(shape, U8, name=name, align_bytes=64)
-            flat = planes[:] if len(shape) == 2 else planes[:].rearrange("p a b -> p (a b)")
+            flat = planes[:].rearrange("p a b -> p (a b)")
             nc.vector.memset(flat.bitcast(I32), 0)
             return planes
 
-        def load_planes(planes, scales):
+        def load_planes(planes, scales, which=range(4)):
             rows = scales.rearrange("e s (q r) w -> r q (e s) w", r=4)
-            for r in range(4):
+            for r in which:
                 nc.sync.dma_start(planes[r:P:32, :, :].bitcast(I32), rows[r].bitcast(I32))
 
         def listed(a, b):
             return offsets[:, a // 16 : b // 16]
 
-        xw = [keep.tile([P, T], I32, name="xw%d" % s, align_bytes=64) for s in range(PASSES)]
+        xw_first = keep.tile([P, T], I32, name="xw_first", align_bytes=64)
+        xw_rest = keep.tile([P, PASSES - 1, T], I32, name="xw_rest", align_bytes=64)
+        xw = [xw_first[:]] + [xw_rest[:, s, :] for s in range(PASSES - 1)]
         offsets = keep.tile([P, T // 16], U16, name="offsets")
-        xs = zeroed_planes("xs", [P, T])
+        xs = shared.tile([P, T], U8, name="xs", align_bytes=64, offset=4 * QUAD * C - T // 2)
+        nc.vector.memset(xs[:].bitcast(I32), 0)
         gate_rows = keep.tile([P, C], F32, name="gate_rows", align_bytes=64)
         nc.vector.memset(gate_rows[:], 0.0)
-
-        def load_words(s):
-            nc.sync.dma_start(xw[s][:], x_words[s].rearrange("p t d -> p (t d)").bitcast(I32))
-
-        load_words(0)
+        nc.sync.dma_start(xw_first[:], x_words[0].rearrange("p t d -> p (t d)").bitcast(I32))
         nc.sync.dma_start(offsets[:], offs)
         for q in range(4):
             queue = nc.sync if q % 2 else nc.scalar
@@ -71,20 +73,18 @@ def tile_moe_hot_mlp_silu_kernel(
                 xs[32 * q : 32 * q + 4 * PASSES, :].bitcast(I32),
                 x_scales[:, 4 * q : 4 * q + 4, :].bitcast(I32),
             )
+        nc.scalar.dma_start(gate_rows[0:E, :], gate[0:1, :].rearrange("o (e c) -> (o e) c", c=C))
         warm = keep.tile([P, 1], F32, name="warm")
         nc.scalar.activation(warm[64:P, :], gate_rows[64:P, 0:1], SILU)
-        for s in range(1, PASSES):
-            load_words(s)
-        nc.sync.dma_start(gate_rows[0:E, :], gate[0:1, :].rearrange("o (e c) -> (o e) c", c=C))
+        nc.sync.dma_start(xw_rest[:], x_words[1:PASSES].rearrange("s p t d -> p s (t d)").bitcast(I32))
 
-        s1_early = zeroed_planes("s1_early", [P, QUAD * PASSES, H])
-        moved = zeroed_planes("moved", [P, PASSES - 1, COLD * C])
+        s1_planes = [zeroed_planes("s1_%d" % b, [P, n * PASSES, H]) for b, n in enumerate(BATCHES) if sum(BATCHES[: b + 1]) <= QUAD]
+        moved = [zeroed_planes("moved%d" % b, [P, PASSES - 1, QUAD * C]) for b in range(2)]
         s2_cold = zeroed_planes("s2_cold", [P, COLD, N])
         ident = keep.tile([P, P], F32, name="ident")
         make_identity(nc, ident[:])
-        w2c = [keep.tile([P, QUAD, 2 * N], U8, name="w2c%d" % b, align_bytes=64) for b in range(COLD // QUAD)]
+        w2c = [keep.tile([P, W2, 2 * N], U8, name="w2c%d" % b, align_bytes=64) for b in range(COLD // W2)]
         w2h = keep.tile([P, HOT, 4 * N], U8, name="w2h", align_bytes=64)
-        gates = keep.tile([P, T], F32, name="gates")
 
         w1_first = keep.tile([P, 2 * PASSES, 2 * H], U8, name="w1_first", align_bytes=64)
         w1 = {HOT + j: w1_first[:, j * PASSES : (j + 1) * PASSES, :] for j in range(2)}
@@ -97,10 +97,14 @@ def tile_moe_hot_mlp_silu_kernel(
                 src = w1c_words[e - HOT].rearrange("s p b -> p s b")
             else:
                 src = w1h_words[e].rearrange("s p i d -> p s (i d)")
-            nc.sync.dma_start(w1[e].bitcast(I32), src.bitcast(I32))
+            if e == ORDER[-1]:
+                for s in range(PASSES):
+                    nc.sync.dma_start(w1[e][:, s, :].bitcast(I32), src[:, s, :].bitcast(I32))
+            else:
+                nc.sync.dma_start(w1[e].bitcast(I32), src.bitcast(I32))
 
         def load_w2c(b):
-            src = w2c_words[b * QUAD : (b + 1) * QUAD].rearrange("e s p b -> p (e s) b")
+            src = w2c_words[b * W2 : (b + 1) * W2].rearrange("e s p b -> p (e s) b")
             nc.sync.dma_start(w2c[b][:].bitcast(I32), src.bitcast(I32))
 
         def as_planes(words_tile, count, width):
@@ -108,21 +112,26 @@ def tile_moe_hot_mlp_silu_kernel(
             return flat[:, 0 : count * width].rearrange("p (a w) -> p a w", w=width)
 
         s1_later = as_planes(w1_first[:], QUAD * PASSES, H)
+        if BATCHES[-1] == QUAD:
+            s1_planes.append(s1_later)
+        else:
+            s1_planes.extend([as_planes(w1[ORDER[j]], 2 * PASSES, H) for j in range(2)])
+        batch_of = [(b, f) for b, n in enumerate(BATCHES) for f in range(n)]
         s1_hot = as_planes(w1[4], HOT * PASSES, H)
         s2_hot = as_planes(w1[5], HOT, N)
 
         def s1(e, s):
             if e < HOT:
                 return s1_hot[:, e * PASSES + s, :]
-            b, f = divmod(e - HOT, QUAD)
-            return (s1_later if b else s1_early)[:, f * PASSES + s, :]
+            b, f = batch_of[e - HOT]
+            return s1_planes[b][:, f * PASSES + s, :]
 
         words = {}
         planes_of = {}
 
         def gather_words(into, slots, s):
             a, b = slots
-            nc.vector.tensor_copy(into, xw[s][:].bitcast(U32).indirect(listed(a, b)))
+            nc.vector.tensor_copy(into, xw[s].bitcast(U32).indirect(listed(a, b)))
             for e in range(a // C, b // C):
                 words[(e, s)] = into[:, e * C - a : (e + 1) * C - a]
 
@@ -130,19 +139,23 @@ def tile_moe_hot_mlp_silu_kernel(
             return keep.tile([P] + shape, U32, name=name, tag=tag or name, align_bytes=64)
 
         gather_words(words_tile("words_early0", [QUAD * C])[:], EARLY, 0)
-        bytes_cold = keep.tile([P, COLD * C], U8, name="bytes_cold", align_bytes=64)
-        for a, b in (EARLY, LATER):
-            nc.vector.tensor_copy(bytes_cold[:, a - PAIR : b - PAIR], xs[:].indirect(listed(a, b)))
-        for s in range(1, PASSES):
-            nc.scalar.dma_start(
-                moved[0:PLANE_ROWS, s - 1, :].bitcast(I32),
-                bytes_cold[4 * s : 4 * s + PLANE_ROWS, :].bitcast(I32),
-            )
-        for e in range(HOT, E):
-            cols = slice((e - HOT) * C, (e - HOT + 1) * C)
-            planes_of[(e, 0)] = bytes_cold[:, cols]
+        bytes_cold = [keep.tile([P, QUAD * C], U8, name="bytes_cold%d" % b, align_bytes=64) for b in range(2)]
+
+        def move_planes(queue, b):
             for s in range(1, PASSES):
-                planes_of[(e, s)] = moved[:, s - 1, cols]
+                queue.dma_start(
+                    moved[b][0:PLANE_ROWS, s - 1, :].bitcast(I32),
+                    bytes_cold[b][4 * s : 4 * s + PLANE_ROWS, :].bitcast(I32),
+                )
+
+        for b, (first, end) in enumerate((EARLY, LATER)):
+            nc.vector.tensor_copy(bytes_cold[b][:], xs[:].indirect(listed(first, end)))
+            for e in range(first // C, end // C):
+                cols = slice(e * C - first, (e + 1) * C - first)
+                planes_of[(e, 0)] = bytes_cold[b][:, cols]
+                for s in range(1, PASSES):
+                    planes_of[(e, s)] = moved[b][:, s - 1, cols]
+        move_planes(nc.scalar, 0)
         for s in range(1, PASSES):
             gather_words(words_tile("words_early%d" % s, [QUAD * C])[:], EARLY, s)
         bytes_hot = keep.tile([P, PAIR], U8, name="bytes_hot", align_bytes=64)
@@ -151,25 +164,38 @@ def tile_moe_hot_mlp_silu_kernel(
             for s in range(PASSES):
                 planes_of[(e, s)] = bytes_hot[4 * s : P, e * C : (e + 1) * C]
 
-        load_planes(s1_early, w1c_scales[0:QUAD])
-        for e in ORDER[0:QUAD]:
-            load_w1(e)
+        def load_batch(b):
+            first = sum(BATCHES[:b])
+            load_planes(s1_planes[b], w1c_scales[first : first + BATCHES[b]])
+
+        def load_w2h():
+            nc.sync.dma_start(w2h[:].bitcast(I32), w2h_words.rearrange("e s p n d -> p (e s) (n d)").bitcast(I32))
+
+        load_batch(0)
+        load_w1(ORDER[0])
+        load_w1(ORDER[1])
+        load_w1(ORDER[2])
+        load_w1(ORDER[3])
         load_w2c(0)
         load_planes(s2_cold, w2c_scales)
+        move_planes(nc.sync, 1)
 
         def load_later():
-            load_planes(s1_later, w1c_scales[QUAD:COLD])
-            for e in ORDER[QUAD:COLD]:
-                load_w1(e)
+            load_batch(1)
+            load_w1(ORDER[4])
+            load_w1(ORDER[5])
+            load_w1(ORDER[6])
+            load_w1(ORDER[7])
             load_w2c(1)
 
         def load_hot():
             load_planes(s1_hot, w1h_scales)
-            for e in ORDER[COLD:]:
-                load_w1(e)
-            nc.sync.dma_start(w2h[:].bitcast(I32), w2h_words.rearrange("e s p n d -> p (e s) (n d)").bitcast(I32))
+            load_w1(ORDER[8])
+            load_w1(ORDER[9])
+            load_w2h()
             load_planes(s2_hot, w2h_scales)
 
+        gates = shared.tile([P, T], F32, name="gates", align_bytes=64, offset=4 * QUAD * C)
         gate_turned = spare_banks[0]
         nc.tensor.transpose(gate_turned[:, 0:P], gate_rows[:], ident[:])
         gate_cols = keep.tile([P, E], F32, name="gate_cols", align_bytes=64)
@@ -181,9 +207,11 @@ def tile_moe_hot_mlp_silu_kernel(
                 nc.tensor.transpose(spread[:, j * C : (j + 1) * C], column.to_broadcast([P, P]), ident[:])
             nc.scalar.copy(gates[:, first * C : (first + count) * C], spread[:, 0 : count * C])
 
-        words_later = words_tile("words_later", [PASSES, QUAD * C], "gate_cols")
-        for s in range(PASSES):
-            gather_words(words_later[:, s, :], LATER, s)
+        words_later = shared.tile([P, QUAD * C], U32, name="words_later0", align_bytes=64, offset=0)
+        gather_words(words_later[:], LATER, 0)
+        for s in range(1, PASSES):
+            gather_words(words_tile("words_later%d" % s, [QUAD * C])[:], LATER, s)
+        gather_words(words_tile("words_hot1", [PAIR])[:], HOT_SLOTS, 1)
 
         outs = [keep.tile([P, T], F32, name="out%d" % h) for h in range(HALVES)]
         hids = {}
@@ -230,7 +258,7 @@ def tile_moe_hot_mlp_silu_kernel(
                 cols = slice(e * C - pair_start(g), (e + 1) * C - pair_start(g))
                 for h in range(HALVES):
                     if e >= HOT:
-                        b, f = divmod(e - HOT, QUAD)
+                        b, f = divmod(e - HOT, W2)
                         lhsT = w2c[b][:, f, h * 2 * P : (h + 1) * 2 * P].bitcast(FP4X4)
                         lhsT_scale = s2_cold[:, e - HOT, h * P : (h + 1) * P]
                     else:
@@ -261,18 +289,16 @@ def tile_moe_hot_mlp_silu_kernel(
             if i == 1:
                 gather_words(words_tile("words_hot0", [PAIR], "grouped0")[:], HOT_SLOTS, 0)
             if i == 2:
-                words_hot = words_tile("words_hot", [PASSES - 1, PAIR], "grouped1")
-                for s in range(1, PASSES):
-                    gather_words(words_hot[:, s - 1, :], HOT_SLOTS, s)
+                gather_words(words_tile("words_hot2", [PAIR], "grouped1")[:], HOT_SLOTS, 2)
             if i >= 3 and i % 2 == 1:
                 g = (i - 3) // 2
-                second_products(g, spare_banks[0] if i - 1 == QUAD else first_bank(i - 1))
+                second_products(g, spare_banks[1 - g % 2] if g in (1,) else first_bank(i - 1))
                 send(g, 0, staging("staged%d" % g))
             if i >= 4 and i % 2 == 0:
                 send((i - 4) // 2, 1, hids[i - 1])
 
         last = E // 2 - 1
-        second_products(last, spare_banks[1])
+        second_products(last, spare_banks[0])
         for h in range(HALVES):
             send(last, h, staging("staged_last%d" % h))
             nc.sync.dma_start(out[h * P : (h + 1) * P, :], outs[h][:])

@@ -49,10 +49,10 @@ def tile_moe_hot_mlp_silu_kernel(
             nc.vector.memset(flat.bitcast(I32), 0)
             return planes
 
-        def load_planes(planes, scales, which=range(4)):
+        def load_planes(planes, scales, which=range(4), queue=nc.sync):
             rows = scales.rearrange("e s (q r) w -> r q (e s) w", r=4)
             for r in which:
-                nc.sync.dma_start(planes[r:P:32, :, :].bitcast(I32), rows[r].bitcast(I32))
+                queue.dma_start(planes[r:P:32, :, :].bitcast(I32), rows[r].bitcast(I32))
 
         def listed(a, b):
             return offsets[:, a // 16 : b // 16]
@@ -79,7 +79,7 @@ def tile_moe_hot_mlp_silu_kernel(
         nc.sync.dma_start(xw_rest[:], x_words[1:PASSES].rearrange("s p t d -> p s (t d)").bitcast(I32))
 
         s1_planes = [zeroed_planes("s1_%d" % b, [P, n * PASSES, H]) for b, n in enumerate(BATCHES) if sum(BATCHES[: b + 1]) <= QUAD]
-        moved = [zeroed_planes("moved%d" % b, [P, PASSES - 1, QUAD * C]) for b in range(2)]
+        moved = zeroed_planes("moved", [P, PASSES - 1, COLD * C])
         s2_cold = zeroed_planes("s2_cold", [P, COLD, N])
         ident = keep.tile([P, P], F32, name="ident")
         make_identity(nc, ident[:])
@@ -111,7 +111,7 @@ def tile_moe_hot_mlp_silu_kernel(
             flat = words_tile.rearrange("p a b -> p (a b)")
             return flat[:, 0 : count * width].rearrange("p (a w) -> p a w", w=width)
 
-        s1_later = as_planes(w1_first[:], QUAD * PASSES, H)
+        s1_later = zeroed_planes("s1_later", [P, QUAD * PASSES, H])
         if BATCHES[-1] == QUAD:
             s1_planes.append(s1_later)
         else:
@@ -139,23 +139,22 @@ def tile_moe_hot_mlp_silu_kernel(
             return keep.tile([P] + shape, U32, name=name, tag=tag or name, align_bytes=64)
 
         gather_words(words_tile("words_early0", [QUAD * C])[:], EARLY, 0)
-        bytes_cold = [keep.tile([P, QUAD * C], U8, name="bytes_cold%d" % b, align_bytes=64) for b in range(2)]
+        bytes_cold = keep.tile([P, COLD * C], U8, name="bytes_cold", align_bytes=64)
+        for a, b in (EARLY, LATER):
+            nc.vector.tensor_copy(bytes_cold[:, a - PAIR : b - PAIR], xs[:].indirect(listed(a, b)))
 
         def move_planes(queue, b):
             for s in range(1, PASSES):
                 queue.dma_start(
-                    moved[b][0:PLANE_ROWS, s - 1, :].bitcast(I32),
-                    bytes_cold[b][4 * s : 4 * s + PLANE_ROWS, :].bitcast(I32),
+                    moved[0:PLANE_ROWS, s - 1, :].bitcast(I32),
+                    bytes_cold[4 * s : 4 * s + PLANE_ROWS, :].bitcast(I32),
                 )
 
-        for b, (first, end) in enumerate((EARLY, LATER)):
-            nc.vector.tensor_copy(bytes_cold[b][:], xs[:].indirect(listed(first, end)))
-            for e in range(first // C, end // C):
-                cols = slice(e * C - first, (e + 1) * C - first)
-                planes_of[(e, 0)] = bytes_cold[b][:, cols]
-                for s in range(1, PASSES):
-                    planes_of[(e, s)] = moved[b][:, s - 1, cols]
-        move_planes(nc.scalar, 0)
+        for e in range(HOT, E):
+            cols = slice((e - HOT) * C, (e - HOT + 1) * C)
+            planes_of[(e, 0)] = bytes_cold[:, cols]
+            for s in range(1, PASSES):
+                planes_of[(e, s)] = moved[:, s - 1, cols]
         for s in range(1, PASSES):
             gather_words(words_tile("words_early%d" % s, [QUAD * C])[:], EARLY, s)
         bytes_hot = keep.tile([P, PAIR], U8, name="bytes_hot", align_bytes=64)
@@ -166,34 +165,34 @@ def tile_moe_hot_mlp_silu_kernel(
 
         def load_batch(b):
             first = sum(BATCHES[:b])
-            load_planes(s1_planes[b], w1c_scales[first : first + BATCHES[b]])
+            load_planes(s1_planes[b], w1c_scales[first : first + BATCHES[b]], queue=nc.gpsimd)
 
         def load_w2h():
             nc.sync.dma_start(w2h[:].bitcast(I32), w2h_words.rearrange("e s p n d -> p (e s) (n d)").bitcast(I32))
 
         load_batch(0)
+        load_planes(s2_cold, w2c_scales, queue=nc.gpsimd)
+        load_batch(1)
         load_w1(ORDER[0])
         load_w1(ORDER[1])
-        load_w1(ORDER[2])
-        load_w1(ORDER[3])
-        load_w2c(0)
-        load_planes(s2_cold, w2c_scales)
         move_planes(nc.sync, 1)
+        load_w1(ORDER[2])
+        load_w2c(0)
+        load_w1(ORDER[3])
 
         def load_later():
-            load_batch(1)
             load_w1(ORDER[4])
             load_w1(ORDER[5])
             load_w1(ORDER[6])
-            load_w1(ORDER[7])
             load_w2c(1)
+            load_w1(ORDER[7])
 
         def load_hot():
-            load_planes(s1_hot, w1h_scales)
+            load_planes(s1_hot, w1h_scales, queue=nc.gpsimd)
+            load_planes(s2_hot, w2h_scales, queue=nc.gpsimd)
             load_w1(ORDER[8])
             load_w1(ORDER[9])
             load_w2h()
-            load_planes(s2_hot, w2h_scales)
 
         gates = shared.tile([P, T], F32, name="gates", align_bytes=64, offset=4 * QUAD * C)
         gate_turned = spare_banks[0]
@@ -292,7 +291,7 @@ def tile_moe_hot_mlp_silu_kernel(
                 gather_words(words_tile("words_hot2", [PAIR], "grouped1")[:], HOT_SLOTS, 2)
             if i >= 3 and i % 2 == 1:
                 g = (i - 3) // 2
-                second_products(g, spare_banks[1 - g % 2] if g in (1,) else first_bank(i - 1))
+                second_products(g, spare_banks[1 - g % 2] if g in () else first_bank(i - 1))
                 send(g, 0, staging("staged%d" % g))
             if i >= 4 and i % 2 == 0:
                 send((i - 4) // 2, 1, hids[i - 1])

@@ -38,14 +38,13 @@ def tile_moe_hot_mlp_silu_kernel(
     nc = tc.nc
     with ExitStack() as ctx:
         keep = ctx.enter_context(tc.tile_pool(name="keep", bufs=1))
-        shared = ctx.enter_context(tc.tile_pool(name="shared", bufs=1))
         psum = ctx.enter_context(tc.psum_pool(name="psum", bufs=1))
         banks = [psum.tile([P, H], F32, name="bank%d" % b) for b in range(8)]
         first_banks, second_banks, turn_banks, spare_banks = banks[0:2], banks[2:4], banks[4:6], banks[6:8]
 
         def zeroed_planes(name, shape):
             planes = keep.tile(shape, U8, name=name, align_bytes=64)
-            flat = planes[:].rearrange("p a b -> p (a b)")
+            flat = planes[:] if len(shape) == 2 else planes[:].rearrange("p a b -> p (a b)")
             nc.vector.memset(flat.bitcast(I32), 0)
             return planes
 
@@ -57,15 +56,16 @@ def tile_moe_hot_mlp_silu_kernel(
         def listed(a, b):
             return offsets[:, a // 16 : b // 16]
 
-        xw_first = keep.tile([P, T], I32, name="xw_first", align_bytes=64)
-        xw_rest = keep.tile([P, PASSES - 1, T], I32, name="xw_rest", align_bytes=64)
-        xw = [xw_first[:]] + [xw_rest[:, s, :] for s in range(PASSES - 1)]
+        xw = [keep.tile([P, T], I32, name="xw%d" % s, align_bytes=64) for s in range(PASSES)]
         offsets = keep.tile([P, T // 16], U16, name="offsets")
-        xs = shared.tile([P, T], U8, name="xs", align_bytes=64, offset=4 * QUAD * C - T // 2)
-        nc.vector.memset(xs[:].bitcast(I32), 0)
+        xs = zeroed_planes("xs", [P, T])
         gate_rows = keep.tile([P, C], F32, name="gate_rows", align_bytes=64)
         nc.vector.memset(gate_rows[:], 0.0)
-        nc.sync.dma_start(xw_first[:], x_words[0].rearrange("p t d -> p (t d)").bitcast(I32))
+
+        def load_words(s):
+            nc.sync.dma_start(xw[s][:], x_words[s].rearrange("p t d -> p (t d)").bitcast(I32))
+
+        load_words(0)
         nc.sync.dma_start(offsets[:], offs)
         for q in range(4):
             queue = nc.sync if q % 2 else nc.scalar
@@ -73,18 +73,20 @@ def tile_moe_hot_mlp_silu_kernel(
                 xs[32 * q : 32 * q + 4 * PASSES, :].bitcast(I32),
                 x_scales[:, 4 * q : 4 * q + 4, :].bitcast(I32),
             )
-        nc.scalar.dma_start(gate_rows[0:E, :], gate[0:1, :].rearrange("o (e c) -> (o e) c", c=C))
         warm = keep.tile([P, 1], F32, name="warm")
         nc.scalar.activation(warm[64:P, :], gate_rows[64:P, 0:1], SILU)
-        nc.sync.dma_start(xw_rest[:], x_words[1:PASSES].rearrange("s p t d -> p s (t d)").bitcast(I32))
+        for s in range(1, PASSES):
+            load_words(s)
+        nc.sync.dma_start(gate_rows[0:E, :], gate[0:1, :].rearrange("o (e c) -> (o e) c", c=C))
 
-        s1_planes = [zeroed_planes("s1_%d" % b, [P, n * PASSES, H]) for b, n in enumerate(BATCHES) if sum(BATCHES[: b + 1]) <= QUAD]
+        s1_planes = [zeroed_planes("s1_%d" % b, [P, n * PASSES, H]) for b, n in enumerate(BATCHES) ]
         moved = zeroed_planes("moved", [P, PASSES - 1, COLD * C])
         s2_cold = zeroed_planes("s2_cold", [P, COLD, N])
         ident = keep.tile([P, P], F32, name="ident")
         make_identity(nc, ident[:])
         w2c = [keep.tile([P, W2, 2 * N], U8, name="w2c%d" % b, align_bytes=64) for b in range(COLD // W2)]
         w2h = keep.tile([P, HOT, 4 * N], U8, name="w2h", align_bytes=64)
+        gates = keep.tile([P, T], F32, name="gates")
 
         w1_first = keep.tile([P, 2 * PASSES, 2 * H], U8, name="w1_first", align_bytes=64)
         w1 = {HOT + j: w1_first[:, j * PASSES : (j + 1) * PASSES, :] for j in range(2)}
@@ -111,11 +113,6 @@ def tile_moe_hot_mlp_silu_kernel(
             flat = words_tile.rearrange("p a b -> p (a b)")
             return flat[:, 0 : count * width].rearrange("p (a w) -> p a w", w=width)
 
-        s1_later = zeroed_planes("s1_later", [P, QUAD * PASSES, H])
-        if BATCHES[-1] == QUAD:
-            s1_planes.append(s1_later)
-        else:
-            s1_planes.extend([as_planes(w1[ORDER[j]], 2 * PASSES, H) for j in range(2)])
         batch_of = [(b, f) for b, n in enumerate(BATCHES) for f in range(n)]
         s1_hot = as_planes(w1[4], HOT * PASSES, H)
         s2_hot = as_planes(w1[5], HOT, N)
@@ -131,7 +128,7 @@ def tile_moe_hot_mlp_silu_kernel(
 
         def gather_words(into, slots, s):
             a, b = slots
-            nc.vector.tensor_copy(into, xw[s].bitcast(U32).indirect(listed(a, b)))
+            nc.vector.tensor_copy(into, xw[s][:].bitcast(U32).indirect(listed(a, b)))
             for e in range(a // C, b // C):
                 words[(e, s)] = into[:, e * C - a : (e + 1) * C - a]
 
@@ -171,30 +168,29 @@ def tile_moe_hot_mlp_silu_kernel(
             nc.sync.dma_start(w2h[:].bitcast(I32), w2h_words.rearrange("e s p n d -> p (e s) (n d)").bitcast(I32))
 
         load_batch(0)
-        load_planes(s2_cold, w2c_scales, queue=nc.gpsimd)
         load_batch(1)
         load_w1(ORDER[0])
         load_w1(ORDER[1])
         move_planes(nc.sync, 1)
         load_w1(ORDER[2])
-        load_w2c(0)
         load_w1(ORDER[3])
+        load_w2c(0)
+        load_planes(s2_cold, w2c_scales)
 
         def load_later():
             load_w1(ORDER[4])
             load_w1(ORDER[5])
             load_w1(ORDER[6])
-            load_w2c(1)
             load_w1(ORDER[7])
+            load_w2c(1)
 
         def load_hot():
             load_planes(s1_hot, w1h_scales, queue=nc.gpsimd)
-            load_planes(s2_hot, w2h_scales, queue=nc.gpsimd)
             load_w1(ORDER[8])
             load_w1(ORDER[9])
             load_w2h()
+            load_planes(s2_hot, w2h_scales)
 
-        gates = shared.tile([P, T], F32, name="gates", align_bytes=64, offset=4 * QUAD * C)
         gate_turned = spare_banks[0]
         nc.tensor.transpose(gate_turned[:, 0:P], gate_rows[:], ident[:])
         gate_cols = keep.tile([P, E], F32, name="gate_cols", align_bytes=64)
@@ -206,11 +202,9 @@ def tile_moe_hot_mlp_silu_kernel(
                 nc.tensor.transpose(spread[:, j * C : (j + 1) * C], column.to_broadcast([P, P]), ident[:])
             nc.scalar.copy(gates[:, first * C : (first + count) * C], spread[:, 0 : count * C])
 
-        words_later = shared.tile([P, QUAD * C], U32, name="words_later0", align_bytes=64, offset=0)
-        gather_words(words_later[:], LATER, 0)
-        for s in range(1, PASSES):
-            gather_words(words_tile("words_later%d" % s, [QUAD * C])[:], LATER, s)
-        gather_words(words_tile("words_hot1", [PAIR])[:], HOT_SLOTS, 1)
+        words_later = words_tile("words_later", [PASSES, QUAD * C], "gate_rows")
+        for s in range(PASSES):
+            gather_words(words_later[:, s, :], LATER, s)
 
         outs = [keep.tile([P, T], F32, name="out%d" % h) for h in range(HALVES)]
         hids = {}
@@ -288,7 +282,9 @@ def tile_moe_hot_mlp_silu_kernel(
             if i == 1:
                 gather_words(words_tile("words_hot0", [PAIR], "grouped0")[:], HOT_SLOTS, 0)
             if i == 2:
-                gather_words(words_tile("words_hot2", [PAIR], "grouped1")[:], HOT_SLOTS, 2)
+                words_hot = words_tile("words_hot", [PASSES - 1, PAIR], "grouped1")
+                for s in range(1, PASSES):
+                    gather_words(words_hot[:, s - 1, :], HOT_SLOTS, s)
             if i >= 3 and i % 2 == 1:
                 g = (i - 3) // 2
                 second_products(g, spare_banks[1 - g % 2] if g in () else first_bank(i - 1))

@@ -21,14 +21,12 @@ P = 128
 PASSES = K // 512
 COLD = E - HOT
 HALVES = N // P
-PAIR = 2 * C
-QUAD = 4
+PAIRS = E // 2
+PAIR_SLOTS = 2 * C
+QUAD = COLD // 2
 PLANE_ROWS = 3 * 32 + 4
 BANK_BLOCKS = H // P
-ORDER = list(range(HOT, E)) + [1, 0]
-BATCHES = [4, 4]
-W2 = 4
-EARLY, LATER, HOT_SLOTS = (PAIR, 3 * PAIR), (3 * PAIR, T), (0, PAIR)
+EARLY, LATER = (T - QUAD * C, T), (0, T - QUAD * C)
 
 
 def tile_moe_hot_mlp_silu_kernel(
@@ -40,17 +38,16 @@ def tile_moe_hot_mlp_silu_kernel(
         keep = ctx.enter_context(tc.tile_pool(name="keep", bufs=1))
         psum = ctx.enter_context(tc.psum_pool(name="psum", bufs=1))
         banks = [psum.tile([P, H], F32, name="bank%d" % b) for b in range(8)]
-        first_banks, second_banks, turn_banks, spare_banks = banks[0:2], banks[2:4], banks[4:6], banks[6:8]
+        lead_banks, follow_banks, turn_banks, spare_banks = banks[0:2], banks[2:4], banks[4:6], banks[6:8]
 
-        def zeroed_planes(name, shape):
-            planes = keep.tile(shape, U8, name=name, align_bytes=64)
-            flat = planes[:] if len(shape) == 2 else planes[:].rearrange("p a b -> p (a b)")
-            nc.vector.memset(flat.bitcast(I32), 0)
+        def zeroed_planes(name, count, width):
+            planes = keep.tile([P, count, width], U8, name=name, align_bytes=64)
+            nc.vector.memset(planes[:].rearrange("p a w -> p (a w)").bitcast(I32), 0)
             return planes
 
-        def load_planes(planes, scales, which=range(4), queue=nc.sync):
+        def load_planes(queue, planes, scales):
             rows = scales.rearrange("e s (q r) w -> r q (e s) w", r=4)
-            for r in which:
+            for r in range(4):
                 queue.dma_start(planes[r:P:32, :, :].bitcast(I32), rows[r].bitcast(I32))
 
         def listed(a, b):
@@ -58,7 +55,7 @@ def tile_moe_hot_mlp_silu_kernel(
 
         xw = [keep.tile([P, T], I32, name="xw%d" % s, align_bytes=64) for s in range(PASSES)]
         offsets = keep.tile([P, T // 16], U16, name="offsets")
-        xs = zeroed_planes("xs", [P, T])
+        xs = zeroed_planes("xs", 1, T)[:, 0, :]
         gate_rows = keep.tile([P, C], F32, name="gate_rows", align_bytes=64)
         nc.vector.memset(gate_rows[:], 0.0)
 
@@ -79,52 +76,34 @@ def tile_moe_hot_mlp_silu_kernel(
             load_words(s)
         nc.sync.dma_start(gate_rows[0:E, :], gate[0:1, :].rearrange("o (e c) -> (o e) c", c=C))
 
-        s1_planes = [zeroed_planes("s1_%d" % b, [P, n * PASSES, H]) for b, n in enumerate(BATCHES) ]
-        moved = zeroed_planes("moved", [P, PASSES - 1, COLD * C])
-        s2_cold = zeroed_planes("s2_cold", [P, COLD, N])
+        s1_cold = {b: zeroed_planes("s1_cold%d" % b, QUAD * PASSES, H) for b in (1, 0)}
+        moved = {b: zeroed_planes("moved%d" % b, PASSES - 1, QUAD * C) for b in (1, 0)}
+        s2_cold = zeroed_planes("s2_cold", COLD, N)
         ident = keep.tile([P, P], F32, name="ident")
         make_identity(nc, ident[:])
-        w2c = [keep.tile([P, W2, 2 * N], U8, name="w2c%d" % b, align_bytes=64) for b in range(COLD // W2)]
+        w1 = [keep.tile([P, PASSES, (4 if e < HOT else 2) * H], U8, name="w1_%d" % e, align_bytes=64) for e in range(E)]
+        w2c = [keep.tile([P, QUAD, 2 * N], U8, name="w2c%d" % b, align_bytes=64) for b in range(2)]
         w2h = keep.tile([P, HOT, 4 * N], U8, name="w2h", align_bytes=64)
         gates = keep.tile([P, T], F32, name="gates")
 
-        w1_first = keep.tile([P, 2 * PASSES, 2 * H], U8, name="w1_first", align_bytes=64)
-        w1 = {HOT + j: w1_first[:, j * PASSES : (j + 1) * PASSES, :] for j in range(2)}
-        for e in ORDER[2:]:
-            width = 2 * H if e >= HOT else 4 * H
-            w1[e] = keep.tile([P, PASSES, width], U8, name="w1_%d" % e, align_bytes=64)[:]
+        def spent_as_planes(e, width):
+            return w1[e][:].rearrange("p s b -> p (s b)").rearrange("p (a w) -> p a w", w=width)
+
+        s1_hot = spent_as_planes(E - 1, H)
+        s2_hot = spent_as_planes(E - 2, N)[:, 0:HOT, :]
 
         def load_w1(e):
             if e >= HOT:
                 src = w1c_words[e - HOT].rearrange("s p b -> p s b")
             else:
                 src = w1h_words[e].rearrange("s p i d -> p s (i d)")
-            if e == ORDER[-1]:
-                for s in range(PASSES):
-                    nc.sync.dma_start(w1[e][:, s, :].bitcast(I32), src[:, s, :].bitcast(I32))
-            else:
-                nc.sync.dma_start(w1[e].bitcast(I32), src.bitcast(I32))
+            nc.sync.dma_start(w1[e][:].bitcast(I32), src.bitcast(I32))
 
         def load_w2c(b):
-            src = w2c_words[b * W2 : (b + 1) * W2].rearrange("e s p b -> p (e s) b")
+            src = w2c_words[b * QUAD : (b + 1) * QUAD].rearrange("e s p b -> p (e s) b")
             nc.sync.dma_start(w2c[b][:].bitcast(I32), src.bitcast(I32))
 
-        def as_planes(words_tile, count, width):
-            flat = words_tile.rearrange("p a b -> p (a b)")
-            return flat[:, 0 : count * width].rearrange("p (a w) -> p a w", w=width)
-
-        batch_of = [(b, f) for b, n in enumerate(BATCHES) for f in range(n)]
-        s1_hot = as_planes(w1[4], HOT * PASSES, H)
-        s2_hot = as_planes(w1[5], HOT, N)
-
-        def s1(e, s):
-            if e < HOT:
-                return s1_hot[:, e * PASSES + s, :]
-            b, f = batch_of[e - HOT]
-            return s1_planes[b][:, f * PASSES + s, :]
-
         words = {}
-        planes_of = {}
 
         def gather_words(into, slots, s):
             a, b = slots
@@ -132,168 +111,144 @@ def tile_moe_hot_mlp_silu_kernel(
             for e in range(a // C, b // C):
                 words[(e, s)] = into[:, e * C - a : (e + 1) * C - a]
 
-        def words_tile(name, shape, tag=None):
-            return keep.tile([P] + shape, U32, name=name, tag=tag or name, align_bytes=64)
+        def words_tile(name, count, slots, tag=None):
+            return keep.tile([P, count, slots[1] - slots[0]], U32, name=name, tag=tag or name, align_bytes=64)
 
-        gather_words(words_tile("words_early0", [QUAD * C])[:], EARLY, 0)
-        bytes_cold = keep.tile([P, COLD * C], U8, name="bytes_cold", align_bytes=64)
+        words_early = [words_tile("words_early%d" % s, 1, EARLY) for s in range(PASSES)]
+        gather_words(words_early[0][:, 0, :], EARLY, 0)
+        slot_bytes = keep.tile([P, T], U8, name="slot_bytes", align_bytes=64)
         for a, b in (EARLY, LATER):
-            nc.vector.tensor_copy(bytes_cold[:, a - PAIR : b - PAIR], xs[:].indirect(listed(a, b)))
+            nc.vector.tensor_copy(slot_bytes[:, a:b], xs[:].indirect(listed(a, b)))
 
         def move_planes(queue, b):
+            first = (HOT + b * QUAD) * C
             for s in range(1, PASSES):
                 queue.dma_start(
-                    moved[0:PLANE_ROWS, s - 1, :].bitcast(I32),
-                    bytes_cold[4 * s : 4 * s + PLANE_ROWS, :].bitcast(I32),
+                    moved[b][0:PLANE_ROWS, s - 1, :].bitcast(I32),
+                    slot_bytes[4 * s : 4 * s + PLANE_ROWS, first : first + QUAD * C].bitcast(I32),
                 )
 
-        for e in range(HOT, E):
-            cols = slice((e - HOT) * C, (e - HOT + 1) * C)
-            planes_of[(e, 0)] = bytes_cold[:, cols]
-            for s in range(1, PASSES):
-                planes_of[(e, s)] = moved[:, s - 1, cols]
         for s in range(1, PASSES):
-            gather_words(words_tile("words_early%d" % s, [QUAD * C])[:], EARLY, s)
-        bytes_hot = keep.tile([P, PAIR], U8, name="bytes_hot", align_bytes=64)
-        nc.vector.tensor_copy(bytes_hot[:], xs[:].indirect(listed(*HOT_SLOTS)))
-        for e in range(HOT):
-            for s in range(PASSES):
-                planes_of[(e, s)] = bytes_hot[4 * s : P, e * C : (e + 1) * C]
+            gather_words(words_early[s][:, 0, :], EARLY, s)
 
-        def load_batch(b):
-            first = sum(BATCHES[:b])
-            load_planes(s1_planes[b], w1c_scales[first : first + BATCHES[b]], queue=nc.gpsimd)
+        def token_plane(e, s):
+            if e < HOT or s == 0:
+                return slot_bytes[4 * s : P, e * C : (e + 1) * C]
+            b, f = divmod(e - HOT, QUAD)
+            return moved[b][:, s - 1, f * C : (f + 1) * C]
 
-        def load_w2h():
-            nc.sync.dma_start(w2h[:].bitcast(I32), w2h_words.rearrange("e s p n d -> p (e s) (n d)").bitcast(I32))
-
-        load_batch(0)
-        load_batch(1)
-        load_w1(ORDER[0])
-        load_w1(ORDER[1])
+        for b in (1, 0):
+            load_planes(nc.gpsimd, s1_cold[b], w1c_scales[b * QUAD : (b + 1) * QUAD])
+        load_w1(E - 1)
         move_planes(nc.sync, 1)
-        load_w1(ORDER[2])
-        load_w1(ORDER[3])
+        load_w1(E - 2)
+        for e in (E - 3, E - 4):
+            load_w1(e)
+        load_w2c(1)
+        load_planes(nc.sync, s2_cold, w2c_scales)
+        move_planes(nc.sync, 0)
+        for e in range(E - QUAD - 1, HOT - 1, -1):
+            load_w1(e)
         load_w2c(0)
-        load_planes(s2_cold, w2c_scales)
-
-        def load_later():
-            load_w1(ORDER[4])
-            load_w1(ORDER[5])
-            load_w1(ORDER[6])
-            load_w1(ORDER[7])
-            load_w2c(1)
-
-        def load_hot():
-            load_planes(s1_hot, w1h_scales, queue=nc.gpsimd)
-            load_w1(ORDER[8])
-            load_w1(ORDER[9])
-            load_w2h()
-            load_planes(s2_hot, w2h_scales)
+        for e in range(HOT - 1, -1, -1):
+            load_w1(e)
+        nc.sync.dma_start(w2h[:].bitcast(I32), w2h_words.rearrange("e s p n d -> p (e s) (n d)").bitcast(I32))
 
         gate_turned = spare_banks[0]
         nc.tensor.transpose(gate_turned[:, 0:P], gate_rows[:], ident[:])
         gate_cols = keep.tile([P, E], F32, name="gate_cols", align_bytes=64)
         nc.scalar.copy(gate_cols[:], gate_turned[:, 0:E])
-        for first, spread in zip(range(0, E, BANK_BLOCKS), (spare_banks[1], turn_banks[1], second_banks[1])):
+        for first, spread in zip(range(0, E, BANK_BLOCKS), (spare_banks[1], turn_banks[1], follow_banks[1])):
             count = min(BANK_BLOCKS, E - first)
             for j in range(count):
                 column = gate_cols[:, first + j : first + j + 1]
                 nc.tensor.transpose(spread[:, j * C : (j + 1) * C], column.to_broadcast([P, P]), ident[:])
             nc.scalar.copy(gates[:, first * C : (first + count) * C], spread[:, 0 : count * C])
 
-        words_later = words_tile("words_later", [PASSES, QUAD * C], "gate_rows")
-        for s in range(PASSES):
+        words_later = words_tile("words_later", PASSES - 1, LATER, "gate_rows")
+        for s in range(PASSES - 1):
             gather_words(words_later[:, s, :], LATER, s)
 
         outs = [keep.tile([P, T], F32, name="out%d" % h) for h in range(HALVES)]
-        hids = {}
-        quantized = {}
-        results = {}
 
-        def first_bank(i):
-            return (second_banks if i % 2 else first_banks)[i // 2 % 2]
+        def experts(g):
+            return (E - 1 - 2 * g, E - 2 - 2 * g)
 
-        def first_product(i):
-            e = ORDER[i]
-            acc = first_bank(i)
-            for s in range(PASSES):
-                nc.tensor.matmul_mx(
-                    out=acc[:], lhsT=words[(e, s)].bitcast(FP8X4), lhsT_scale=planes_of[(e, s)],
-                    rhs=w1[e][:, s, :].bitcast(FP4X4 if e >= HOT else FP8X4), rhs_scale=s1(e, s),
-                    start=(s == 0), stop=(s == PASSES - 1),
-                )
-            hids[i] = keep.tile([P, H // 2], F32, name="hid%d" % e, align_bytes=64)[:]
-            hid = hids[i].bitcast(BF16).rearrange("c (u p v) -> c u p v", u=2, v=2)
-            nc.scalar.activation(hid, acc[:].rearrange("c (p u v) -> c u p v", u=2, v=2), SILU)
+        def first_products(g):
+            hids = []
+            for e, acc in zip(experts(g), (lead_banks[g % 2], follow_banks[g % 2])):
+                b, f = divmod(e - HOT, QUAD)
+                planes = s1_cold[b][:, f * PASSES :, :] if e >= HOT else s1_hot[:, e * PASSES :, :]
+                for s in range(PASSES):
+                    nc.tensor.matmul_mx(
+                        out=acc[:], lhsT=words[(e, s)].bitcast(FP8X4), lhsT_scale=token_plane(e, s),
+                        rhs=w1[e][:, s, :].bitcast(FP4X4 if e >= HOT else FP8X4), rhs_scale=planes[:, s, :],
+                        start=(s == 0), stop=(s == PASSES - 1),
+                    )
+                hid = keep.tile([P, H // 2], F32, name="hid%d" % e, align_bytes=64)
+                ordered = hid[:].bitcast(BF16).rearrange("c (u p v) -> c u p v", u=2, v=2)
+                nc.scalar.activation(ordered, acc[:].rearrange("c (p u v) -> c u p v", u=2, v=2), SILU)
+                hids.append(hid)
+            return hids
 
-        def turn_and_quantize(i):
-            e = ORDER[i]
-            turned = turn_banks[i % 2][:, 0 : 2 * C].rearrange("p (u c) -> p u c", u=2)
-            for u in range(2):
-                nc.tensor.transpose(turned[:, u, :], hids[i][:, u * P : (u + 1) * P], ident[:])
-            grouped = keep.tile([P, C * 4], BF16, name="grouped%d" % i, align_bytes=64)
+        def turn_and_quantize(g, hids):
+            turned = turn_banks[g % 2][:].rearrange("p (j u c) -> p j u c", u=2, c=C)
+            for j, hid in enumerate(hids):
+                for u in range(2):
+                    nc.tensor.transpose(turned[:, j, u, :], hid[:, u * P : (u + 1) * P], ident[:])
+            grouped = keep.tile([P, PAIR_SLOTS * 4], BF16, name="grouped%d" % g, align_bytes=64)
             nc.scalar.copy(
-                grouped[:].bitcast(F32).rearrange("p (c u) -> p c u", u=2), turned.rearrange("p u c -> p c u"),
+                grouped[:].bitcast(F32).rearrange("p (j c u) -> p j c u", u=2, c=C),
+                turned.rearrange("p j u c -> p j c u"),
             )
-            codes = keep.tile([P, C], U32, name="codes%d" % e, align_bytes=64)
-            scales = keep.tile([P, C], U8, name="scales%d" % e, align_bytes=64)
+            codes = keep.tile([P, PAIR_SLOTS], U32, name="codes%d" % g, align_bytes=64)
+            scales = keep.tile([P, PAIR_SLOTS], U8, name="scales%d" % g, align_bytes=64)
             nc.vector.quantize_mx(out=codes[:].bitcast(FP8X4), scales=scales[:], in_=grouped[:])
-            quantized[e] = codes, scales
+            return codes, scales
 
-        def pair_start(g):
-            return min(ORDER[2 * g : 2 * g + 2]) * C
-
-        def second_products(g, bank):
-            results[g] = [bank[:, h * PAIR : (h + 1) * PAIR] for h in range(HALVES)]
-            for e in ORDER[2 * g : 2 * g + 2]:
-                codes, scales = quantized[e]
-                cols = slice(e * C - pair_start(g), (e + 1) * C - pair_start(g))
-                for h in range(HALVES):
+        def second_products(g, bank, codes, scales):
+            results = [bank[:, h * PAIR_SLOTS : (h + 1) * PAIR_SLOTS] for h in range(HALVES)]
+            for h in range(HALVES):
+                for j, e in enumerate(experts(g)):
                     if e >= HOT:
-                        b, f = divmod(e - HOT, W2)
+                        b, f = divmod(e - HOT, QUAD)
                         lhsT = w2c[b][:, f, h * 2 * P : (h + 1) * 2 * P].bitcast(FP4X4)
                         lhsT_scale = s2_cold[:, e - HOT, h * P : (h + 1) * P]
                     else:
                         lhsT = w2h[:, e, h * 4 * P : (h + 1) * 4 * P].bitcast(FP8X4)
                         lhsT_scale = s2_hot[:, e, h * P : (h + 1) * P]
                     nc.tensor.matmul_mx(
-                        out=results[g][h][:, cols], lhsT=lhsT, lhsT_scale=lhsT_scale,
-                        rhs=codes[:].bitcast(FP8X4), rhs_scale=scales[:], start=True, stop=True,
+                        out=results[h][:, (1 - j) * C : (2 - j) * C], lhsT=lhsT, lhsT_scale=lhsT_scale,
+                        rhs=codes[:, j * C : (j + 1) * C].bitcast(FP8X4), rhs_scale=scales[:, j * C : (j + 1) * C],
+                        start=True, stop=True,
                     )
+            return results
 
-        def send(g, h, staged):
-            a = pair_start(g)
-            nc.scalar.copy(staged, results[g][h])
-            nc.vector.tensor_tensor(outs[h][:].indirect(listed(a, a + PAIR)), staged, gates[:, a : a + PAIR], MULT)
+        def send(g, h, result, staged):
+            a = min(experts(g)) * C
+            nc.scalar.copy(staged[:], result)
+            window = outs[h][:].indirect(listed(a, a + PAIR_SLOTS))
+            nc.vector.tensor_tensor(window, staged[:], gates[:, a : a + PAIR_SLOTS], MULT)
 
         def staging(name):
-            return keep.tile([P, PAIR], F32, name=name, align_bytes=64)[:]
+            return keep.tile([P, PAIR_SLOTS], F32, name=name, align_bytes=64)
 
-        for i in range(E + 1):
-            if i < E:
-                first_product(i)
-            if i == 1:
-                load_later()
-            if i == 3:
-                load_hot()
-            if i >= 1:
-                turn_and_quantize(i - 1)
-            if i == 1:
-                gather_words(words_tile("words_hot0", [PAIR], "grouped0")[:], HOT_SLOTS, 0)
-            if i == 2:
-                words_hot = words_tile("words_hot", [PASSES - 1, PAIR], "grouped1")
-                for s in range(1, PASSES):
-                    gather_words(words_hot[:, s - 1, :], HOT_SLOTS, s)
-            if i >= 3 and i % 2 == 1:
-                g = (i - 3) // 2
-                second_products(g, spare_banks[1 - g % 2] if g in () else first_bank(i - 1))
-                send(g, 0, staging("staged%d" % g))
-            if i >= 4 and i % 2 == 0:
-                send((i - 4) // 2, 1, hids[i - 1])
+        quantized = None
+        for g in range(PAIRS):
+            hids = first_products(g)
+            if g == 0:
+                load_planes(nc.gpsimd, s1_hot, w1h_scales)
+                load_planes(nc.sync, s2_hot, w2h_scales)
+            else:
+                results = second_products(g - 1, lead_banks[g % 2], *quantized)
+                send(g - 1, 0, results[0], staging("staged%d" % g))
+            quantized = turn_and_quantize(g, hids)
+            if g == 0:
+                gather_words(words_tile("words_last", 1, LATER, "grouped0")[:, 0, :], LATER, PASSES - 1)
+            else:
+                send(g - 1, 1, results[1], hids[-1])
 
-        last = E // 2 - 1
-        second_products(last, spare_banks[0])
+        results = second_products(PAIRS - 1, spare_banks[0], *quantized)
         for h in range(HALVES):
-            send(last, h, staging("staged_last%d" % h))
+            send(PAIRS - 1, h, results[h], staging("staged_last%d" % h))
             nc.sync.dma_start(out[h * P : (h + 1) * P, :], outs[h][:])

@@ -70,8 +70,6 @@ def tile_moe_hot_mlp_silu_kernel(
                 xs[32 * q : 32 * q + 4 * PASSES, :].bitcast(I32),
                 x_scales[:, 4 * q : 4 * q + 4, :].bitcast(I32),
             )
-        warm = keep.tile([P, 1], F32, name="warm")
-        nc.scalar.activation(warm[64:P, :], gate_rows[64:P, 0:1], SILU)
         for s in range(1, PASSES):
             load_words(s)
         nc.sync.dma_start(gate_rows[0:E, :], gate[0:1, :].rearrange("o (e c) -> (o e) c", c=C))

@@ -15,6 +15,7 @@ U8 = mybir.dt.uint8
 FP8X4 = mybir.dt.float8_e4m3fn_x4
 FP4X4 = mybir.dt.float4_e2m1fn_x4
 SILU = mybir.ActivationFunctionType.Silu
+COPY = mybir.ActivationFunctionType.Copy
 MULT = mybir.AluOpType.mult
 
 P = 128
@@ -25,6 +26,7 @@ PAIRS = E // 2
 PAIR_SLOTS = 2 * C
 QUAD = COLD // 2
 PLANE_ROWS = 3 * 32 + 4
+HOT_ROW = 4
 BANK_BLOCKS = H // P
 EARLY, LATER = (T - QUAD * C, T), (0, T - QUAD * C)
 
@@ -45,10 +47,10 @@ def tile_moe_hot_mlp_silu_kernel(
             nc.vector.memset(planes[:].rearrange("p a w -> p (a w)").bitcast(I32), 0)
             return planes
 
-        def load_planes(queue, planes, scales):
+        def load_planes(queue, planes, scales, first_row=0):
             rows = scales.rearrange("e s (q r) w -> r q (e s) w", r=4)
             for r in range(4):
-                queue.dma_start(planes[r:P:32, :, :].bitcast(I32), rows[r].bitcast(I32))
+                queue.dma_start(planes[first_row + r : P : 32, :, :].bitcast(I32), rows[r].bitcast(I32))
 
         def listed(a, b):
             return offsets[:, a // 16 : b // 16]
@@ -97,9 +99,9 @@ def tile_moe_hot_mlp_silu_kernel(
                 src = w1h_words[e].rearrange("s p i d -> p s (i d)")
             nc.sync.dma_start(w1[e][:].bitcast(I32), src.bitcast(I32))
 
-        def load_w2c(b):
-            src = w2c_words[b * QUAD : (b + 1) * QUAD].rearrange("e s p b -> p (e s) b")
-            nc.sync.dma_start(w2c[b][:].bitcast(I32), src.bitcast(I32))
+        def load_w2c(b, first=0, last=QUAD):
+            src = w2c_words[b * QUAD + first : b * QUAD + last].rearrange("e s p b -> p (e s) b")
+            nc.sync.dma_start(w2c[b][:, first:last, :].bitcast(I32), src.bitcast(I32))
 
         words = {}
 
@@ -147,9 +149,10 @@ def tile_moe_hot_mlp_silu_kernel(
         move_planes(nc.sync, 0)
         for e in range(E - QUAD - 1, HOT - 1, -1):
             load_w1(e)
-        load_w2c(0)
-        for e in range(HOT - 1, -1, -1):
-            load_w1(e)
+        load_w2c(0, 2, 4)
+        load_w1(1)
+        load_w2c(0, 0, 2)
+        load_w1(0)
         nc.sync.dma_start(w2h[:].bitcast(I32), w2h_words.rearrange("e s p n d -> p (e s) (n d)").bitcast(I32))
 
         gate_turned = spare_banks[0]
@@ -174,39 +177,43 @@ def tile_moe_hot_mlp_silu_kernel(
 
         def first_products(g):
             hids = []
+            both = keep.tile([P, 2, H // 2], F32, name="hids%d" % g, align_bytes=64)
             for e, acc in zip(experts(g), (lead_banks[g % 2], follow_banks[g % 2])):
                 b, f = divmod(e - HOT, QUAD)
-                planes = s1_cold[b][:, f * PASSES :, :] if e >= HOT else s1_hot[:, e * PASSES :, :]
+                planes = s1_cold[b][:, f * PASSES :, :] if e >= HOT else s1_hot[HOT_ROW:P, e * PASSES :, :]
                 for s in range(PASSES):
                     nc.tensor.matmul_mx(
                         out=acc[:], lhsT=words[(e, s)].bitcast(FP8X4), lhsT_scale=token_plane(e, s),
                         rhs=w1[e][:, s, :].bitcast(FP4X4 if e >= HOT else FP8X4), rhs_scale=planes[:, s, :],
                         start=(s == 0), stop=(s == PASSES - 1),
                     )
-                hid = keep.tile([P, H // 2], F32, name="hid%d" % e, align_bytes=64)
+                hid = both[:, len(hids), :]
                 ordered = hid[:].bitcast(BF16).rearrange("c (u p v) -> c u p v", u=2, v=2)
                 nc.scalar.activation(ordered, acc[:].rearrange("c (p u v) -> c u p v", u=2, v=2), SILU)
                 hids.append(hid)
             return hids
 
-        def turn_and_quantize(g, hids):
+        def turn(g, hids, tag=None):
             turned = turn_banks[g % 2][:].rearrange("p (j u c) -> p j u c", u=2, c=C)
             for j, hid in enumerate(hids):
                 for u in range(2):
                     nc.tensor.transpose(turned[:, j, u, :], hid[:, u * P : (u + 1) * P], ident[:])
-            grouped = keep.tile([P, PAIR_SLOTS * 4], BF16, name="grouped%d" % g, align_bytes=64)
+            grouped = keep.tile([P, PAIR_SLOTS * 4], BF16, name="grouped%d" % g, tag=tag or "grouped%d" % g, align_bytes=64)
             nc.scalar.copy(
                 grouped[:].bitcast(F32).rearrange("p (j c u) -> p j c u", u=2, c=C),
                 turned.rearrange("p j u c -> p j c u"),
             )
+            return grouped
+
+        def quantize(g, grouped):
             codes = keep.tile([P, PAIR_SLOTS], U32, name="codes%d" % g, align_bytes=64)
             scales = keep.tile([P, PAIR_SLOTS], U8, name="scales%d" % g, align_bytes=64)
             nc.vector.quantize_mx(out=codes[:].bitcast(FP8X4), scales=scales[:], in_=grouped[:])
             return codes, scales
 
-        def second_products(g, bank, codes, scales):
-            results = [bank[:, h * PAIR_SLOTS : (h + 1) * PAIR_SLOTS] for h in range(HALVES)]
-            for h in range(HALVES):
+        def second_products(g, homes, codes, scales):
+            results = [homes[h][:, h * PAIR_SLOTS : (h + 1) * PAIR_SLOTS] for h in range(HALVES)]
+            for h in ((1, 0) if g == PAIRS - 1 else (0, 1)):
                 for j, e in enumerate(experts(g)):
                     if e >= HOT:
                         b, f = divmod(e - HOT, QUAD)
@@ -214,7 +221,7 @@ def tile_moe_hot_mlp_silu_kernel(
                         lhsT_scale = s2_cold[:, e - HOT, h * P : (h + 1) * P]
                     else:
                         lhsT = w2h[:, e, h * 4 * P : (h + 1) * 4 * P].bitcast(FP8X4)
-                        lhsT_scale = s2_hot[:, e, h * P : (h + 1) * P]
+                        lhsT_scale = s2_hot[HOT_ROW:P, e, h * P : (h + 1) * P]
                     nc.tensor.matmul_mx(
                         out=results[h][:, (1 - j) * C : (2 - j) * C], lhsT=lhsT, lhsT_scale=lhsT_scale,
                         rhs=codes[:, j * C : (j + 1) * C].bitcast(FP8X4), rhs_scale=scales[:, j * C : (j + 1) * C],
@@ -223,30 +230,59 @@ def tile_moe_hot_mlp_silu_kernel(
             return results
 
         def send(g, h, result, staged):
-            a = min(experts(g)) * C
             nc.scalar.copy(staged[:], result)
+            scatter(g, h, staged)
+
+        def scatter(g, h, staged):
+            a = min(experts(g)) * C
             window = outs[h][:].indirect(listed(a, a + PAIR_SLOTS))
             nc.vector.tensor_tensor(window, staged[:], gates[:, a : a + PAIR_SLOTS], MULT)
 
-        def staging(name):
-            return keep.tile([P, PAIR_SLOTS], F32, name=name, align_bytes=64)
+        def staging(name, tag=None):
+            return keep.tile([P, PAIR_SLOTS], F32, name=name, tag=tag or name, align_bytes=64)
+
+        def gated(g, result, staged):
+            a = min(experts(g)) * C
+            nc.vector.tensor_tensor(staged[:], result, gates[:, a : a + PAIR_SLOTS], MULT)
+            return staged
+
+        def scalar_scatter(g, staged):
+            a = min(experts(g)) * C
+            nc.scalar.activation(outs[1][:].indirect(listed(a, a + PAIR_SLOTS)), staged[:], COPY)
 
         quantized = None
-        for g in range(PAIRS):
+        for g in range(3):
             hids = first_products(g)
             if g == 0:
-                load_planes(nc.gpsimd, s1_hot, w1h_scales)
-                load_planes(nc.sync, s2_hot, w2h_scales)
+                load_planes(nc.gpsimd, s1_hot, w1h_scales, HOT_ROW)
+                load_planes(nc.sync, s2_hot, w2h_scales, HOT_ROW)
             else:
-                results = second_products(g - 1, lead_banks[g % 2], *quantized)
+                results = second_products(g - 1, [lead_banks[g % 2]] * 2, *quantized)
                 send(g - 1, 0, results[0], staging("staged%d" % g))
-            quantized = turn_and_quantize(g, hids)
+            quantized = quantize(g, turn(g, hids))
             if g == 0:
                 gather_words(words_tile("words_last", 1, LATER, "grouped0")[:, 0, :], LATER, PASSES - 1)
             else:
                 send(g - 1, 1, results[1], hids[-1])
 
-        results = second_products(PAIRS - 1, spare_banks[0], *quantized)
+        hids = first_products(3)
+        results = second_products(2, [lead_banks[1]] * 2, *quantized)
+        grouped = turn(3, hids)
+        both = keep.tile([P, HALVES, PAIR_SLOTS], F32, name="staged3", tag="hids3", align_bytes=64)
+        gated(2, results[1], both[:, 1, :])
+        quantized = quantize(3, grouped)
+        send(2, 0, results[0], both[:, 0, :])
+        scalar_scatter(2, both[:, 1, :])
+        results = second_products(3, [spare_banks[1]] * 2, *quantized)
+        send(3, 0, results[0], staging("staged4"))
+
+        grouped = turn(4, first_products(4))
+        for_scalar = gated(3, results[1], staging("gated3", "hids4"))
+        quantized = quantize(4, grouped)
+        scalar_scatter(3, for_scalar)
+        results = second_products(4, [spare_banks[0], lead_banks[1]], *quantized)
+        for_scalar = gated(4, results[1], staging("gated4"))
+        send(4, 0, results[0], staging("staged5"))
+        scalar_scatter(4, for_scalar)
         for h in range(HALVES):
-            send(PAIRS - 1, h, results[h], staging("staged_last%d" % h))
             nc.sync.dma_start(out[h * P : (h + 1) * P, :], outs[h][:])

@@ -92,12 +92,12 @@ def tile_moe_hot_mlp_silu_kernel(
         s1_hot = spent_as_planes(E - 1, H)
         s2_hot = spent_as_planes(E - 2, N)[:, 0:HOT, :]
 
-        def load_w1(e):
+        def load_w1(e, first=0, last=PASSES):
             if e >= HOT:
-                src = w1c_words[e - HOT].rearrange("s p b -> p s b")
+                src = w1c_words[e - HOT, first:last].rearrange("s p b -> p s b")
             else:
-                src = w1h_words[e].rearrange("s p i d -> p s (i d)")
-            nc.sync.dma_start(w1[e][:].bitcast(I32), src.bitcast(I32))
+                src = w1h_words[e, first:last].rearrange("s p i d -> p s (i d)")
+            nc.sync.dma_start(w1[e][:, first:last, :].bitcast(I32), src.bitcast(I32))
 
         def load_w2c(b, first=0, last=QUAD):
             src = w2c_words[b * QUAD + first : b * QUAD + last].rearrange("e s p b -> p (e s) b")
@@ -151,8 +151,9 @@ def tile_moe_hot_mlp_silu_kernel(
             load_w1(e)
         load_w2c(0, 2, 4)
         load_w1(1)
+        load_w1(0, 0, PASSES - 1)
+        load_w1(0, PASSES - 1)
         load_w2c(0, 0, 2)
-        load_w1(0)
         nc.sync.dma_start(w2h[:].bitcast(I32), w2h_words.rearrange("e s p n d -> p (e s) (n d)").bitcast(I32))
 
         gate_turned = spare_banks[0]
@@ -246,6 +247,10 @@ def tile_moe_hot_mlp_silu_kernel(
             nc.vector.tensor_tensor(staged[:], result, gates[:, a : a + PAIR_SLOTS], MULT)
             return staged
 
+        def copy_scatter(g, staged):
+            a = min(experts(g)) * C
+            nc.vector.tensor_copy(outs[0][:].indirect(listed(a, a + PAIR_SLOTS)), staged[:])
+
         def scalar_scatter(g, staged):
             a = min(experts(g)) * C
             nc.scalar.activation(outs[1][:].indirect(listed(a, a + PAIR_SLOTS)), staged[:], COPY)
@@ -269,12 +274,13 @@ def tile_moe_hot_mlp_silu_kernel(
         results = second_products(2, [lead_banks[1]] * 2, *quantized)
         grouped = turn(3, hids)
         both = keep.tile([P, HALVES, PAIR_SLOTS], F32, name="staged3", tag="hids3", align_bytes=64)
-        gated(2, results[1], both[:, 1, :])
+        for h in (1, 0):
+            gated(2, results[h], both[:, h, :])
         quantized = quantize(3, grouped)
-        send(2, 0, results[0], both[:, 0, :])
         scalar_scatter(2, both[:, 1, :])
+        copy_scatter(2, both[:, 0, :])
         results = second_products(3, [spare_banks[1]] * 2, *quantized)
-        send(3, 0, results[0], staging("staged4"))
+        copy_scatter(3, gated(3, results[0], staging("staged4")))
 
         grouped = turn(4, first_products(4))
         for_scalar = gated(3, results[1], staging("gated3", "hids4"))

from contextlib import ExitStack

import concourse.mybir as mybir
from concourse.masks import make_identity

K, T, E, C, H, N, HOT = 1536, 1280, 10, 128, 512, 256, 2
FLOPS = 2 * T * (K * H + H * N)

F32 = mybir.dt.float32
BF16 = mybir.dt.bfloat16
I32 = mybir.dt.int32
U32 = mybir.dt.uint32
U16 = mybir.dt.uint16
U8 = mybir.dt.uint8
FP8X4 = mybir.dt.float8_e4m3fn_x4
FP4X4 = mybir.dt.float4_e2m1fn_x4
SILU = mybir.ActivationFunctionType.Silu
COPY = mybir.ActivationFunctionType.Copy
MULT = mybir.AluOpType.mult

P = 128
PASSES = K // 512
COLD = E - HOT
HALVES = N // P
PAIRS = E // 2
PAIR_SLOTS = 2 * C
QUAD = COLD // 2
PLANE_ROWS = 3 * 32 + 4
HOT_ROW = 4
BANK_BLOCKS = H // P
EARLY, LATER = (T - QUAD * C, T), (0, T - QUAD * C)


def tile_moe_hot_mlp_silu_kernel(
    tc, x_words, x_scales, w1h_words, w1h_scales, w2h_words, w2h_scales,
    w1c_words, w1c_scales, w2c_words, w2c_scales, gate, offs, out,
):
    nc = tc.nc
    with ExitStack() as ctx:
        keep = ctx.enter_context(tc.tile_pool(name="keep", bufs=1))
        psum = ctx.enter_context(tc.psum_pool(name="psum", bufs=1))
        banks = [psum.tile([P, H], F32, name="bank%d" % b) for b in range(8)]
        lead_banks, follow_banks, turn_banks, spare_banks = banks[0:2], banks[2:4], banks[4:6], banks[6:8]

        def zeroed_planes(name, count, width):
            planes = keep.tile([P, count, width], U8, name=name, align_bytes=64)
            nc.vector.memset(planes[:].rearrange("p a w -> p (a w)").bitcast(I32), 0)
            return planes

        def load_planes(queue, planes, scales, first_row=0):
            rows = scales.rearrange("e s (q r) w -> r q (e s) w", r=4)
            for r in range(4):
                queue.dma_start(planes[first_row + r : P : 32, :, :].bitcast(I32), rows[r].bitcast(I32))

        def listed(a, b):
            return offsets[:, a // 16 : b // 16]

        xw = [keep.tile([P, T], I32, name="xw%d" % s, align_bytes=64) for s in range(PASSES)]
        offsets = keep.tile([P, T // 16], U16, name="offsets")
        xs = zeroed_planes("xs", 1, T)[:, 0, :]
        gate_rows = keep.tile([P, C], F32, name="gate_rows", align_bytes=64)
        nc.vector.memset(gate_rows[:], 0.0)

        def load_words(s):
            nc.sync.dma_start(xw[s][:], x_words[s].rearrange("p t d -> p (t d)").bitcast(I32))

        load_words(0)
        nc.sync.dma_start(offsets[:], offs)
        for q in range(4):
            queue = nc.sync if q % 2 else nc.scalar
            queue.dma_start(
                xs[32 * q : 32 * q + 4 * PASSES, :].bitcast(I32),
                x_scales[:, 4 * q : 4 * q + 4, :].bitcast(I32),
            )
        for s in range(1, PASSES):
            load_words(s)
        nc.sync.dma_start(gate_rows[0:E, :], gate[0:1, :].rearrange("o (e c) -> (o e) c", c=C))

        s1_cold = {b: zeroed_planes("s1_cold%d" % b, QUAD * PASSES, H) for b in (1, 0)}
        moved = {b: zeroed_planes("moved%d" % b, PASSES - 1, QUAD * C) for b in (1, 0)}
        s2_cold = zeroed_planes("s2_cold", COLD, N)
        ident = keep.tile([P, P], F32, name="ident")
        make_identity(nc, ident[:])
        w1 = [keep.tile([P, PASSES, (4 if e < HOT else 2) * H], U8, name="w1_%d" % e, align_bytes=64) for e in range(E)]
        w2c = [keep.tile([P, QUAD, 2 * N], U8, name="w2c%d" % b, align_bytes=64) for b in range(2)]
        w2h = keep.tile([P, HOT, 4 * N], U8, name="w2h", align_bytes=64)
        gates = keep.tile([P, T], F32, name="gates")

        def spent_as_planes(e, width):
            return w1[e][:].rearrange("p s b -> p (s b)").rearrange("p (a w) -> p a w", w=width)

        s1_hot = spent_as_planes(E - 1, H)
        s2_hot = spent_as_planes(E - 2, N)[:, 0:HOT, :]

        def load_w1(e, first=0, last=PASSES):
            if e >= HOT:
                src = w1c_words[e - HOT, first:last].rearrange("s p b -> p s b")
            else:
                src = w1h_words[e, first:last].rearrange("s p i d -> p s (i d)")
            nc.sync.dma_start(w1[e][:, first:last, :].bitcast(I32), src.bitcast(I32))

        def load_w2c(b, first=0, last=QUAD):
            src = w2c_words[b * QUAD + first : b * QUAD + last].rearrange("e s p b -> p (e s) b")
            nc.sync.dma_start(w2c[b][:, first:last, :].bitcast(I32), src.bitcast(I32))

        words = {}

        def gather_words(into, slots, s):
            a, b = slots
            nc.vector.tensor_copy(into, xw[s][:].bitcast(U32).indirect(listed(a, b)))
            for e in range(a // C, b // C):
                words[(e, s)] = into[:, e * C - a : (e + 1) * C - a]

        def words_tile(name, count, slots, tag=None):
            return keep.tile([P, count, slots[1] - slots[0]], U32, name=name, tag=tag or name, align_bytes=64)

        words_early = [words_tile("words_early%d" % s, 1, EARLY) for s in range(PASSES)]
        gather_words(words_early[0][:, 0, :], EARLY, 0)
        slot_bytes = keep.tile([P, T], U8, name="slot_bytes", align_bytes=64)
        for a, b in (EARLY, LATER):
            nc.vector.tensor_copy(slot_bytes[:, a:b], xs[:].indirect(listed(a, b)))

        def move_planes(queue, b):
            first = (HOT + b * QUAD) * C
            for s in range(1, PASSES):
                queue.dma_start(
                    moved[b][0:PLANE_ROWS, s - 1, :].bitcast(I32),
                    slot_bytes[4 * s : 4 * s + PLANE_ROWS, first : first + QUAD * C].bitcast(I32),
                )

        for s in range(1, PASSES):
            gather_words(words_early[s][:, 0, :], EARLY, s)

        def token_plane(e, s):
            if e < HOT or s == 0:
                return slot_bytes[4 * s : P, e * C : (e + 1) * C]
            b, f = divmod(e - HOT, QUAD)
            return moved[b][:, s - 1, f * C : (f + 1) * C]

        for b in (1, 0):
            load_planes(nc.gpsimd, s1_cold[b], w1c_scales[b * QUAD : (b + 1) * QUAD])
        load_w1(E - 1)
        move_planes(nc.sync, 1)
        load_w1(E - 2)
        for e in (E - 3, E - 4):
            load_w1(e)
        load_w2c(1)
        load_planes(nc.sync, s2_cold, w2c_scales)
        move_planes(nc.sync, 0)
        for e in range(E - QUAD - 1, HOT - 1, -1):
            load_w1(e)
        load_w2c(0, 2, 4)
        load_w1(1)
        load_w1(0, 0, PASSES - 1)
        load_w1(0, PASSES - 1)
        load_w2c(0, 0, 2)
        nc.sync.dma_start(w2h[:].bitcast(I32), w2h_words.rearrange("e s p n d -> p (e s) (n d)").bitcast(I32))

        gate_turned = spare_banks[0]
        nc.tensor.transpose(gate_turned[:, 0:P], gate_rows[:], ident[:])
        gate_cols = keep.tile([P, E], F32, name="gate_cols", align_bytes=64)
        nc.scalar.copy(gate_cols[:], gate_turned[:, 0:E])
        for first, spread in zip(range(0, E, BANK_BLOCKS), (spare_banks[1], turn_banks[1], follow_banks[1])):
            count = min(BANK_BLOCKS, E - first)
            for j in range(count):
                column = gate_cols[:, first + j : first + j + 1]
                nc.tensor.transpose(spread[:, j * C : (j + 1) * C], column.to_broadcast([P, P]), ident[:])
            nc.scalar.copy(gates[:, first * C : (first + count) * C], spread[:, 0 : count * C])

        words_later = words_tile("words_later", PASSES - 1, LATER, "gate_rows")
        for s in range(PASSES - 1):
            gather_words(words_later[:, s, :], LATER, s)

        outs = [keep.tile([P, T], F32, name="out%d" % h) for h in range(HALVES)]

        def experts(g):
            return (E - 1 - 2 * g, E - 2 - 2 * g)

        def first_products(g):
            hids = []
            both = keep.tile([P, 2, H // 2], F32, name="hids%d" % g, align_bytes=64)
            for e, acc in zip(experts(g), (lead_banks[g % 2], follow_banks[g % 2])):
                b, f = divmod(e - HOT, QUAD)
                planes = s1_cold[b][:, f * PASSES :, :] if e >= HOT else s1_hot[HOT_ROW:P, e * PASSES :, :]
                for s in range(PASSES):
                    nc.tensor.matmul_mx(
                        out=acc[:], lhsT=words[(e, s)].bitcast(FP8X4), lhsT_scale=token_plane(e, s),
                        rhs=w1[e][:, s, :].bitcast(FP4X4 if e >= HOT else FP8X4), rhs_scale=planes[:, s, :],
                        start=(s == 0), stop=(s == PASSES - 1),
                    )
                hid = both[:, len(hids), :]
                ordered = hid[:].bitcast(BF16).rearrange("c (u p v) -> c u p v", u=2, v=2)
                nc.scalar.activation(ordered, acc[:].rearrange("c (p u v) -> c u p v", u=2, v=2), SILU)
                hids.append(hid)
            return hids

        def turn(g, hids, tag=None):
            turned = turn_banks[g % 2][:].rearrange("p (j u c) -> p j u c", u=2, c=C)
            for j, hid in enumerate(hids):
                for u in range(2):
                    nc.tensor.transpose(turned[:, j, u, :], hid[:, u * P : (u + 1) * P], ident[:])
            grouped = keep.tile([P, PAIR_SLOTS * 4], BF16, name="grouped%d" % g, tag=tag or "grouped%d" % g, align_bytes=64)
            nc.scalar.copy(
                grouped[:].bitcast(F32).rearrange("p (j c u) -> p j c u", u=2, c=C),
                turned.rearrange("p j u c -> p j c u"),
            )
            return grouped

        def quantize(g, grouped):
            codes = keep.tile([P, PAIR_SLOTS], U32, name="codes%d" % g, align_bytes=64)
            scales = keep.tile([P, PAIR_SLOTS], U8, name="scales%d" % g, align_bytes=64)
            nc.vector.quantize_mx(out=codes[:].bitcast(FP8X4), scales=scales[:], in_=grouped[:])
            return codes, scales

        def second_products(g, homes, codes, scales):
            results = [homes[h][:, h * PAIR_SLOTS : (h + 1) * PAIR_SLOTS] for h in range(HALVES)]
            for h in ((1, 0) if g == PAIRS - 1 else (0, 1)):
                for j, e in enumerate(experts(g)):
                    if e >= HOT:
                        b, f = divmod(e - HOT, QUAD)
                        lhsT = w2c[b][:, f, h * 2 * P : (h + 1) * 2 * P].bitcast(FP4X4)
                        lhsT_scale = s2_cold[:, e - HOT, h * P : (h + 1) * P]
                    else:
                        lhsT = w2h[:, e, h * 4 * P : (h + 1) * 4 * P].bitcast(FP8X4)
                        lhsT_scale = s2_hot[HOT_ROW:P, e, h * P : (h + 1) * P]
                    nc.tensor.matmul_mx(
                        out=results[h][:, (1 - j) * C : (2 - j) * C], lhsT=lhsT, lhsT_scale=lhsT_scale,
                        rhs=codes[:, j * C : (j + 1) * C].bitcast(FP8X4), rhs_scale=scales[:, j * C : (j + 1) * C],
                        start=True, stop=True,
                    )
            return results

        def send(g, h, result, staged):
            nc.scalar.copy(staged[:], result)
            scatter(g, h, staged)

        def scatter(g, h, staged):
            a = min(experts(g)) * C
            window = outs[h][:].indirect(listed(a, a + PAIR_SLOTS))
            nc.vector.tensor_tensor(window, staged[:], gates[:, a : a + PAIR_SLOTS], MULT)

        def staging(name, tag=None):
            return keep.tile([P, PAIR_SLOTS], F32, name=name, tag=tag or name, align_bytes=64)

        def gated(g, result, staged):
            a = min(experts(g)) * C
            nc.vector.tensor_tensor(staged[:], result, gates[:, a : a + PAIR_SLOTS], MULT)
            return staged

        def copy_scatter(g, staged):
            a = min(experts(g)) * C
            nc.vector.tensor_copy(outs[0][:].indirect(listed(a, a + PAIR_SLOTS)), staged[:])

        def scalar_scatter(g, staged):
            a = min(experts(g)) * C
            nc.scalar.activation(outs[1][:].indirect(listed(a, a + PAIR_SLOTS)), staged[:], COPY)

        quantized = None
        for g in range(3):
            hids = first_products(g)
            if g == 0:
                load_planes(nc.gpsimd, s1_hot, w1h_scales, HOT_ROW)
                load_planes(nc.sync, s2_hot, w2h_scales, HOT_ROW)
            else:
                results = second_products(g - 1, [lead_banks[g % 2]] * 2, *quantized)
                send(g - 1, 0, results[0], staging("staged%d" % g))
            quantized = quantize(g, turn(g, hids))
            if g == 0:
                gather_words(words_tile("words_last", 1, LATER, "grouped0")[:, 0, :], LATER, PASSES - 1)
            else:
                send(g - 1, 1, results[1], hids[-1])

        hids = first_products(3)
        results = second_products(2, [lead_banks[1]] * 2, *quantized)
        grouped = turn(3, hids)
        both = keep.tile([P, HALVES, PAIR_SLOTS], F32, name="staged3", tag="hids3", align_bytes=64)
        for h in (1, 0):
            gated(2, results[h], both[:, h, :])
        quantized = quantize(3, grouped)
        scalar_scatter(2, both[:, 1, :])
        copy_scatter(2, both[:, 0, :])
        results = second_products(3, [spare_banks[1]] * 2, *quantized)
        copy_scatter(3, gated(3, results[0], staging("staged4")))

        grouped = turn(4, first_products(4))
        for_scalar = gated(3, results[1], staging("gated3", "hids4"))
        quantized = quantize(4, grouped)
        scalar_scatter(3, for_scalar)
        results = second_products(4, [spare_banks[0], lead_banks[1]], *quantized)
        for_scalar = gated(4, results[1], staging("gated4"))
        send(4, 0, results[0], staging("staged5"))
        scalar_scatter(4, for_scalar)
        for h in range(HALVES):
            nc.sync.dma_start(out[h * P : (h + 1) * P, :], outs[h][:])
